import numpy as np
import ml_dtypes


def mxq(x, axis, fmt="e4m3"):
    dtype, down = {"e4m3": (ml_dtypes.float8_e4m3fn, 7), "e5m2": (ml_dtypes.float8_e5m2, 14)}[fmt]
    v = np.moveaxis(np.asarray(x, np.float32).astype(ml_dtypes.bfloat16).astype(np.float64), axis, -1)
    blocks = v.reshape(v.shape[:-1] + (-1, 32))
    amax = np.abs(blocks).max(-1, keepdims=True)
    byte = np.maximum(np.where(amax > 0, np.frexp(amax)[1] - 1 + 127, 0) - down, 1)
    scale = np.exp2(byte - 127.0)
    codes = (blocks / scale).astype(np.float32).astype(dtype).astype(np.float64)
    return np.moveaxis((codes * scale).reshape(v.shape), -1, axis)


WIDE = False


def mx_kscale(k):
    if not WIDE:
        return np.ones(k)
    levels = np.array([10, -10, 5, -5, 0])
    if k % 512:
        return np.exp2(np.random.permutation(np.resize(levels, k // 32))).repeat(32)
    a = np.empty((k // 512, 16))
    for p in range(k // 512):
        a[p, :8] = np.random.permutation(np.resize(levels, 8))
        for g in range(8):
            far = levels[np.abs(levels - a[p, g]) >= 10]
            a[p, g + 8] = far[np.random.randint(len(far))]
    return np.exp2(a.ravel()).repeat(32)


def f64(x):
    return np.asarray(x).astype(np.float64)


def striped(idx):
    return np.tile(np.asarray(idx).reshape(-1, 16).T, (8, 1)).astype(np.uint16)


def unstriped(offs):
    return offs[:16].T.reshape(-1).astype(np.int64)


E2M1 = np.array([0.0, 0.5, 1.0, 1.5, 2.0, 3.0, 4.0, 6.0, -0.0, -0.5, -1.0, -1.5, -2.0, -3.0, -4.0, -6.0])


def pack_weight(w, fmt):
    k, n = w.shape
    w = f64(np.asarray(w, np.float32).astype(ml_dtypes.bfloat16)).reshape(k // 32, 32, n)
    amax = np.abs(w).max(1)
    if fmt == "e4m3":
        byte = np.frexp(amax)[1] - 1 + 127 - 7
    else:
        mant, ex = np.frexp(amax / 6.0)
        byte = np.where(mant > 0.5, ex, ex - 1) + 127
    byte = np.clip(np.where(amax > 0, byte, 1), 1, 254)
    scaled = (w * np.exp2(127.0 - byte)[:, None, :]).reshape(k, n).astype(np.float32)
    by_word = np.ascontiguousarray(scaled.reshape(k // 512, 128, 4, n).transpose(0, 1, 3, 2))
    if fmt == "e4m3":
        words = by_word.astype(ml_dtypes.float8_e4m3fn).view(np.uint8)
    else:
        c = by_word.astype(ml_dtypes.float4_e2m1fn).view(np.uint8) & 0xF
        words = (c[..., 0::2] | (c[..., 1::2] << 4)).reshape(k // 512, 128, 2 * n)
    return np.ascontiguousarray(words), np.ascontiguousarray(byte.astype(np.uint8).reshape(k // 512, 16, n))


def unpack_weight(words, scales, fmt):
    g, _, n = scales.shape
    words = np.ascontiguousarray(words).reshape(g, 128, n, -1)
    if fmt == "e4m3":
        vals = words.view(ml_dtypes.float8_e4m3fn).astype(np.float64)
    else:
        nib = np.empty((g, 128, n, 4), np.uint8)
        nib[..., 0::2] = words & 0xF
        nib[..., 1::2] = words >> 4
        vals = E2M1[nib]
    vals = vals * np.repeat(np.exp2(scales.astype(np.float64) - 127.0), 8, axis=1)[..., None]
    return vals.transpose(0, 1, 3, 2).reshape(g * 512, n)


def bf(x):
    return np.asarray(x, np.float32).astype(ml_dtypes.bfloat16)


def planes(Y):
    r, m = Y.shape
    b = f64(bf(Y)).reshape(r // 32, 32, m)
    amax = np.abs(b).max(1)
    byte = np.clip(np.where(amax > 0, np.frexp(amax)[1] - 1 + 127 - 7, 1), 1, 254)
    codes = (b * np.exp2(127.0 - byte)[:, None, :]).reshape(r, m).astype(np.float32).astype(ml_dtypes.float8_e4m3fn).view(np.uint8)
    words = codes.reshape(r // 512, 128, 4, m).transpose(0, 1, 3, 2)
    return np.ascontiguousarray(words), np.ascontiguousarray(byte.astype(np.uint8).reshape(r // 512, 16, m))


D, T, I, U, J, Q = 512, 2048, 512, 2048, 512, 512


def setup_inputs():
    n = np.random.standard_normal
    idx = np.random.permutation(T)[:I]
    idx2 = np.random.permutation(U)[:J]
    fd = mx_kscale(D)
    fi = mx_kscale(I)
    keysp = pack_weight(n((D, T)) / fd[:, None], "e2m1")
    qpoolp = pack_weight(n((D, T)) * 0.6 / np.sqrt(D) * fd[:, None], "e4m3")
    keys2p = pack_weight(n((D, U)) / fd[:, None], "e4m3")
    return {
        "query": (n((D, Q)) * 0.6 / np.sqrt(D) * fd[:, None]).astype(np.float32),
        "keys_words": keysp[0],
        "keys_scales": keysp[1],
        "qpool_words": qpoolp[0],
        "qpool_scales": qpoolp[1],
        "keys2_words": keys2p[0],
        "keys2_scales": keys2p[1],
        "sa": (np.random.uniform(0.5, 2.0, (1, I)) * fi).astype(np.float32),
        "sb": (np.random.uniform(0.5, 2.0, (I, 1)) / fi[:, None]).astype(np.float32),
        "offs": striped(idx),
        "offs2": striped(idx2),
    }


def reference(query, keys_words, keys_scales, qpool_words, qpool_scales, keys2_words, keys2_scales, sa, sb, offs, offs2):
    idx = unstriped(offs)
    idx2 = unstriped(offs2)
    keysu = unpack_weight(keys_words, keys_scales, "e2m1")
    qpoolu = unpack_weight(qpool_words, qpool_scales, "e4m3")
    keys2u = unpack_weight(keys2_words, keys2_scales, "e4m3")
    queryq = mxq(f64(query), 0, "e4m3")
    keysidxg = keysu[:, idx]
    a = queryq.T @ keysidxg
    p = np.exp(a - np.max(a, axis=1, keepdims=True))
    w = p * f64(sa) / np.sum(p, axis=1, keepdims=True)
    wt = w.T
    qpoolidxg = qpoolu[:, idx]
    keys2idx2g = keys2u[:, idx2]
    b = qpoolidxg.T @ keys2idx2g
    r = np.exp(b - np.max(b, axis=1, keepdims=True))
    x = r * f64(sb) / np.sum(r, axis=1, keepdims=True) * 512.0
    wtq = mxq(wt, 0, "e4m3")
    xq = mxq(x, 0, "e4m3")
    y = wtq.T @ xq
    words, scales = planes(y)
    return y, words, scales

@@ -1,0 +1,227 @@
+from contextlib import ExitStack
+
+import concourse.mybir as mybir
+from concourse.masks import make_identity
+
+F32 = mybir.dt.float32
+BF16 = mybir.dt.bfloat16
+I32 = mybir.dt.int32
+U32 = mybir.dt.uint32
+U16 = mybir.dt.uint16
+U8 = mybir.dt.uint8
+FP8X4 = mybir.dt.float8_e4m3fn_x4
+FP4X4 = mybir.dt.float4_e2m1fn_x4
+ALU = mybir.AluOpType
+ACT = mybir.ActivationFunctionType
+AX = mybir.AxisListType
+
+P = 128
+PACK = 4
+D, T, I, U, J, Q = 512, 2048, 512, 2048, 512, 512
+FLOPS = 2 * D * Q * I + 2 * D * I * J + 2 * I * Q * J
+KEYS_ROW, KEYS2_ROW, QPOOL_ROW = 0, 4, 8
+CHUNKS = 4
+JC = J // CHUNKS
+
+
+def tile_attend_rollout_pl_kernel(tc, query, keys_words, keys_scales, qpool_words, qpool_scales,
+                                   keys2_words, keys2_scales, sa, sb, offs, offs2, out_0, out_1, out_2):
+    nc = tc.nc
+    with ExitStack() as ctx:
+        lists = ctx.enter_context(tc.tile_pool(name="lists", bufs=1))
+        keep = ctx.enter_context(tc.tile_pool(name="keep", bufs=1))
+        psum = ctx.enter_context(tc.psum_pool(name="psum", bufs=1))
+
+        def sb_tile(shape, dtype, name, tag=None):
+            return keep.tile(shape, dtype, name=name, tag=tag or name, align_bytes=64)
+
+        def bank(index, shape, name):
+            return psum.tile(shape, F32, name=name, tag="bank%d" % index)
+
+        def zeroed_scale_window(name, tag=None):
+            window = sb_tile([P, T], U8, name, tag)
+            nc.vector.memset(window[:].bitcast(I32), 0)
+            return window
+
+        def load_scale_rows(queues, window, scales, row):
+            for quad in range(4):
+                queues[quad].dma_start(out=window[32 * quad + row: 32 * quad + row + 4, :].bitcast(I32),
+                                in_=scales[0, 4 * quad: 4 * quad + 4, :].bitcast(I32))
+
+        ident = sb_tile([P, P], F32, "ident")
+        make_identity(nc, ident[:])
+        vec_rows = sb_tile([P, P], F32, "vec_rows")
+        nc.gpsimd.memset(vec_rows[:], 0.0)
+        nc.gpsimd.dma_start(out=vec_rows[4:8, :], in_=sa.rearrange("o (m c) -> (o m) c", m=4))
+        nc.gpsimd.dma_start(out=vec_rows[0:4, :].rearrange("t (g r) -> t g r", r=8),
+                            in_=sb.rearrange("(g t r) o -> t g (r o)", t=4, r=8))
+        ks_win = zeroed_scale_window("ks_win", "slot_b")
+        qs_win = zeroed_scale_window("qs_win")
+        k2s_win = zeroed_scale_window("k2s_win")
+        offs_sb = lists.tile([P, I // 16], U16, name="offs_sb")
+        offs2_sb = lists.tile([P, J // 16], U16, name="offs2_sb")
+        nc.sync.dma_start(offs_sb[:], offs)
+        nc.sync.dma_start(offs2_sb[:], offs2)
+        kw_win = sb_tile([P, T], U16, "kw_win", "slot_a")
+        nc.sync.dma_start(out=kw_win[:].bitcast(I32), in_=keys_words[0].bitcast(I32))
+        q_rows = query.rearrange("(p t) q -> p t q", t=PACK)
+        warm = sb_tile([P, 1], F32, "warm", "q_raw1")
+        nc.scalar.activation(out=warm[:], in_=ident[:, 0:1], func=ACT.Exp)
+        q_raw = [sb_tile([P, PACK, Q // 2], F32, "q_raw%d" % h) for h in range(2)]
+        nc.sync.dma_start(out=q_raw[0][:], in_=q_rows[:, :, 0:256])
+        load_scale_rows([nc.sync] * 4, ks_win, keys_scales, KEYS_ROW)
+        nc.sync.dma_start(out=q_raw[1][:], in_=q_rows[:, :, 256:512])
+        load_scale_rows([nc.sync] * 4, qs_win, qpool_scales, QPOOL_ROW)
+
+        kw = sb_tile([P, I], U16, "kw")
+        nc.vector.tensor_copy(out=kw[:], in_=kw_win[:].indirect(offs_sb[:]))
+        ks = sb_tile([P, I], U8, "ks")
+        nc.vector.tensor_copy(out=ks[:], in_=ks_win[:].indirect(offs_sb[:]))
+        qw_win = sb_tile([P, T], I32, "qw_win", "slot_a")
+        nc.sync.dma_start(out=qw_win[:], in_=qpool_words[0].rearrange("p n t -> p (n t)").bitcast(I32))
+        load_scale_rows([nc.sync, nc.sync, nc.gpsimd, nc.gpsimd], k2s_win, keys2_scales, KEYS2_ROW)
+        k2w_win = sb_tile([P, U], I32, "k2w_win", "slot_b")
+        nc.sync.dma_start(out=k2w_win[:], in_=keys2_words[0].rearrange("p n t -> p (n t)").bitcast(I32))
+
+        q_codes = sb_tile([P, Q], U32, "q_codes")
+        q_scales = sb_tile([P, Q], U8, "q_scales")
+        for h in range(2):
+            q_bf = sb_tile([P, Q // 2, PACK], BF16, "q_bf%d" % h)
+            nc.scalar.copy(out=q_bf[:].rearrange("p (c i) t -> p c t i", i=4),
+                           in_=q_raw[h][:].rearrange("p t (c i) -> p c t i", i=4))
+            cols = slice(h * 256, (h + 1) * 256)
+            nc.vector.quantize_mx(out=q_codes[:, cols].bitcast(FP8X4), scales=q_scales[:, cols],
+                                  in_=q_bf[:].rearrange("p c t -> p (c t)"))
+
+        qs_list = sb_tile([P, I], U8, "qs_list")
+        nc.vector.tensor_copy(out=qs_list[:], in_=qs_win[:].indirect(offs_sb[:]))
+        k2s = sb_tile([P, J], U8, "k2s")
+        nc.vector.tensor_copy(out=k2s[:], in_=k2s_win[:].indirect(offs2_sb[:]))
+        qs = sb_tile([P, I], U8, "qs")
+        nc.vector.tensor_copy(out=qs[:].bitcast(I32).rearrange("p (t g w) -> p g t w", t=4, w=2),
+                              in_=qs_list[:].bitcast(I32).rearrange("p (g t w) -> p g t w", t=4, w=2))
+
+        neg_max = sb_tile([P, 8], F32, "neg_max")
+        sums = sb_tile([P, 8], F32, "sums")
+        inv = sb_tile([P, 8], F32, "inv")
+        p_tiles = []
+        for n in range(4):
+            a_ps = bank(n, [P, I], "a_ps%d" % n)
+            cols = slice(n * P, (n + 1) * P)
+            nc.tensor.matmul_mx(out=a_ps[:], lhsT=q_codes[:, cols].bitcast(FP8X4), lhsT_scale=q_scales[:, cols],
+                                rhs=kw[:].bitcast(FP4X4), rhs_scale=ks[:], start=True, stop=True)
+            nc.vector.tensor_reduce(out=neg_max[:, n:n + 1], in_=a_ps[:], axis=AX.X, op=ALU.max, negate=True)
+            p_n = sb_tile([P, I], F32, "p%d" % n)
+            nc.scalar.activation(out=p_n[:].rearrange("p (u g r e) -> p g u r e", u=2, r=8, e=2),
+                                 in_=a_ps[:].rearrange("p (g u e r) -> p g u r e", u=2, r=8, e=2),
+                                 func=ACT.Exp, bias=neg_max[:, n:n + 1], accum_out=sums[:, n:n + 1])
+            p_tiles.append(p_n)
+
+        vec_ps = bank(7, [P, P], "vec_ps")
+        nc.tensor.transpose(vec_ps[:], vec_rows[:], ident[:])
+        sb_cols = sb_tile([P, 4], F32, "sb_cols")
+        nc.scalar.activation(out=sb_cols[:], in_=vec_ps[:, 0:4], func=ACT.Copy, scale=512.0)
+        sa_cols = sb_tile([P, 4], F32, "sa_cols")
+        nc.scalar.copy(out=sa_cols[:], in_=vec_ps[:, 4:8])
+        sa_ps = bank(6, [P, I], "sa_ps")
+        for m in range(4):
+            nc.tensor.transpose(sa_ps[:, m * P:(m + 1) * P], sa_cols[:, m:m + 1].to_broadcast([P, P]), ident[:])
+        sa_all = sb_tile([P, I], F32, "sa_all")
+        nc.scalar.copy(out=sa_all[:].rearrange("p (u g r e) -> p g u r e", u=2, r=8, e=2),
+                       in_=sa_ps[:].rearrange("p (g u e r) -> p g u r e", u=2, r=8, e=2))
+
+        qw = sb_tile([P, I], U32, "qw")
+        nc.vector.tensor_copy(out=qw[:].rearrange("p (t g r) -> p g t r", t=4, r=8),
+                              in_=qw_win[:].bitcast(U32).indirect(offs_sb[:]))
+        k2w = sb_tile([P, J], U32, "k2w")
+        nc.vector.tensor_copy(out=k2w[:], in_=k2w_win[:].bitcast(U32).indirect(offs2_sb[:]))
+
+        wt_bf = sb_tile([P, Q * PACK], BF16, "wt_bf")
+        wt_words = wt_bf[:].bitcast(F32).rearrange("p (t m u) -> p t m u", t=4, u=2)
+
+        def weights_half(h):
+            nc.vector.reciprocal(out=inv[:, 2 * h:2 * h + 2], in_=sums[:, 2 * h:2 * h + 2])
+            wt_ps = bank(h, [P, 2, 256], "wt_ps%d" % h)
+            for n in (2 * h, 2 * h + 1):
+                w_n = sb_tile([P, I], BF16, "w%d" % n, "slot_b" if n == 2 else None)
+                nc.vector.scalar_tensor_tensor(out=w_n[:], in0=p_tiles[n][:], scalar=inv[:, n:n + 1], in1=sa_all[:],
+                                               op0=ALU.mult, op1=ALU.mult)
+                words = w_n[:].bitcast(F32)
+                for u in range(2):
+                    nc.tensor.transpose(wt_ps[:, u, (n % 2) * P:(n % 2 + 1) * P], words[:, u * P:(u + 1) * P], ident[:])
+            nc.scalar.copy(out=wt_words[:, :, 64 * h:64 * (h + 1), :],
+                           in_=wt_ps[:].rearrange("p u (m t) -> p t m u", t=4))
+
+        weights_half(0)
+
+        r_all = sb_tile([P, PACK, J], F32, "r_all")
+        for t in range(4):
+            b_ps = bank(4 + t, [P, J], "b_ps%d" % t)
+            cols = slice(t * P, (t + 1) * P)
+            nc.tensor.matmul_mx(out=b_ps[:], lhsT=qw[:, cols].bitcast(FP8X4), lhsT_scale=qs[QPOOL_ROW:P, cols],
+                                rhs=k2w[:].bitcast(FP8X4), rhs_scale=k2s[KEYS2_ROW:P, :], start=True, stop=True)
+            nc.vector.tensor_reduce(out=neg_max[:, 4 + t:5 + t], in_=b_ps[:], axis=AX.X, op=ALU.max, negate=True)
+            nc.scalar.activation(out=r_all[:, t, :], in_=b_ps[:], func=ACT.Exp,
+                                 bias=neg_max[:, 4 + t:5 + t], accum_out=sums[:, 4 + t:5 + t])
+
+        weights_half(1)
+        wt_codes = sb_tile([P, Q], U32, "wt_codes")
+        wt_scales = sb_tile([P, Q], U8, "wt_scales")
+        nc.vector.quantize_mx(out=wt_codes[:].bitcast(FP8X4), scales=wt_scales[:], in_=wt_bf[:])
+
+        nc.vector.reciprocal(out=inv[:, 4:8], in_=sums[:, 4:8])
+        row_scale = sb_tile([P, 4], F32, "row_scale")
+        nc.vector.tensor_tensor(out=row_scale[:], in0=inv[:, 4:8], in1=sb_cols[:], op=ALU.mult)
+        row_scale_all = row_scale[:].unsqueeze(1).unsqueeze(3).to_broadcast([P, JC // 4, PACK, 4])
+
+        x_codes = sb_tile([P, J], U32, "x_codes")
+        x_scales = sb_tile([P, J], U8, "x_scales")
+        y_codes = sb_tile([P, J], U32, "y_codes")
+        y_scales = sb_tile([P, J], U8, "y_scales")
+        y_rows = out_0.rearrange("(p t) j -> p t j", t=PACK)
+        y_words = out_1[0].rearrange("p c r -> p (c r)").bitcast(I32)
+        x_bf = [sb_tile([P, JC, PACK], BF16, "x_bf%d" % c) for c in range(CHUNKS)]
+        y_bf = [sb_tile([P, JC, PACK], BF16, "y_bf%d" % c) for c in range(CHUNKS)]
+
+        def scale_x(c):
+            cols = slice(c * JC, (c + 1) * JC)
+            nc.vector.tensor_tensor(out=x_bf[c][:].rearrange("p (c i) t -> p c t i", i=4),
+                                    in0=r_all[:, :, cols].rearrange("p t (c i) -> p c t i", i=4),
+                                    in1=row_scale_all, op=ALU.mult)
+
+        def product(c):
+            cols = slice(c * JC, (c + 1) * JC)
+            nc.vector.quantize_mx(out=x_codes[:, cols].bitcast(FP8X4), scales=x_scales[:, cols],
+                                  in_=x_bf[c][:].rearrange("p c t -> p (c t)"))
+            y_ps = bank(2 + c, [P, PACK, JC], "y_ps%d" % c)
+            for t in range(4):
+                q_cols = slice(t * P, (t + 1) * P)
+                nc.tensor.matmul_mx(out=y_ps[:, t, :], lhsT=wt_codes[:, q_cols].bitcast(FP8X4),
+                                    lhsT_scale=wt_scales[:, q_cols], rhs=x_codes[:, cols].bitcast(FP8X4),
+                                    rhs_scale=x_scales[:, cols], start=True, stop=True)
+            y_sb = sb_tile([P, PACK, JC], F32, "y_sb%d" % c)
+            nc.scalar.copy(out=y_sb[:], in_=y_ps[:])
+            nc.sync.dma_start(out=y_rows[:, :, cols], in_=y_sb[:])
+            y_woven = y_bf[c][:].rearrange("p (c i) t -> p c t i", i=4)
+            if c < CHUNKS // 2:
+                nc.scalar.copy(out=y_bf[c][:], in_=y_ps[:].rearrange("p t j -> p j t"))
+            else:
+                nc.vector.tensor_copy(out=y_woven, in_=y_sb[:].rearrange("p t (c i) -> p c t i", i=4))
+
+        def planes(c):
+            cols = slice(c * JC, (c + 1) * JC)
+            nc.vector.quantize_mx(out=y_codes[:, cols].bitcast(FP8X4), scales=y_scales[:, cols],
+                                  in_=y_bf[c][:].rearrange("p c t -> p (c t)"))
+            nc.sync.dma_start(out=y_words[:, cols], in_=y_codes[:, cols].bitcast(I32))
+
+        scale_x(0)
+        for c in range(CHUNKS):
+            if c + 1 < CHUNKS:
+                scale_x(c + 1)
+            product(c)
+        for c in range(CHUNKS):
+            planes(c)
+        for quad in range(4):
+            queue = nc.scalar if quad % 2 else nc.sync
+            queue.dma_start(out=out_2[0, 4 * quad:4 * quad + 4, :].bitcast(I32),
+                            in_=y_scales[32 * quad:32 * quad + 4, :].bitcast(I32))

@@ -43,18 +43,13 @@ def tile_attend_rollout_pl_kernel(tc, query, keys_words, keys_scales, qpool_word
             nc.vector.memset(window[:].bitcast(I32), 0)
             return window
 
-        def load_scale_rows(queues, window, scales, row):
+        def load_scale_rows(queue, window, scales, row):
             for quad in range(4):
-                queues[quad].dma_start(out=window[32 * quad + row: 32 * quad + row + 4, :].bitcast(I32),
+                queue.dma_start(out=window[32 * quad + row: 32 * quad + row + 4, :].bitcast(I32),
                                 in_=scales[0, 4 * quad: 4 * quad + 4, :].bitcast(I32))
 
         ident = sb_tile([P, P], F32, "ident")
         make_identity(nc, ident[:])
-        vec_rows = sb_tile([P, P], F32, "vec_rows")
-        nc.gpsimd.memset(vec_rows[:], 0.0)
-        nc.gpsimd.dma_start(out=vec_rows[4:8, :], in_=sa.rearrange("o (m c) -> (o m) c", m=4))
-        nc.gpsimd.dma_start(out=vec_rows[0:4, :].rearrange("t (g r) -> t g r", r=8),
-                            in_=sb.rearrange("(g t r) o -> t g (r o)", t=4, r=8))
         ks_win = zeroed_scale_window("ks_win", "slot_b")
         qs_win = zeroed_scale_window("qs_win")
         k2s_win = zeroed_scale_window("k2s_win")
@@ -65,13 +60,15 @@ def tile_attend_rollout_pl_kernel(tc, query, keys_words, keys_scales, qpool_word
         kw_win = sb_tile([P, T], U16, "kw_win", "slot_a")
         nc.sync.dma_start(out=kw_win[:].bitcast(I32), in_=keys_words[0].bitcast(I32))
         q_rows = query.rearrange("(p t) q -> p t q", t=PACK)
-        warm = sb_tile([P, 1], F32, "warm", "q_raw1")
+        warm = sb_tile([P, 1], F32, "warm")
         nc.scalar.activation(out=warm[:], in_=ident[:, 0:1], func=ACT.Exp)
         q_raw = [sb_tile([P, PACK, Q // 2], F32, "q_raw%d" % h) for h in range(2)]
         nc.sync.dma_start(out=q_raw[0][:], in_=q_rows[:, :, 0:256])
-        load_scale_rows([nc.sync] * 4, ks_win, keys_scales, KEYS_ROW)
+        sa_cols = sb_tile([P, 4], F32, "sa_cols")
+        nc.sync.dma_start(out=sa_cols[:], in_=sa.rearrange("o (p m) -> (o p) m", m=4))
+        load_scale_rows(nc.sync, ks_win, keys_scales, KEYS_ROW)
         nc.sync.dma_start(out=q_raw[1][:], in_=q_rows[:, :, 256:512])
-        load_scale_rows([nc.sync] * 4, qs_win, qpool_scales, QPOOL_ROW)
+        load_scale_rows(nc.sync, qs_win, qpool_scales, QPOOL_ROW)
 
         kw = sb_tile([P, I], U16, "kw")
         nc.vector.tensor_copy(out=kw[:], in_=kw_win[:].indirect(offs_sb[:]))
@@ -79,9 +76,21 @@ def tile_attend_rollout_pl_kernel(tc, query, keys_words, keys_scales, qpool_word
         nc.vector.tensor_copy(out=ks[:], in_=ks_win[:].indirect(offs_sb[:]))
         qw_win = sb_tile([P, T], I32, "qw_win", "slot_a")
         nc.sync.dma_start(out=qw_win[:], in_=qpool_words[0].rearrange("p n t -> p (n t)").bitcast(I32))
-        load_scale_rows([nc.sync, nc.sync, nc.gpsimd, nc.gpsimd], k2s_win, keys2_scales, KEYS2_ROW)
+        vec_rows = sb_tile([P, P], F32, "vec_rows")
+        nc.gpsimd.memset(vec_rows[:], 0.0)
+        nc.sync.dma_start(out=vec_rows[0:4, :].rearrange("t (g r) -> t g r", r=8),
+                          in_=sb.rearrange("(g t r) o -> t g (r o)", t=4, r=8))
+        load_scale_rows(nc.sync, k2s_win, keys2_scales, KEYS2_ROW)
         k2w_win = sb_tile([P, U], I32, "k2w_win", "slot_b")
         nc.sync.dma_start(out=k2w_win[:], in_=keys2_words[0].rearrange("p n t -> p (n t)").bitcast(I32))
+
+        sa_ps = bank(6, [P, 4, P], "sa_ps")
+        for m in range(4):
+            nc.tensor.transpose(sa_ps[:, m, :], sa_cols[:, m:m + 1].to_broadcast([P, P]), ident[:])
+        sa_all = sb_tile([P, I], F32, "sa_all")
+        for u in range(2):
+            nc.scalar.copy(out=sa_all[:].rearrange("p (u g s m e) -> p u g s m e", u=2, s=2, m=4, e=2)[:, u],
+                           in_=sa_ps[:].rearrange("p m (g u e s) -> p u g s m e", u=2, e=2, s=2)[:, u])
 
         q_codes = sb_tile([P, Q], U32, "q_codes")
         q_scales = sb_tile([P, Q], U8, "q_scales")
@@ -95,13 +104,13 @@ def tile_attend_rollout_pl_kernel(tc, query, keys_words, keys_scales, qpool_word
 
         qs_list = sb_tile([P, I], U8, "qs_list")
         nc.vector.tensor_copy(out=qs_list[:], in_=qs_win[:].indirect(offs_sb[:]))
-        k2s = sb_tile([P, J], U8, "k2s")
+        k2s = sb_tile([P, J], U8, "k2s", "q_bf1")
         nc.vector.tensor_copy(out=k2s[:], in_=k2s_win[:].indirect(offs2_sb[:]))
         qs = sb_tile([P, I], U8, "qs")
         nc.vector.tensor_copy(out=qs[:].bitcast(I32).rearrange("p (t g w) -> p g t w", t=4, w=2),
                               in_=qs_list[:].bitcast(I32).rearrange("p (g t w) -> p g t w", t=4, w=2))
 
-        neg_max = sb_tile([P, 8], F32, "neg_max")
+        neg_max = sb_tile([P, 4], F32, "neg_max")
         sums = sb_tile([P, 8], F32, "sums")
         inv = sb_tile([P, 8], F32, "inv")
         p_tiles = []
@@ -117,57 +126,56 @@ def tile_attend_rollout_pl_kernel(tc, query, keys_words, keys_scales, qpool_word
                                  func=ACT.Exp, bias=neg_max[:, n:n + 1], accum_out=sums[:, n:n + 1])
             p_tiles.append(p_n)
 
-        vec_ps = bank(7, [P, P], "vec_ps")
-        nc.tensor.transpose(vec_ps[:], vec_rows[:], ident[:])
-        sb_cols = sb_tile([P, 4], F32, "sb_cols")
-        nc.scalar.activation(out=sb_cols[:], in_=vec_ps[:, 0:4], func=ACT.Copy, scale=512.0)
-        sa_cols = sb_tile([P, 4], F32, "sa_cols")
-        nc.scalar.copy(out=sa_cols[:], in_=vec_ps[:, 4:8])
-        sa_ps = bank(6, [P, I], "sa_ps")
-        for m in range(4):
-            nc.tensor.transpose(sa_ps[:, m * P:(m + 1) * P], sa_cols[:, m:m + 1].to_broadcast([P, P]), ident[:])
-        sa_all = sb_tile([P, I], F32, "sa_all")
-        nc.scalar.copy(out=sa_all[:].rearrange("p (u g r e) -> p g u r e", u=2, r=8, e=2),
-                       in_=sa_ps[:].rearrange("p (g u e r) -> p g u r e", u=2, r=8, e=2))
-
         qw = sb_tile([P, I], U32, "qw")
         nc.vector.tensor_copy(out=qw[:].rearrange("p (t g r) -> p g t r", t=4, r=8),
                               in_=qw_win[:].bitcast(U32).indirect(offs_sb[:]))
-        k2w = sb_tile([P, J], U32, "k2w")
-        nc.vector.tensor_copy(out=k2w[:], in_=k2w_win[:].bitcast(U32).indirect(offs2_sb[:]))
 
         wt_bf = sb_tile([P, Q * PACK], BF16, "wt_bf")
         wt_words = wt_bf[:].bitcast(F32).rearrange("p (t m u) -> p t m u", t=4, u=2)
 
-        def weights_half(h):
-            nc.vector.reciprocal(out=inv[:, 2 * h:2 * h + 2], in_=sums[:, 2 * h:2 * h + 2])
-            wt_ps = bank(h, [P, 2, 256], "wt_ps%d" % h)
-            for n in (2 * h, 2 * h + 1):
-                w_n = sb_tile([P, I], BF16, "w%d" % n, "slot_b" if n == 2 else None)
-                nc.vector.scalar_tensor_tensor(out=w_n[:], in0=p_tiles[n][:], scalar=inv[:, n:n + 1], in1=sa_all[:],
-                                               op0=ALU.mult, op1=ALU.mult)
-                words = w_n[:].bitcast(F32)
-                for u in range(2):
-                    nc.tensor.transpose(wt_ps[:, u, (n % 2) * P:(n % 2 + 1) * P], words[:, u * P:(u + 1) * P], ident[:])
-            nc.scalar.copy(out=wt_words[:, :, 64 * h:64 * (h + 1), :],
-                           in_=wt_ps[:].rearrange("p u (m t) -> p t m u", t=4))
+        wt_ps = [None, None]
 
-        weights_half(0)
+        def weights(n, tag):
+            h = n // 2
+            if n % 2 == 0:
+                nc.vector.reciprocal(out=inv[:, n:n + 2], in_=sums[:, n:n + 2])
+                wt_ps[h] = bank(h, [P, 2, 256], "wt_ps%d" % h)
+            w_n = sb_tile([P, I], BF16, "w%d" % n, tag)
+            nc.vector.scalar_tensor_tensor(out=w_n[:], in0=p_tiles[n][:], scalar=inv[:, n:n + 1], in1=sa_all[:],
+                                           op0=ALU.mult, op1=ALU.mult)
+            words = w_n[:].bitcast(F32)
+            for u in range(2):
+                nc.tensor.transpose(wt_ps[h][:, u, (n % 2) * P:(n % 2 + 1) * P], words[:, u * P:(u + 1) * P], ident[:])
+            if n % 2 == 1:
+                nc.scalar.copy(out=wt_words[:, :, 64 * h:64 * (h + 1), :],
+                               in_=wt_ps[h][:].rearrange("p u (m t) -> p t m u", t=4))
 
+        weights(0, None)
+        weights(1, None)
+        k2w = sb_tile([P, J], U32, "k2w", "p1")
+        nc.vector.tensor_copy(out=k2w[:], in_=k2w_win[:].bitcast(U32).indirect(offs2_sb[:]))
+
+        vec_ps = bank(7, [P, P], "vec_ps")
+        nc.tensor.transpose(vec_ps[:], vec_rows[:], ident[:])
+        sb_cols = sb_tile([P, 4], F32, "sb_cols")
+        nc.scalar.activation(out=sb_cols[:], in_=vec_ps[:, 0:4], func=ACT.Copy, scale=512.0)
         r_all = sb_tile([P, PACK, J], F32, "r_all")
         for t in range(4):
             b_ps = bank(4 + t, [P, J], "b_ps%d" % t)
             cols = slice(t * P, (t + 1) * P)
             nc.tensor.matmul_mx(out=b_ps[:], lhsT=qw[:, cols].bitcast(FP8X4), lhsT_scale=qs[QPOOL_ROW:P, cols],
                                 rhs=k2w[:].bitcast(FP8X4), rhs_scale=k2s[KEYS2_ROW:P, :], start=True, stop=True)
-            nc.vector.tensor_reduce(out=neg_max[:, 4 + t:5 + t], in_=b_ps[:], axis=AX.X, op=ALU.max, negate=True)
+            neg_max_b = sb_tile([P, 1], F32, "neg_max_b%d" % t)
+            nc.vector.tensor_reduce(out=neg_max_b[:], in_=b_ps[:], axis=AX.X, op=ALU.max, negate=True)
             nc.scalar.activation(out=r_all[:, t, :], in_=b_ps[:], func=ACT.Exp,
-                                 bias=neg_max[:, 4 + t:5 + t], accum_out=sums[:, 4 + t:5 + t])
+                                 bias=neg_max_b[:], accum_out=sums[:, 4 + t:5 + t])
 
-        weights_half(1)
+        weights(2, "slot_b")
+        weights(3, "neg_max_b1")
         wt_codes = sb_tile([P, Q], U32, "wt_codes")
         wt_scales = sb_tile([P, Q], U8, "wt_scales")
         nc.vector.quantize_mx(out=wt_codes[:].bitcast(FP8X4), scales=wt_scales[:], in_=wt_bf[:])
+
 
         nc.vector.reciprocal(out=inv[:, 4:8], in_=sums[:, 4:8])
         row_scale = sb_tile([P, 4], F32, "row_scale")
@@ -189,6 +197,15 @@ def tile_attend_rollout_pl_kernel(tc, query, keys_words, keys_scales, qpool_word
                                     in0=r_all[:, :, cols].rearrange("p t (c i) -> p c t i", i=4),
                                     in1=row_scale_all, op=ALU.mult)
 
+        def scale_x_on_scalar(c):
+            cols = slice(c * JC, (c + 1) * JC)
+            x_rows = sb_tile([P, PACK, JC], BF16, "x_rows")
+            for t in range(PACK):
+                nc.scalar.activation(out=x_rows[:, t, :], in_=r_all[:, t, cols], func=ACT.Copy,
+                                     scale=row_scale[:, t:t + 1])
+            nc.scalar.copy(out=x_bf[c][:].rearrange("p (c i) t -> p c t i", i=4),
+                           in_=x_rows[:].rearrange("p t (c i) -> p c t i", i=4))
+
         def product(c):
             cols = slice(c * JC, (c + 1) * JC)
             nc.vector.quantize_mx(out=x_codes[:, cols].bitcast(FP8X4), scales=x_scales[:, cols],
@@ -202,24 +219,29 @@ def tile_attend_rollout_pl_kernel(tc, query, keys_words, keys_scales, qpool_word
             y_sb = sb_tile([P, PACK, JC], F32, "y_sb%d" % c)
             nc.scalar.copy(out=y_sb[:], in_=y_ps[:])
             nc.sync.dma_start(out=y_rows[:, :, cols], in_=y_sb[:])
-            y_woven = y_bf[c][:].rearrange("p (c i) t -> p c t i", i=4)
-            if c < CHUNKS // 2:
-                nc.scalar.copy(out=y_bf[c][:], in_=y_ps[:].rearrange("p t j -> p j t"))
-            else:
-                nc.vector.tensor_copy(out=y_woven, in_=y_sb[:].rearrange("p t (c i) -> p c t i", i=4))
+            return y_sb
+
+        def round_y(c, y_sb):
+            nc.vector.tensor_copy(out=y_bf[c][:].rearrange("p (c i) t -> p c t i", i=4),
+                                  in_=y_sb[:].rearrange("p t (c i) -> p c t i", i=4))
 
         def planes(c):
             cols = slice(c * JC, (c + 1) * JC)
             nc.vector.quantize_mx(out=y_codes[:, cols].bitcast(FP8X4), scales=y_scales[:, cols],
                                   in_=y_bf[c][:].rearrange("p c t -> p (c t)"))
-            nc.sync.dma_start(out=y_words[:, cols], in_=y_codes[:, cols].bitcast(I32))
+            if c >= CHUNKS - 2:
+                done = slice(0, (c + 1) * JC) if c == CHUNKS - 2 else cols
+                nc.sync.dma_start(out=y_words[:, done], in_=y_codes[:, done].bitcast(I32))
 
-        scale_x(0)
+        y_tiles = []
         for c in range(CHUNKS):
-            if c + 1 < CHUNKS:
-                scale_x(c + 1)
-            product(c)
+            if c == 1:
+                scale_x_on_scalar(c)
+            else:
+                scale_x(c)
+            y_tiles.append(product(c))
         for c in range(CHUNKS):
+            round_y(c, y_tiles[c])
             planes(c)
         for quad in range(4):
             queue = nc.scalar if quad % 2 else nc.sync

@@ -30,6 +30,7 @@ def tile_attend_rollout_pl_kernel(tc, query, keys_words, keys_scales, qpool_word
     with ExitStack() as ctx:
         lists = ctx.enter_context(tc.tile_pool(name="lists", bufs=1))
         keep = ctx.enter_context(tc.tile_pool(name="keep", bufs=1))
+        placed = ctx.enter_context(tc.tile_pool(name="placed", bufs=1))
         psum = ctx.enter_context(tc.psum_pool(name="psum", bufs=1))
 
         def sb_tile(shape, dtype, name, tag=None):
@@ -38,9 +39,9 @@ def tile_attend_rollout_pl_kernel(tc, query, keys_words, keys_scales, qpool_word
         def bank(index, shape, name):
             return psum.tile(shape, F32, name=name, tag="bank%d" % index)
 
-        def zeroed_scale_window(name, tag=None):
-            window = sb_tile([P, T], U8, name, tag)
-            nc.vector.memset(window[:].bitcast(I32), 0)
+        def zeroed_scale_window(engine, name):
+            window = sb_tile([P, T], U8, name)
+            engine.memset(window[:].bitcast(I32), 0)
             return window
 
         def load_scale_rows(queue, window, scales, row):
@@ -48,73 +49,75 @@ def tile_attend_rollout_pl_kernel(tc, query, keys_words, keys_scales, qpool_word
                 queue.dma_start(out=window[32 * quad + row: 32 * quad + row + 4, :].bitcast(I32),
                                 in_=scales[0, 4 * quad: 4 * quad + 4, :].bitcast(I32))
 
+        query_bytes = PACK * Q * 4
+        ks_win = zeroed_scale_window(nc.vector, "ks_win")
+        zeros = placed.tile([P, P], F32, name="zeros", offset=query_bytes - 256, align_bytes=64)
+        nc.vector.memset(zeros[:], 0.0)
+        vec_rows = sb_tile([P, P], F32, "vec_rows")
+        nc.vector.tensor_copy(out=vec_rows[:], in_=zeros[:])
         ident = sb_tile([P, P], F32, "ident")
         make_identity(nc, ident[:])
-        ks_win = zeroed_scale_window("ks_win", "slot_b")
-        qs_win = zeroed_scale_window("qs_win")
-        k2s_win = zeroed_scale_window("k2s_win")
+        qs_win = zeroed_scale_window(nc.vector, "qs_win")
+        k2s_win = zeroed_scale_window(nc.vector, "k2s_win")
+
         offs_sb = lists.tile([P, I // 16], U16, name="offs_sb")
         offs2_sb = lists.tile([P, J // 16], U16, name="offs2_sb")
         nc.sync.dma_start(offs_sb[:], offs)
         nc.sync.dma_start(offs2_sb[:], offs2)
         kw_win = sb_tile([P, T], U16, "kw_win", "slot_a")
         nc.sync.dma_start(out=kw_win[:].bitcast(I32), in_=keys_words[0].bitcast(I32))
-        q_rows = query.rearrange("(p t) q -> p t q", t=PACK)
-        warm = sb_tile([P, 1], F32, "warm")
-        nc.scalar.activation(out=warm[:], in_=ident[:, 0:1], func=ACT.Exp)
-        q_raw = [sb_tile([P, PACK, Q // 2], F32, "q_raw%d" % h) for h in range(2)]
-        nc.sync.dma_start(out=q_raw[0][:], in_=q_rows[:, :, 0:256])
-        sa_cols = sb_tile([P, 4], F32, "sa_cols")
-        nc.sync.dma_start(out=sa_cols[:], in_=sa.rearrange("o (p m) -> (o p) m", m=4))
         load_scale_rows(nc.sync, ks_win, keys_scales, KEYS_ROW)
-        nc.sync.dma_start(out=q_raw[1][:], in_=q_rows[:, :, 256:512])
+        qw_win = placed.tile([P, T], I32, name="qw_win", offset=query_bytes, align_bytes=64)
+        nc.sync.dma_start(out=qw_win[:], in_=qpool_words[0].rearrange("p n t -> p (n t)").bitcast(I32))
+        q_rows = query.rearrange("(p t) q -> p t q", t=PACK)
+        q_both = placed.tile([P, 2, PACK, Q // 2], F32, name="q_both", offset=0, align_bytes=64)
+        q_raw = [q_both[:, 0], q_both[:, 1]]
+        nc.sync.dma_start(out=q_raw[0], in_=q_rows[:, :, 0:256])
+        nc.sync.dma_start(out=q_raw[1], in_=q_rows[:, :, 256:512])
         load_scale_rows(nc.sync, qs_win, qpool_scales, QPOOL_ROW)
 
         kw = sb_tile([P, I], U16, "kw")
         nc.vector.tensor_copy(out=kw[:], in_=kw_win[:].indirect(offs_sb[:]))
         ks = sb_tile([P, I], U8, "ks")
         nc.vector.tensor_copy(out=ks[:], in_=ks_win[:].indirect(offs_sb[:]))
-        qw_win = sb_tile([P, T], I32, "qw_win", "slot_a")
-        nc.sync.dma_start(out=qw_win[:], in_=qpool_words[0].rearrange("p n t -> p (n t)").bitcast(I32))
-        vec_rows = sb_tile([P, P], F32, "vec_rows")
-        nc.gpsimd.memset(vec_rows[:], 0.0)
+        qw = sb_tile([P, I], U32, "qw")
+        nc.vector.tensor_copy(out=qw[:].rearrange("p (t g r) -> p g t r", t=4, r=8),
+                              in_=qw_win[:].bitcast(U32).indirect(offs_sb[:]))
+        k2w_win = sb_tile([P, U], I32, "k2w_win", "slot_a")
+        nc.sync.dma_start(out=k2w_win[:], in_=keys2_words[0].rearrange("p n t -> p (n t)").bitcast(I32))
+        nc.sync.dma_start(out=vec_rows[4:8, :].rearrange("t (g r) -> t g r", r=8),
+                          in_=sa.rearrange("o (g t r) -> t g (r o)", t=4, r=8))
         nc.sync.dma_start(out=vec_rows[0:4, :].rearrange("t (g r) -> t g r", r=8),
                           in_=sb.rearrange("(g t r) o -> t g (r o)", t=4, r=8))
         load_scale_rows(nc.sync, k2s_win, keys2_scales, KEYS2_ROW)
-        k2w_win = sb_tile([P, U], I32, "k2w_win", "slot_b")
-        nc.sync.dma_start(out=k2w_win[:], in_=keys2_words[0].rearrange("p n t -> p (n t)").bitcast(I32))
 
-        sa_ps = bank(6, [P, 4, P], "sa_ps")
-        for m in range(4):
-            nc.tensor.transpose(sa_ps[:, m, :], sa_cols[:, m:m + 1].to_broadcast([P, P]), ident[:])
-        sa_all = sb_tile([P, I], F32, "sa_all")
-        for u in range(2):
-            nc.scalar.copy(out=sa_all[:].rearrange("p (u g s m e) -> p u g s m e", u=2, s=2, m=4, e=2)[:, u],
-                           in_=sa_ps[:].rearrange("p m (g u e s) -> p u g s m e", u=2, e=2, s=2)[:, u])
+        vec_ps = bank(6, [P, P], "vec_ps")
+        nc.tensor.transpose(vec_ps[:], vec_rows[:], ident[:])
+        sa_cols = sb_tile([P, 4], F32, "sa_cols")
+        nc.scalar.copy(out=sa_cols[:], in_=vec_ps[:, 4:8])
+        sb_cols = sb_tile([P, 4], F32, "sb_cols")
+        nc.scalar.activation(out=sb_cols[:], in_=vec_ps[:, 0:4], func=ACT.Copy, scale=512.0)
+        sa_ps = bank(7, [P, 2, P, 2], "sa_ps")
+        for t in range(PACK):
+            nc.tensor.transpose(sa_ps[:, t // 2, :, t % 2], sa_cols[:, t:t + 1].to_broadcast([P, P]), ident[:])
+        sa_all = sa_ps[:].rearrange("p u n e -> p (u n e)")
 
         q_codes = sb_tile([P, Q], U32, "q_codes")
         q_scales = sb_tile([P, Q], U8, "q_scales")
-        for h in range(2):
+        neg_max = sb_tile([P, 8], F32, "neg_max")
+        sums = sb_tile([P, 8], F32, "sums")
+        inv = sb_tile([P, 8], F32, "inv")
+        p_tiles = []
+
+        def quantise_query(h):
             q_bf = sb_tile([P, Q // 2, PACK], BF16, "q_bf%d" % h)
             nc.scalar.copy(out=q_bf[:].rearrange("p (c i) t -> p c t i", i=4),
-                           in_=q_raw[h][:].rearrange("p t (c i) -> p c t i", i=4))
+                           in_=q_raw[h].rearrange("p t (c i) -> p c t i", i=4))
             cols = slice(h * 256, (h + 1) * 256)
             nc.vector.quantize_mx(out=q_codes[:, cols].bitcast(FP8X4), scales=q_scales[:, cols],
                                   in_=q_bf[:].rearrange("p c t -> p (c t)"))
 
-        qs_list = sb_tile([P, I], U8, "qs_list")
-        nc.vector.tensor_copy(out=qs_list[:], in_=qs_win[:].indirect(offs_sb[:]))
-        k2s = sb_tile([P, J], U8, "k2s", "q_bf1")
-        nc.vector.tensor_copy(out=k2s[:], in_=k2s_win[:].indirect(offs2_sb[:]))
-        qs = sb_tile([P, I], U8, "qs")
-        nc.vector.tensor_copy(out=qs[:].bitcast(I32).rearrange("p (t g w) -> p g t w", t=4, w=2),
-                              in_=qs_list[:].bitcast(I32).rearrange("p (g t w) -> p g t w", t=4, w=2))
-
-        neg_max = sb_tile([P, 4], F32, "neg_max")
-        sums = sb_tile([P, 8], F32, "sums")
-        inv = sb_tile([P, 8], F32, "inv")
-        p_tiles = []
-        for n in range(4):
+        def first_map(n):
             a_ps = bank(n, [P, I], "a_ps%d" % n)
             cols = slice(n * P, (n + 1) * P)
             nc.tensor.matmul_mx(out=a_ps[:], lhsT=q_codes[:, cols].bitcast(FP8X4), lhsT_scale=q_scales[:, cols],
@@ -126,61 +129,73 @@ def tile_attend_rollout_pl_kernel(tc, query, keys_words, keys_scales, qpool_word
                                  func=ACT.Exp, bias=neg_max[:, n:n + 1], accum_out=sums[:, n:n + 1])
             p_tiles.append(p_n)
 
-        qw = sb_tile([P, I], U32, "qw")
-        nc.vector.tensor_copy(out=qw[:].rearrange("p (t g r) -> p g t r", t=4, r=8),
-                              in_=qw_win[:].bitcast(U32).indirect(offs_sb[:]))
+        quantise_query(0)
+        qs_list = sb_tile([P, I], U8, "qs_list")
+        nc.vector.tensor_copy(out=qs_list[:], in_=qs_win[:].indirect(offs_sb[:]))
+        quantise_query(1)
+        first_map(0)
+        first_map(1)
+        qs = sb_tile([P, I], U8, "qs")
+        nc.vector.tensor_copy(out=qs[:].bitcast(I32).rearrange("p (t g w) -> p g t w", t=4, w=2),
+                              in_=qs_list[:].bitcast(I32).rearrange("p (g t w) -> p g t w", t=4, w=2))
+        k2w = sb_tile([P, J], U32, "k2w")
+        nc.vector.tensor_copy(out=k2w[:], in_=k2w_win[:].bitcast(U32).indirect(offs2_sb[:]))
+        first_map(2)
+        k2s = sb_tile([P, J], U8, "k2s")
+        nc.vector.tensor_copy(out=k2s[:], in_=k2s_win[:].indirect(offs2_sb[:]))
+        first_map(3)
 
         wt_bf = sb_tile([P, Q * PACK], BF16, "wt_bf")
         wt_words = wt_bf[:].bitcast(F32).rearrange("p (t m u) -> p t m u", t=4, u=2)
 
-        wt_ps = [None, None]
+        def weights(h):
+            nc.vector.reciprocal(out=inv[:, 2 * h:2 * h + 2], in_=sums[:, 2 * h:2 * h + 2])
+            wt_ps = bank(h, [P, 2, 256], "wt_ps%d" % h)
+            for k in range(2):
+                n = 2 * h + k
+                w_n = sb_tile([P, I], BF16, "w%d" % n, "k2s_win" if n == 0 else None)
+                nc.vector.scalar_tensor_tensor(out=w_n[:], in0=p_tiles[n][:], scalar=inv[:, n:n + 1], in1=sa_all,
+                                               op0=ALU.mult, op1=ALU.mult)
+                words = w_n[:].bitcast(F32)
+                for u in range(2):
+                    nc.tensor.transpose(wt_ps[:, u, k * P:(k + 1) * P], words[:, u * P:(u + 1) * P], ident[:])
+            nc.scalar.copy(out=wt_words[:, :, 64 * h:64 * (h + 1), :],
+                           in_=wt_ps[:].rearrange("p u (m t) -> p t m u", t=4))
 
-        def weights(n, tag):
-            h = n // 2
-            if n % 2 == 0:
-                nc.vector.reciprocal(out=inv[:, n:n + 2], in_=sums[:, n:n + 2])
-                wt_ps[h] = bank(h, [P, 2, 256], "wt_ps%d" % h)
-            w_n = sb_tile([P, I], BF16, "w%d" % n, tag)
-            nc.vector.scalar_tensor_tensor(out=w_n[:], in0=p_tiles[n][:], scalar=inv[:, n:n + 1], in1=sa_all[:],
-                                           op0=ALU.mult, op1=ALU.mult)
-            words = w_n[:].bitcast(F32)
-            for u in range(2):
-                nc.tensor.transpose(wt_ps[h][:, u, (n % 2) * P:(n % 2 + 1) * P], words[:, u * P:(u + 1) * P], ident[:])
-            if n % 2 == 1:
-                nc.scalar.copy(out=wt_words[:, :, 64 * h:64 * (h + 1), :],
-                               in_=wt_ps[h][:].rearrange("p u (m t) -> p t m u", t=4))
-
-        weights(0, None)
-        weights(1, None)
-        k2w = sb_tile([P, J], U32, "k2w", "p1")
-        nc.vector.tensor_copy(out=k2w[:], in_=k2w_win[:].bitcast(U32).indirect(offs2_sb[:]))
-
-        vec_ps = bank(7, [P, P], "vec_ps")
-        nc.tensor.transpose(vec_ps[:], vec_rows[:], ident[:])
-        sb_cols = sb_tile([P, 4], F32, "sb_cols")
-        nc.scalar.activation(out=sb_cols[:], in_=vec_ps[:, 0:4], func=ACT.Copy, scale=512.0)
         r_all = sb_tile([P, PACK, J], F32, "r_all")
-        for t in range(4):
-            b_ps = bank(4 + t, [P, J], "b_ps%d" % t)
+
+        def second_map(t):
+            b_ps = bank((4, 5, 6, 2)[t], [P, J], "b_ps%d" % t)
             cols = slice(t * P, (t + 1) * P)
             nc.tensor.matmul_mx(out=b_ps[:], lhsT=qw[:, cols].bitcast(FP8X4), lhsT_scale=qs[QPOOL_ROW:P, cols],
                                 rhs=k2w[:].bitcast(FP8X4), rhs_scale=k2s[KEYS2_ROW:P, :], start=True, stop=True)
-            neg_max_b = sb_tile([P, 1], F32, "neg_max_b%d" % t)
-            nc.vector.tensor_reduce(out=neg_max_b[:], in_=b_ps[:], axis=AX.X, op=ALU.max, negate=True)
+            nc.vector.tensor_reduce(out=neg_max[:, 4 + t:5 + t], in_=b_ps[:], axis=AX.X, op=ALU.max, negate=True)
             nc.scalar.activation(out=r_all[:, t, :], in_=b_ps[:], func=ACT.Exp,
-                                 bias=neg_max_b[:], accum_out=sums[:, 4 + t:5 + t])
+                                 bias=neg_max[:, 4 + t:5 + t], accum_out=sums[:, 4 + t:5 + t])
 
-        weights(2, "slot_b")
-        weights(3, "neg_max_b1")
+        weights(0)
+        second_map(0)
+        second_map(1)
+        weights(1)
+        second_map(2)
+        second_map(3)
         wt_codes = sb_tile([P, Q], U32, "wt_codes")
         wt_scales = sb_tile([P, Q], U8, "wt_scales")
+
+        x_rows = sb_tile([P, PACK, J], BF16, "x_rows")
+
+        def scale_x(t):
+            nc.vector.tensor_scalar(out=x_rows[:, t, :], in0=r_all[:, t, :], scalar1=inv[:, 4 + t:5 + t],
+                                    scalar2=sb_cols[:, t:t + 1], op0=ALU.mult, op1=ALU.mult)
+
+        nc.vector.reciprocal(out=inv[:, 4:6], in_=sums[:, 4:6])
+        nc.vector.reciprocal(out=inv[:, 6:7], in_=sums[:, 6:7])
+        scale_x(0)
+        scale_x(1)
         nc.vector.quantize_mx(out=wt_codes[:].bitcast(FP8X4), scales=wt_scales[:], in_=wt_bf[:])
-
-
-        nc.vector.reciprocal(out=inv[:, 4:8], in_=sums[:, 4:8])
-        row_scale = sb_tile([P, 4], F32, "row_scale")
-        nc.vector.tensor_tensor(out=row_scale[:], in0=inv[:, 4:8], in1=sb_cols[:], op=ALU.mult)
-        row_scale_all = row_scale[:].unsqueeze(1).unsqueeze(3).to_broadcast([P, JC // 4, PACK, 4])
+        nc.vector.reciprocal(out=inv[:, 7:8], in_=sums[:, 7:8])
+        scale_x(2)
+        scale_x(3)
 
         x_codes = sb_tile([P, J], U32, "x_codes")
         x_scales = sb_tile([P, J], U8, "x_scales")
@@ -191,26 +206,17 @@ def tile_attend_rollout_pl_kernel(tc, query, keys_words, keys_scales, qpool_word
         x_bf = [sb_tile([P, JC, PACK], BF16, "x_bf%d" % c) for c in range(CHUNKS)]
         y_bf = [sb_tile([P, JC, PACK], BF16, "y_bf%d" % c) for c in range(CHUNKS)]
 
-        def scale_x(c):
+        def interleave_x(c):
             cols = slice(c * JC, (c + 1) * JC)
-            nc.vector.tensor_tensor(out=x_bf[c][:].rearrange("p (c i) t -> p c t i", i=4),
-                                    in0=r_all[:, :, cols].rearrange("p t (c i) -> p c t i", i=4),
-                                    in1=row_scale_all, op=ALU.mult)
-
-        def scale_x_on_scalar(c):
-            cols = slice(c * JC, (c + 1) * JC)
-            x_rows = sb_tile([P, PACK, JC], BF16, "x_rows")
-            for t in range(PACK):
-                nc.scalar.activation(out=x_rows[:, t, :], in_=r_all[:, t, cols], func=ACT.Copy,
-                                     scale=row_scale[:, t:t + 1])
-            nc.scalar.copy(out=x_bf[c][:].rearrange("p (c i) t -> p c t i", i=4),
-                           in_=x_rows[:].rearrange("p t (c i) -> p c t i", i=4))
+            copy = nc.scalar.copy if c in (1, 2) else nc.vector.tensor_copy
+            copy(out=x_bf[c][:].rearrange("p (c i) t -> p c t i", i=4),
+                 in_=x_rows[:, :, cols].rearrange("p t (c i) -> p c t i", i=4))
 
         def product(c):
             cols = slice(c * JC, (c + 1) * JC)
             nc.vector.quantize_mx(out=x_codes[:, cols].bitcast(FP8X4), scales=x_scales[:, cols],
                                   in_=x_bf[c][:].rearrange("p c t -> p (c t)"))
-            y_ps = bank(2 + c, [P, PACK, JC], "y_ps%d" % c)
+            y_ps = bank((3, 7, 0, 1)[c], [P, PACK, JC], "y_ps%d" % c)
             for t in range(4):
                 q_cols = slice(t * P, (t + 1) * P)
                 nc.tensor.matmul_mx(out=y_ps[:, t, :], lhsT=wt_codes[:, q_cols].bitcast(FP8X4),
@@ -235,10 +241,7 @@ def tile_attend_rollout_pl_kernel(tc, query, keys_words, keys_scales, qpool_word
 
         y_tiles = []
         for c in range(CHUNKS):
-            if c == 1:
-                scale_x_on_scalar(c)
-            else:
-                scale_x(c)
+            interleave_x(c)
             y_tiles.append(product(c))
         for c in range(CHUNKS):
             round_y(c, y_tiles[c])

@@ -45,9 +45,8 @@ def tile_attend_rollout_pl_kernel(tc, query, keys_words, keys_scales, qpool_word
             return window
 
         def load_scale_rows(queue, window, scales, row):
-            for quad in range(4):
-                queue.dma_start(out=window[32 * quad + row: 32 * quad + row + 4, :].bitcast(I32),
-                                in_=scales[0, 4 * quad: 4 * quad + 4, :].bitcast(I32))
+            for r in range(4):
+                queue.dma_start(out=window[row + r:P:32, :].bitcast(I32), in_=scales[0, r:16:4, :].bitcast(I32))
 
         query_bytes = PACK * Q * 4
         ks_win = zeroed_scale_window(nc.vector, "ks_win")
@@ -67,22 +66,19 @@ def tile_attend_rollout_pl_kernel(tc, query, keys_words, keys_scales, qpool_word
         kw_win = sb_tile([P, T], U16, "kw_win", "slot_a")
         nc.sync.dma_start(out=kw_win[:].bitcast(I32), in_=keys_words[0].bitcast(I32))
         load_scale_rows(nc.sync, ks_win, keys_scales, KEYS_ROW)
-        qw_win = placed.tile([P, T], I32, name="qw_win", offset=query_bytes, align_bytes=64)
-        nc.sync.dma_start(out=qw_win[:], in_=qpool_words[0].rearrange("p n t -> p (n t)").bitcast(I32))
         q_rows = query.rearrange("(p t) q -> p t q", t=PACK)
         q_both = placed.tile([P, 2, PACK, Q // 2], F32, name="q_both", offset=0, align_bytes=64)
         q_raw = [q_both[:, 0], q_both[:, 1]]
         nc.sync.dma_start(out=q_raw[0], in_=q_rows[:, :, 0:256])
         nc.sync.dma_start(out=q_raw[1], in_=q_rows[:, :, 256:512])
         load_scale_rows(nc.sync, qs_win, qpool_scales, QPOOL_ROW)
+        qw_win = placed.tile([P, T], I32, name="qw_win", offset=query_bytes, align_bytes=64)
+        nc.sync.dma_start(out=qw_win[:], in_=qpool_words[0].rearrange("p n t -> p (n t)").bitcast(I32))
 
         kw = sb_tile([P, I], U16, "kw")
         nc.vector.tensor_copy(out=kw[:], in_=kw_win[:].indirect(offs_sb[:]))
         ks = sb_tile([P, I], U8, "ks")
         nc.vector.tensor_copy(out=ks[:], in_=ks_win[:].indirect(offs_sb[:]))
-        qw = sb_tile([P, I], U32, "qw")
-        nc.vector.tensor_copy(out=qw[:].rearrange("p (t g r) -> p g t r", t=4, r=8),
-                              in_=qw_win[:].bitcast(U32).indirect(offs_sb[:]))
         k2w_win = sb_tile([P, U], I32, "k2w_win", "slot_a")
         nc.sync.dma_start(out=k2w_win[:], in_=keys2_words[0].rearrange("p n t -> p (n t)").bitcast(I32))
         nc.sync.dma_start(out=vec_rows[4:8, :].rearrange("t (g r) -> t g r", r=8),
@@ -138,6 +134,9 @@ def tile_attend_rollout_pl_kernel(tc, query, keys_words, keys_scales, qpool_word
         qs = sb_tile([P, I], U8, "qs")
         nc.vector.tensor_copy(out=qs[:].bitcast(I32).rearrange("p (t g w) -> p g t w", t=4, w=2),
                               in_=qs_list[:].bitcast(I32).rearrange("p (g t w) -> p g t w", t=4, w=2))
+        qw = sb_tile([P, I], U32, "qw")
+        nc.vector.tensor_copy(out=qw[:].rearrange("p (t g r) -> p g t r", t=4, r=8),
+                              in_=qw_win[:].bitcast(U32).indirect(offs_sb[:]))
         k2w = sb_tile([P, J], U32, "k2w")
         nc.vector.tensor_copy(out=k2w[:], in_=k2w_win[:].bitcast(U32).indirect(offs2_sb[:]))
         first_map(2)
@@ -162,7 +161,7 @@ def tile_attend_rollout_pl_kernel(tc, query, keys_words, keys_scales, qpool_word
             nc.scalar.copy(out=wt_words[:, :, 64 * h:64 * (h + 1), :],
                            in_=wt_ps[:].rearrange("p u (m t) -> p t m u", t=4))
 
-        r_all = sb_tile([P, PACK, J], F32, "r_all")
+        r_rows = []
 
         def second_map(t):
             b_ps = bank((4, 5, 6, 2)[t], [P, J], "b_ps%d" % t)
@@ -170,32 +169,48 @@ def tile_attend_rollout_pl_kernel(tc, query, keys_words, keys_scales, qpool_word
             nc.tensor.matmul_mx(out=b_ps[:], lhsT=qw[:, cols].bitcast(FP8X4), lhsT_scale=qs[QPOOL_ROW:P, cols],
                                 rhs=k2w[:].bitcast(FP8X4), rhs_scale=k2s[KEYS2_ROW:P, :], start=True, stop=True)
             nc.vector.tensor_reduce(out=neg_max[:, 4 + t:5 + t], in_=b_ps[:], axis=AX.X, op=ALU.max, negate=True)
-            nc.scalar.activation(out=r_all[:, t, :], in_=b_ps[:], func=ACT.Exp,
+            r_rows.append(sb_tile([P, J], F32, "r%d" % t, "w3" if t == 2 else None))
+            nc.scalar.activation(out=r_rows[t][:], in_=b_ps[:], func=ACT.Exp,
                                  bias=neg_max[:, 4 + t:5 + t], accum_out=sums[:, 4 + t:5 + t])
+
+        x_pairs = sb_tile([P, 2 * J * 2], BF16, "x_pairs")
+        x_places = x_pairs[:].rearrange("p (u j e) -> p u j e", u=2, e=2)
+        x_both = x_pairs[:].bitcast(F32).rearrange("p (u j) -> p u j", u=2)
+        x_bf = [sb_tile([P, JC, PACK], BF16, "x_bf%d" % c) for c in range(CHUNKS)]
+
+        def scale_x(engine, t, cols, out, inv_t):
+            engine.tensor_scalar(out=out, in0=r_rows[t][:, cols], scalar1=inv_t,
+                                 scalar2=sb_cols[:, t:t + 1], op0=ALU.mult, op1=ALU.mult)
+
+        def weave_x(copy, c, halves):
+            words = x_bf[c][:].rearrange("p c t -> p (c t)").bitcast(F32).rearrange("p (c u) -> p c u", u=2)
+            copy(out=words[:, :, halves], in_=x_both[:, halves, c * JC:(c + 1) * JC].rearrange("p u c -> p c u"))
+
+        first, rest = slice(0, JC), slice(JC, J)
+
+        def early_row(t):
+            nc.vector.reciprocal(out=inv[:, 4 + t:5 + t], in_=sums[:, 4 + t:5 + t])
+            scale_x(nc.gpsimd, t, slice(0, J), x_places[:, 0, :, t], inv[:, 4 + t:5 + t])
 
         weights(0)
         second_map(0)
         second_map(1)
+        early_row(0)
+        early_row(1)
         weights(1)
         second_map(2)
         second_map(3)
         wt_codes = sb_tile([P, Q], U32, "wt_codes")
         wt_scales = sb_tile([P, Q], U8, "wt_scales")
 
-        x_rows = sb_tile([P, PACK, J], BF16, "x_rows")
-
-        def scale_x(t):
-            nc.vector.tensor_scalar(out=x_rows[:, t, :], in0=r_all[:, t, :], scalar1=inv[:, 4 + t:5 + t],
-                                    scalar2=sb_cols[:, t:t + 1], op0=ALU.mult, op1=ALU.mult)
-
-        nc.vector.reciprocal(out=inv[:, 4:6], in_=sums[:, 4:6])
-        nc.vector.reciprocal(out=inv[:, 6:7], in_=sums[:, 6:7])
-        scale_x(0)
-        scale_x(1)
         nc.vector.quantize_mx(out=wt_codes[:].bitcast(FP8X4), scales=wt_scales[:], in_=wt_bf[:])
-        nc.vector.reciprocal(out=inv[:, 7:8], in_=sums[:, 7:8])
-        scale_x(2)
-        scale_x(3)
+        nc.vector.reciprocal(out=inv[:, 6:7], in_=sums[:, 6:7])
+        weave_x(nc.vector.tensor_copy, 0, slice(0, 1))
+        scale_x(nc.vector, 2, first, x_bf[0][:, :, 2], inv[:, 6:7])
+        last_inv = sb_tile([P, 2], F32, "last_inv")
+        nc.vector.reciprocal(out=last_inv[:], in_=sums[:, 6:8])
+        scale_x(nc.vector, 3, first, x_bf[0][:, :, 3], last_inv[:, 1:2])
+        scale_x(nc.vector, 2, rest, x_places[:, 1, rest, 0], last_inv[:, 0:1])
 
         x_codes = sb_tile([P, J], U32, "x_codes")
         x_scales = sb_tile([P, J], U8, "x_scales")
@@ -203,27 +218,23 @@ def tile_attend_rollout_pl_kernel(tc, query, keys_words, keys_scales, qpool_word
         y_scales = sb_tile([P, J], U8, "y_scales")
         y_rows = out_0.rearrange("(p t) j -> p t j", t=PACK)
         y_words = out_1[0].rearrange("p c r -> p (c r)").bitcast(I32)
-        x_bf = [sb_tile([P, JC, PACK], BF16, "x_bf%d" % c) for c in range(CHUNKS)]
         y_bf = [sb_tile([P, JC, PACK], BF16, "y_bf%d" % c) for c in range(CHUNKS)]
-
-        def interleave_x(c):
-            cols = slice(c * JC, (c + 1) * JC)
-            copy = nc.scalar.copy if c in (1, 2) else nc.vector.tensor_copy
-            copy(out=x_bf[c][:].rearrange("p (c i) t -> p c t i", i=4),
-                 in_=x_rows[:, :, cols].rearrange("p t (c i) -> p c t i", i=4))
 
         def product(c):
             cols = slice(c * JC, (c + 1) * JC)
             nc.vector.quantize_mx(out=x_codes[:, cols].bitcast(FP8X4), scales=x_scales[:, cols],
                                   in_=x_bf[c][:].rearrange("p c t -> p (c t)"))
-            y_ps = bank((3, 7, 0, 1)[c], [P, PACK, JC], "y_ps%d" % c)
-            for t in range(4):
-                q_cols = slice(t * P, (t + 1) * P)
-                nc.tensor.matmul_mx(out=y_ps[:, t, :], lhsT=wt_codes[:, q_cols].bitcast(FP8X4),
-                                    lhsT_scale=wt_scales[:, q_cols], rhs=x_codes[:, cols].bitcast(FP8X4),
-                                    rhs_scale=x_scales[:, cols], start=True, stop=True)
             y_sb = sb_tile([P, PACK, JC], F32, "y_sb%d" % c)
-            nc.scalar.copy(out=y_sb[:], in_=y_ps[:])
+            banks = ((3, 4), (7,), (0,), (1,))[c]
+            places = PACK // len(banks)
+            for b, index in enumerate(banks):
+                y_ps = bank(index, [P, places, JC], "y_ps%d_%d" % (c, b))
+                for k in range(places):
+                    q_cols = slice((b * places + k) * P, (b * places + k + 1) * P)
+                    nc.tensor.matmul_mx(out=y_ps[:, k, :], lhsT=wt_codes[:, q_cols].bitcast(FP8X4),
+                                        lhsT_scale=wt_scales[:, q_cols], rhs=x_codes[:, cols].bitcast(FP8X4),
+                                        rhs_scale=x_scales[:, cols], start=True, stop=True)
+                nc.scalar.copy(out=y_sb[:, b * places:(b + 1) * places, :], in_=y_ps[:])
             nc.sync.dma_start(out=y_rows[:, :, cols], in_=y_sb[:])
             return y_sb
 
@@ -239,13 +250,19 @@ def tile_attend_rollout_pl_kernel(tc, query, keys_words, keys_scales, qpool_word
                 done = slice(0, (c + 1) * JC) if c == CHUNKS - 2 else cols
                 nc.sync.dma_start(out=y_words[:, done], in_=y_codes[:, done].bitcast(I32))
 
-        y_tiles = []
-        for c in range(CHUNKS):
-            interleave_x(c)
+        y_tiles = [product(0)]
+        scale_x(nc.vector, 3, rest, x_places[:, 1, rest, 1], last_inv[:, 1:2])
+        for c in range(1, CHUNKS):
+            weave_x(nc.scalar.copy if c == 2 else nc.vector.tensor_copy, c, slice(0, 2))
+        for c in range(1, CHUNKS):
             y_tiles.append(product(c))
-        for c in range(CHUNKS):
-            round_y(c, y_tiles[c])
+        round_y(0, y_tiles[0])
+        for c in range(CHUNKS - 2):
+            round_y(c + 1, y_tiles[c + 1])
             planes(c)
+        planes(CHUNKS - 2)
+        round_y(CHUNKS - 1, y_tiles[CHUNKS - 1])
+        planes(CHUNKS - 1)
         for quad in range(4):
             queue = nc.scalar if quad % 2 else nc.sync
             queue.dma_start(out=out_2[0, 4 * quad:4 * quad + 4, :].bitcast(I32),

@@ -178,9 +178,9 @@ def tile_attend_rollout_pl_kernel(tc, query, keys_words, keys_scales, qpool_word
         x_both = x_pairs[:].bitcast(F32).rearrange("p (u j) -> p u j", u=2)
         x_bf = [sb_tile([P, JC, PACK], BF16, "x_bf%d" % c) for c in range(CHUNKS)]
 
-        def scale_x(engine, t, cols, out, inv_t):
-            engine.tensor_scalar(out=out, in0=r_rows[t][:, cols], scalar1=inv_t,
-                                 scalar2=sb_cols[:, t:t + 1], op0=ALU.mult, op1=ALU.mult)
+        def scale_x(t, cols, out, inv_t):
+            nc.vector.tensor_scalar(out=out, in0=r_rows[t][:, cols], scalar1=inv_t,
+                                    scalar2=sb_cols[:, t:t + 1], op0=ALU.mult, op1=ALU.mult)
 
         def weave_x(copy, c, halves):
             words = x_bf[c][:].rearrange("p c t -> p (c t)").bitcast(F32).rearrange("p (c u) -> p c u", u=2)
@@ -190,7 +190,7 @@ def tile_attend_rollout_pl_kernel(tc, query, keys_words, keys_scales, qpool_word
 
         def early_row(t):
             nc.vector.reciprocal(out=inv[:, 4 + t:5 + t], in_=sums[:, 4 + t:5 + t])
-            scale_x(nc.gpsimd, t, slice(0, J), x_places[:, 0, :, t], inv[:, 4 + t:5 + t])
+            scale_x(t, slice(0, J), x_places[:, 0, :, t], inv[:, 4 + t:5 + t])
 
         weights(0)
         second_map(0)
@@ -206,11 +206,11 @@ def tile_attend_rollout_pl_kernel(tc, query, keys_words, keys_scales, qpool_word
         nc.vector.quantize_mx(out=wt_codes[:].bitcast(FP8X4), scales=wt_scales[:], in_=wt_bf[:])
         nc.vector.reciprocal(out=inv[:, 6:7], in_=sums[:, 6:7])
         weave_x(nc.vector.tensor_copy, 0, slice(0, 1))
-        scale_x(nc.vector, 2, first, x_bf[0][:, :, 2], inv[:, 6:7])
+        scale_x(2, first, x_bf[0][:, :, 2], inv[:, 6:7])
         last_inv = sb_tile([P, 2], F32, "last_inv")
         nc.vector.reciprocal(out=last_inv[:], in_=sums[:, 6:8])
-        scale_x(nc.vector, 3, first, x_bf[0][:, :, 3], last_inv[:, 1:2])
-        scale_x(nc.vector, 2, rest, x_places[:, 1, rest, 0], last_inv[:, 0:1])
+        scale_x(3, first, x_bf[0][:, :, 3], last_inv[:, 1:2])
+        scale_x(2, rest, x_places[:, 1, rest, 0], last_inv[:, 0:1])
 
         x_codes = sb_tile([P, J], U32, "x_codes")
         x_scales = sb_tile([P, J], U8, "x_scales")
@@ -251,7 +251,7 @@ def tile_attend_rollout_pl_kernel(tc, query, keys_words, keys_scales, qpool_word
                 nc.sync.dma_start(out=y_words[:, done], in_=y_codes[:, done].bitcast(I32))
 
         y_tiles = [product(0)]
-        scale_x(nc.vector, 3, rest, x_places[:, 1, rest, 1], last_inv[:, 1:2])
+        scale_x(3, rest, x_places[:, 1, rest, 1], last_inv[:, 1:2])
         for c in range(1, CHUNKS):
             weave_x(nc.scalar.copy if c == 2 else nc.vector.tensor_copy, c, slice(0, 2))
         for c in range(1, CHUNKS):

@@ -22,6 +22,7 @@ FLOPS = 2 * D * Q * I + 2 * D * I * J + 2 * I * Q * J
 KEYS_ROW, KEYS2_ROW, QPOOL_ROW = 0, 4, 8
 CHUNKS = 4
 JC = J // CHUNKS
+SCALAR_COLS = 256
 
 
 def tile_attend_rollout_pl_kernel(tc, query, keys_words, keys_scales, qpool_words, qpool_scales,
@@ -134,21 +135,21 @@ def tile_attend_rollout_pl_kernel(tc, query, keys_words, keys_scales, qpool_word
         qs = sb_tile([P, I], U8, "qs")
         nc.vector.tensor_copy(out=qs[:].bitcast(I32).rearrange("p (t g w) -> p g t w", t=4, w=2),
                               in_=qs_list[:].bitcast(I32).rearrange("p (g t w) -> p g t w", t=4, w=2))
+        first_map(2)
+        first_map(3)
         qw = sb_tile([P, I], U32, "qw")
         nc.vector.tensor_copy(out=qw[:].rearrange("p (t g r) -> p g t r", t=4, r=8),
                               in_=qw_win[:].bitcast(U32).indirect(offs_sb[:]))
+        nc.vector.reciprocal(out=inv[:, 0:4], in_=sums[:, 0:4])
         k2w = sb_tile([P, J], U32, "k2w")
         nc.vector.tensor_copy(out=k2w[:], in_=k2w_win[:].bitcast(U32).indirect(offs2_sb[:]))
-        first_map(2)
         k2s = sb_tile([P, J], U8, "k2s")
         nc.vector.tensor_copy(out=k2s[:], in_=k2s_win[:].indirect(offs2_sb[:]))
-        first_map(3)
 
         wt_bf = sb_tile([P, Q * PACK], BF16, "wt_bf")
         wt_words = wt_bf[:].bitcast(F32).rearrange("p (t m u) -> p t m u", t=4, u=2)
 
         def weights(h):
-            nc.vector.reciprocal(out=inv[:, 2 * h:2 * h + 2], in_=sums[:, 2 * h:2 * h + 2])
             wt_ps = bank(h, [P, 2, 256], "wt_ps%d" % h)
             for k in range(2):
                 n = 2 * h + k
@@ -188,22 +189,30 @@ def tile_attend_rollout_pl_kernel(tc, query, keys_words, keys_scales, qpool_word
 
         first, rest = slice(0, JC), slice(JC, J)
 
-        def early_row(t):
-            nc.vector.reciprocal(out=inv[:, 4 + t:5 + t], in_=sums[:, 4 + t:5 + t])
-            scale_x(t, slice(0, J), x_places[:, 0, :, t], inv[:, 4 + t:5 + t])
-
         weights(0)
         second_map(0)
         second_map(1)
-        early_row(0)
-        early_row(1)
+        nc.vector.reciprocal(out=inv[:, 4:6], in_=sums[:, 4:6])
+        row_scale = sb_tile([P, 2], F32, "row_scale")
+        for t in range(2):
+            nc.scalar.activation(out=row_scale[:, t:t + 1], in_=sb_cols[:, t:t + 1], func=ACT.Copy,
+                                 scale=inv[:, 4 + t:5 + t])
+        for t in range(2):
+            nc.scalar.activation(out=x_places[:, 0, 0:SCALAR_COLS, t], in_=r_rows[t][:, 0:SCALAR_COLS], func=ACT.Copy,
+                                 scale=row_scale[:, t:t + 1])
         weights(1)
         second_map(2)
         second_map(3)
+        spare_ps = bank(6, [P, J], "spare_ps")
+        for repeat in range(3):
+            nc.tensor.matmul_mx(out=spare_ps[:], lhsT=qw[:, 0:P].bitcast(FP8X4), lhsT_scale=qs[QPOOL_ROW:P, 0:P],
+                                rhs=k2w[:].bitcast(FP8X4), rhs_scale=k2s[KEYS2_ROW:P, :], start=True, stop=True)
         wt_codes = sb_tile([P, Q], U32, "wt_codes")
         wt_scales = sb_tile([P, Q], U8, "wt_scales")
 
         nc.vector.quantize_mx(out=wt_codes[:].bitcast(FP8X4), scales=wt_scales[:], in_=wt_bf[:])
+        for t in range(2):
+            scale_x(t, slice(SCALAR_COLS, J), x_places[:, 0, SCALAR_COLS:J, t], inv[:, 4 + t:5 + t])
         nc.vector.reciprocal(out=inv[:, 6:7], in_=sums[:, 6:7])
         weave_x(nc.vector.tensor_copy, 0, slice(0, 1))
         scale_x(2, first, x_bf[0][:, :, 2], inv[:, 6:7])

@@ -55,10 +55,11 @@ def tile_attend_rollout_pl_kernel(tc, query, keys_words, keys_scales, qpool_word
         nc.vector.memset(zeros[:], 0.0)
         vec_rows = sb_tile([P, P], F32, "vec_rows")
         nc.vector.tensor_copy(out=vec_rows[:], in_=zeros[:])
-        ident = sb_tile([P, P], F32, "ident")
-        make_identity(nc, ident[:])
         qs_win = zeroed_scale_window(nc.vector, "qs_win")
         k2s_win = zeroed_scale_window(nc.vector, "k2s_win")
+        ident = sb_tile([P, P], F32, "ident")
+        nc.vector.memset(ident[:], 0.0)
+        make_identity(nc, ident[:], nomemset=True)
 
         offs_sb = lists.tile([P, I // 16], U16, name="offs_sb")
         offs2_sb = lists.tile([P, J // 16], U16, name="offs2_sb")
@@ -66,7 +67,7 @@ def tile_attend_rollout_pl_kernel(tc, query, keys_words, keys_scales, qpool_word
         nc.sync.dma_start(offs2_sb[:], offs2)
         kw_win = sb_tile([P, T], U16, "kw_win", "slot_a")
         nc.sync.dma_start(out=kw_win[:].bitcast(I32), in_=keys_words[0].bitcast(I32))
-        load_scale_rows(nc.sync, ks_win, keys_scales, KEYS_ROW)
+        load_scale_rows(nc.scalar, ks_win, keys_scales, KEYS_ROW)
         q_rows = query.rearrange("(p t) q -> p t q", t=PACK)
         q_both = placed.tile([P, 2, PACK, Q // 2], F32, name="q_both", offset=0, align_bytes=64)
         q_raw = [q_both[:, 0], q_both[:, 1]]

@@ -244,8 +244,9 @@ def tile_attend_rollout_pl_kernel(tc, query, keys_words, keys_scales, qpool_word
                     nc.tensor.matmul_mx(out=y_ps[:, k, :], lhsT=wt_codes[:, q_cols].bitcast(FP8X4),
                                         lhsT_scale=wt_scales[:, q_cols], rhs=x_codes[:, cols].bitcast(FP8X4),
                                         rhs_scale=x_scales[:, cols], start=True, stop=True)
-                nc.scalar.copy(out=y_sb[:, b * places:(b + 1) * places, :], in_=y_ps[:])
-            nc.sync.dma_start(out=y_rows[:, :, cols], in_=y_sb[:])
+                part = slice(b * places, (b + 1) * places)
+                nc.scalar.copy(out=y_sb[:, part, :], in_=y_ps[:])
+                nc.sync.dma_start(out=y_rows[:, part, cols], in_=y_sb[:, part, :])
             return y_sb
 
         def round_y(c, y_sb):

@@ -22,7 +22,6 @@ FLOPS = 2 * D * Q * I + 2 * D * I * J + 2 * I * Q * J
 KEYS_ROW, KEYS2_ROW, QPOOL_ROW = 0, 4, 8
 CHUNKS = 4
 JC = J // CHUNKS
-SCALAR_COLS = 256
 
 
 def tile_attend_rollout_pl_kernel(tc, query, keys_words, keys_scales, qpool_words, qpool_scales,
@@ -81,12 +80,12 @@ def tile_attend_rollout_pl_kernel(tc, query, keys_words, keys_scales, qpool_word
         nc.vector.tensor_copy(out=kw[:], in_=kw_win[:].indirect(offs_sb[:]))
         ks = sb_tile([P, I], U8, "ks")
         nc.vector.tensor_copy(out=ks[:], in_=ks_win[:].indirect(offs_sb[:]))
-        k2w_win = sb_tile([P, U], I32, "k2w_win", "slot_a")
-        nc.sync.dma_start(out=k2w_win[:], in_=keys2_words[0].rearrange("p n t -> p (n t)").bitcast(I32))
         nc.sync.dma_start(out=vec_rows[4:8, :].rearrange("t (g r) -> t g r", r=8),
                           in_=sa.rearrange("o (g t r) -> t g (r o)", t=4, r=8))
         nc.sync.dma_start(out=vec_rows[0:4, :].rearrange("t (g r) -> t g r", r=8),
                           in_=sb.rearrange("(g t r) o -> t g (r o)", t=4, r=8))
+        k2w_win = sb_tile([P, U], I32, "k2w_win", "slot_a")
+        nc.sync.dma_start(out=k2w_win[:], in_=keys2_words[0].rearrange("p n t -> p (n t)").bitcast(I32))
         load_scale_rows(nc.sync, k2s_win, keys2_scales, KEYS2_ROW)
 
         vec_ps = bank(6, [P, P], "vec_ps")
@@ -122,9 +121,13 @@ def tile_attend_rollout_pl_kernel(tc, query, keys_words, keys_scales, qpool_word
                                 rhs=kw[:].bitcast(FP4X4), rhs_scale=ks[:], start=True, stop=True)
             nc.vector.tensor_reduce(out=neg_max[:, n:n + 1], in_=a_ps[:], axis=AX.X, op=ALU.max, negate=True)
             p_n = sb_tile([P, I], F32, "p%d" % n)
-            nc.scalar.activation(out=p_n[:].rearrange("p (u g r e) -> p g u r e", u=2, r=8, e=2),
-                                 in_=a_ps[:].rearrange("p (g u e r) -> p g u r e", u=2, r=8, e=2),
-                                 func=ACT.Exp, bias=neg_max[:, n:n + 1], accum_out=sums[:, n:n + 1])
+            if n < 2:
+                dealt = p_n[:].rearrange("p (t g r) -> p g t r", t=PACK, r=8)
+                scores = a_ps[:].rearrange("p (g t r) -> p g t r", t=PACK, r=8)
+            else:
+                dealt = p_n[:].rearrange("p (u g r e) -> p g u r e", u=2, r=8, e=2)
+                scores = a_ps[:].rearrange("p (g u e r) -> p g u r e", u=2, r=8, e=2)
+            nc.scalar.activation(out=dealt, in_=scores, func=ACT.Exp, bias=neg_max[:, n:n + 1], accum_out=sums[:, n:n + 1])
             p_tiles.append(p_n)
 
         quantise_query(0)
@@ -137,11 +140,18 @@ def tile_attend_rollout_pl_kernel(tc, query, keys_words, keys_scales, qpool_word
         nc.vector.tensor_copy(out=qs[:].bitcast(I32).rearrange("p (t g w) -> p g t w", t=4, w=2),
                               in_=qs_list[:].bitcast(I32).rearrange("p (g t w) -> p g t w", t=4, w=2))
         first_map(2)
+        minus_one = sb_tile([P, 2], F32, "minus_one")
+        nc.vector.memset(minus_one[:], -1.0)
+        early_inv = sb_tile([P, 2], F32, "early_inv")
+        nc.gpsimd.tensor_tensor(out=early_inv[:], in0=sums[:, 0:2], in1=minus_one[:], op=ALU.pow)
         first_map(3)
+        shares = [sb_tile([P, I], F32, "share%d" % n) for n in range(2)]
+        for n in range(2):
+            nc.scalar.activation(out=shares[n][:], in_=p_tiles[n][:], func=ACT.Copy, scale=early_inv[:, n:n + 1])
         qw = sb_tile([P, I], U32, "qw")
         nc.vector.tensor_copy(out=qw[:].rearrange("p (t g r) -> p g t r", t=4, r=8),
                               in_=qw_win[:].bitcast(U32).indirect(offs_sb[:]))
-        nc.vector.reciprocal(out=inv[:, 0:4], in_=sums[:, 0:4])
+        nc.vector.reciprocal(out=inv[:, 2:4], in_=sums[:, 2:4])
         k2w = sb_tile([P, J], U32, "k2w")
         nc.vector.tensor_copy(out=k2w[:], in_=k2w_win[:].bitcast(U32).indirect(offs2_sb[:]))
         k2s = sb_tile([P, J], U8, "k2s")
@@ -150,18 +160,27 @@ def tile_attend_rollout_pl_kernel(tc, query, keys_words, keys_scales, qpool_word
         wt_bf = sb_tile([P, Q * PACK], BF16, "wt_bf")
         wt_words = wt_bf[:].bitcast(F32).rearrange("p (t m u) -> p t m u", t=4, u=2)
 
-        def weights(h):
-            wt_ps = bank(h, [P, 2, 256], "wt_ps%d" % h)
-            for k in range(2):
-                n = 2 * h + k
-                w_n = sb_tile([P, I], BF16, "w%d" % n, "k2s_win" if n == 0 else None)
-                nc.vector.scalar_tensor_tensor(out=w_n[:], in0=p_tiles[n][:], scalar=inv[:, n:n + 1], in1=sa_all,
-                                               op0=ALU.mult, op1=ALU.mult)
-                words = w_n[:].bitcast(F32)
-                for u in range(2):
-                    nc.tensor.transpose(wt_ps[:, u, k * P:(k + 1) * P], words[:, u * P:(u + 1) * P], ident[:])
-            nc.scalar.copy(out=wt_words[:, :, 64 * h:64 * (h + 1), :],
-                           in_=wt_ps[:].rearrange("p u (m t) -> p t m u", t=4))
+        def weights_on_scalar():
+            turned = [bank(u, [P, 2, 256], "turned%d" % u) for u in range(2)]
+            for n in range(2):
+                for t in range(PACK):
+                    nc.tensor.transpose(turned[t // 2][:, t % 2, n * P:(n + 1) * P], shares[n][:, t * P:(t + 1) * P],
+                                        ident[:])
+            pairs = sb_tile([P, 2 * 256 * 2], BF16, "w_pairs")
+            places = pairs[:].rearrange("p (u k m e) -> p u e k m", u=2, k=PACK, e=2)
+            for t in range(PACK):
+                nc.scalar.activation(out=places[:, t // 2, t % 2], func=ACT.Copy, scale=sa_cols[:, t:t + 1],
+                                     in_=turned[t // 2][:, t % 2, :].rearrange("p (m k) -> p k m", k=PACK))
+            nc.scalar.copy(out=wt_words[:, :, 0:64, :],
+                           in_=pairs[:].bitcast(F32).rearrange("p (u k m) -> p k m u", u=2, k=PACK))
+
+        def weigh(n, tag):
+            w_n = sb_tile([P, I], BF16, "w%d" % n, tag)
+            nc.vector.scalar_tensor_tensor(out=w_n[:], in0=p_tiles[n][:], scalar=inv[:, n:n + 1], in1=sa_all,
+                                           op0=ALU.mult, op1=ALU.mult)
+            words = w_n[:].bitcast(F32)
+            for u in range(2):
+                nc.tensor.transpose(wt_ps[:, u, (n - 2) * P:(n - 1) * P], words[:, u * P:(u + 1) * P], ident[:])
 
         r_rows = []
 
@@ -190,18 +209,13 @@ def tile_attend_rollout_pl_kernel(tc, query, keys_words, keys_scales, qpool_word
 
         first, rest = slice(0, JC), slice(JC, J)
 
-        weights(0)
+        weights_on_scalar()
+        wt_ps = bank(3, [P, 2, 256], "wt_ps")
+        weigh(2, "k2s_win")
         second_map(0)
         second_map(1)
-        nc.vector.reciprocal(out=inv[:, 4:6], in_=sums[:, 4:6])
-        row_scale = sb_tile([P, 2], F32, "row_scale")
-        for t in range(2):
-            nc.scalar.activation(out=row_scale[:, t:t + 1], in_=sb_cols[:, t:t + 1], func=ACT.Copy,
-                                 scale=inv[:, 4 + t:5 + t])
-        for t in range(2):
-            nc.scalar.activation(out=x_places[:, 0, 0:SCALAR_COLS, t], in_=r_rows[t][:, 0:SCALAR_COLS], func=ACT.Copy,
-                                 scale=row_scale[:, t:t + 1])
-        weights(1)
+        weigh(3, None)
+        nc.scalar.copy(out=wt_words[:, :, 64:128, :], in_=wt_ps[:].rearrange("p u (m t) -> p t m u", t=4))
         second_map(2)
         second_map(3)
         spare_ps = bank(6, [P, J], "spare_ps")
@@ -211,16 +225,17 @@ def tile_attend_rollout_pl_kernel(tc, query, keys_words, keys_scales, qpool_word
         wt_codes = sb_tile([P, Q], U32, "wt_codes")
         wt_scales = sb_tile([P, Q], U8, "wt_scales")
 
-        nc.vector.quantize_mx(out=wt_codes[:].bitcast(FP8X4), scales=wt_scales[:], in_=wt_bf[:])
+        nc.vector.reciprocal(out=inv[:, 4:6], in_=sums[:, 4:6])
         for t in range(2):
-            scale_x(t, slice(SCALAR_COLS, J), x_places[:, 0, SCALAR_COLS:J, t], inv[:, 4 + t:5 + t])
+            scale_x(t, slice(0, J), x_places[:, 0, :, t], inv[:, 4 + t:5 + t])
+        nc.vector.quantize_mx(out=wt_codes[:].bitcast(FP8X4), scales=wt_scales[:], in_=wt_bf[:])
         nc.vector.reciprocal(out=inv[:, 6:7], in_=sums[:, 6:7])
         weave_x(nc.vector.tensor_copy, 0, slice(0, 1))
         scale_x(2, first, x_bf[0][:, :, 2], inv[:, 6:7])
-        last_inv = sb_tile([P, 2], F32, "last_inv")
-        nc.vector.reciprocal(out=last_inv[:], in_=sums[:, 6:8])
-        scale_x(3, first, x_bf[0][:, :, 3], last_inv[:, 1:2])
-        scale_x(2, rest, x_places[:, 1, rest, 0], last_inv[:, 0:1])
+        scale_x(2, rest, x_places[:, 1, rest, 0], inv[:, 6:7])
+        nc.vector.reciprocal(out=inv[:, 7:8], in_=sums[:, 7:8])
+        scale_x(3, first, x_bf[0][:, :, 3], inv[:, 7:8])
+        scale_x(3, rest, x_places[:, 1, rest, 1], inv[:, 7:8])
 
         x_codes = sb_tile([P, J], U32, "x_codes")
         x_scales = sb_tile([P, J], U8, "x_scales")
@@ -235,7 +250,7 @@ def tile_attend_rollout_pl_kernel(tc, query, keys_words, keys_scales, qpool_word
             nc.vector.quantize_mx(out=x_codes[:, cols].bitcast(FP8X4), scales=x_scales[:, cols],
                                   in_=x_bf[c][:].rearrange("p c t -> p (c t)"))
             y_sb = sb_tile([P, PACK, JC], F32, "y_sb%d" % c)
-            banks = ((3, 4), (7,), (0,), (1,))[c]
+            banks = ((5, 4), (7,), (0,), (1,))[c]
             places = PACK // len(banks)
             for b, index in enumerate(banks):
                 y_ps = bank(index, [P, places, JC], "y_ps%d_%d" % (c, b))
@@ -262,7 +277,6 @@ def tile_attend_rollout_pl_kernel(tc, query, keys_words, keys_scales, qpool_word
                 nc.sync.dma_start(out=y_words[:, done], in_=y_codes[:, done].bitcast(I32))
 
         y_tiles = [product(0)]
-        scale_x(3, rest, x_places[:, 1, rest, 1], last_inv[:, 1:2])
         for c in range(1, CHUNKS):
             weave_x(nc.scalar.copy if c == 2 else nc.vector.tensor_copy, c, slice(0, 2))
         for c in range(1, CHUNKS):

@@ -226,14 +226,19 @@ def tile_attend_rollout_pl_kernel(tc, query, keys_words, keys_scales, qpool_word
         wt_scales = sb_tile([P, Q], U8, "wt_scales")
 
         nc.vector.reciprocal(out=inv[:, 4:6], in_=sums[:, 4:6])
-        for t in range(2):
-            scale_x(t, slice(0, J), x_places[:, 0, :, t], inv[:, 4 + t:5 + t])
+        row_scale = sb_tile([P, 2], F32, "row_scale")
+        nc.vector.tensor_tensor(out=row_scale[:], in0=inv[:, 4:6], in1=sb_cols[:, 0:2], op=ALU.mult)
+        scale_x(0, first, x_bf[0][:, :, 0], inv[:, 4:5])
         nc.vector.quantize_mx(out=wt_codes[:].bitcast(FP8X4), scales=wt_scales[:], in_=wt_bf[:])
+        scale_x(1, first, x_bf[0][:, :, 1], inv[:, 5:6])
         nc.vector.reciprocal(out=inv[:, 6:7], in_=sums[:, 6:7])
-        weave_x(nc.vector.tensor_copy, 0, slice(0, 1))
         scale_x(2, first, x_bf[0][:, :, 2], inv[:, 6:7])
-        scale_x(2, rest, x_places[:, 1, rest, 0], inv[:, 6:7])
+        for t in range(2):
+            for cols in (slice(JC, 2 * JC), slice(2 * JC, J)):
+                nc.scalar.activation(out=x_places[:, 0, cols, t], in_=r_rows[t][:, cols], func=ACT.Copy,
+                                     scale=row_scale[:, t:t + 1])
         nc.vector.reciprocal(out=inv[:, 7:8], in_=sums[:, 7:8])
+        scale_x(2, rest, x_places[:, 1, rest, 0], inv[:, 6:7])
         scale_x(3, first, x_bf[0][:, :, 3], inv[:, 7:8])
         scale_x(3, rest, x_places[:, 1, rest, 1], inv[:, 7:8])
 
@@ -277,9 +282,10 @@ def tile_attend_rollout_pl_kernel(tc, query, keys_words, keys_scales, qpool_word
                 nc.sync.dma_start(out=y_words[:, done], in_=y_codes[:, done].bitcast(I32))
 
         y_tiles = [product(0)]
+        weave_x(nc.vector.tensor_copy, 1, slice(0, 2))
         for c in range(1, CHUNKS):
-            weave_x(nc.scalar.copy if c == 2 else nc.vector.tensor_copy, c, slice(0, 2))
-        for c in range(1, CHUNKS):
+            if c + 1 < CHUNKS:
+                weave_x(nc.vector.tensor_copy, c + 1, slice(0, 2))
             y_tiles.append(product(c))
         round_y(0, y_tiles[0])
         for c in range(CHUNKS - 2):

@@ -218,10 +218,6 @@ def tile_attend_rollout_pl_kernel(tc, query, keys_words, keys_scales, qpool_word
         nc.scalar.copy(out=wt_words[:, :, 64:128, :], in_=wt_ps[:].rearrange("p u (m t) -> p t m u", t=4))
         second_map(2)
         second_map(3)
-        spare_ps = bank(6, [P, J], "spare_ps")
-        for repeat in range(3):
-            nc.tensor.matmul_mx(out=spare_ps[:], lhsT=qw[:, 0:P].bitcast(FP8X4), lhsT_scale=qs[QPOOL_ROW:P, 0:P],
-                                rhs=k2w[:].bitcast(FP8X4), rhs_scale=k2s[KEYS2_ROW:P, :], start=True, stop=True)
         wt_codes = sb_tile([P, Q], U32, "wt_codes")
         wt_scales = sb_tile([P, Q], U8, "wt_scales")
 

@@ -22,10 +22,11 @@ FLOPS = 2 * D * Q * I + 2 * D * I * J + 2 * I * Q * J
 KEYS_ROW, KEYS2_ROW, QPOOL_ROW = 0, 4, 8
 CHUNKS = 4
 JC = J // CHUNKS
+HALF = Q // 2
 
 
 def tile_attend_rollout_pl_kernel(tc, query, keys_words, keys_scales, qpool_words, qpool_scales,
-                                   keys2_words, keys2_scales, sa, sb, offs, offs2, out_0, out_1, out_2):
+                                       keys2_words, keys2_scales, sa, sb, offs, offs2, out_0, out_1, out_2):
     nc = tc.nc
     with ExitStack() as ctx:
         lists = ctx.enter_context(tc.tile_pool(name="lists", bufs=1))
@@ -39,23 +40,26 @@ def tile_attend_rollout_pl_kernel(tc, query, keys_words, keys_scales, qpool_word
         def bank(index, shape, name):
             return psum.tile(shape, F32, name=name, tag="bank%d" % index)
 
-        def zeroed_scale_window(engine, name):
+        def zeroed_scale_window(name):
             window = sb_tile([P, T], U8, name)
-            engine.memset(window[:].bitcast(I32), 0)
+            nc.vector.memset(window[:].bitcast(I32), 0)
             return window
 
         def load_scale_rows(queue, window, scales, row):
             for r in range(4):
                 queue.dma_start(out=window[row + r:P:32, :].bitcast(I32), in_=scales[0, r:16:4, :].bitcast(I32))
 
+        def quantise(codes, scales, values):
+            nc.vector.quantize_mx(out=codes.bitcast(FP8X4), scales=scales, in_=values)
+
         query_bytes = PACK * Q * 4
-        ks_win = zeroed_scale_window(nc.vector, "ks_win")
+        ks_win = zeroed_scale_window("ks_win")
         zeros = placed.tile([P, P], F32, name="zeros", offset=query_bytes - 256, align_bytes=64)
         nc.vector.memset(zeros[:], 0.0)
         vec_rows = sb_tile([P, P], F32, "vec_rows")
         nc.vector.tensor_copy(out=vec_rows[:], in_=zeros[:])
-        qs_win = zeroed_scale_window(nc.vector, "qs_win")
-        k2s_win = zeroed_scale_window(nc.vector, "k2s_win")
+        qs_win = zeroed_scale_window("qs_win")
+        k2s_win = zeroed_scale_window("k2s_win")
         ident = sb_tile([P, P], F32, "ident")
         nc.vector.memset(ident[:], 0.0)
         make_identity(nc, ident[:], nomemset=True)
@@ -68,11 +72,14 @@ def tile_attend_rollout_pl_kernel(tc, query, keys_words, keys_scales, qpool_word
         nc.sync.dma_start(out=kw_win[:].bitcast(I32), in_=keys_words[0].bitcast(I32))
         load_scale_rows(nc.scalar, ks_win, keys_scales, KEYS_ROW)
         q_rows = query.rearrange("(p t) q -> p t q", t=PACK)
-        q_both = placed.tile([P, 2, PACK, Q // 2], F32, name="q_both", offset=0, align_bytes=64)
-        q_raw = [q_both[:, 0], q_both[:, 1]]
-        nc.sync.dma_start(out=q_raw[0], in_=q_rows[:, :, 0:256])
-        nc.sync.dma_start(out=q_raw[1], in_=q_rows[:, :, 256:512])
+        q_both = placed.tile([P, 2, PACK, HALF], F32, name="q_both", offset=0, align_bytes=64)
+        for h in range(2):
+            nc.sync.dma_start(out=q_both[:, h], in_=q_rows[:, :, h * HALF:(h + 1) * HALF])
         load_scale_rows(nc.sync, qs_win, qpool_scales, QPOOL_ROW)
+        nc.sync.dma_start(out=vec_rows[4:8, :].rearrange("t (g r) -> t g r", r=8),
+                          in_=sa.rearrange("o (g t r) -> t g (r o)", t=4, r=8))
+        nc.sync.dma_start(out=vec_rows[0:4, :].rearrange("t (g r) -> t g r", r=8),
+                          in_=sb.rearrange("(g t r) o -> t g (r o)", t=4, r=8))
         qw_win = placed.tile([P, T], I32, name="qw_win", offset=query_bytes, align_bytes=64)
         nc.sync.dma_start(out=qw_win[:], in_=qpool_words[0].rearrange("p n t -> p (n t)").bitcast(I32))
 
@@ -80,19 +87,15 @@ def tile_attend_rollout_pl_kernel(tc, query, keys_words, keys_scales, qpool_word
         nc.vector.tensor_copy(out=kw[:], in_=kw_win[:].indirect(offs_sb[:]))
         ks = sb_tile([P, I], U8, "ks")
         nc.vector.tensor_copy(out=ks[:], in_=ks_win[:].indirect(offs_sb[:]))
-        nc.sync.dma_start(out=vec_rows[4:8, :].rearrange("t (g r) -> t g r", r=8),
-                          in_=sa.rearrange("o (g t r) -> t g (r o)", t=4, r=8))
-        nc.sync.dma_start(out=vec_rows[0:4, :].rearrange("t (g r) -> t g r", r=8),
-                          in_=sb.rearrange("(g t r) o -> t g (r o)", t=4, r=8))
         k2w_win = sb_tile([P, U], I32, "k2w_win", "slot_a")
         nc.sync.dma_start(out=k2w_win[:], in_=keys2_words[0].rearrange("p n t -> p (n t)").bitcast(I32))
         load_scale_rows(nc.sync, k2s_win, keys2_scales, KEYS2_ROW)
 
         vec_ps = bank(6, [P, P], "vec_ps")
         nc.tensor.transpose(vec_ps[:], vec_rows[:], ident[:])
-        sa_cols = sb_tile([P, 4], F32, "sa_cols")
+        sa_cols = sb_tile([P, PACK], F32, "sa_cols")
         nc.scalar.copy(out=sa_cols[:], in_=vec_ps[:, 4:8])
-        sb_cols = sb_tile([P, 4], F32, "sb_cols")
+        sb_cols = sb_tile([P, PACK], F32, "sb_cols")
         nc.scalar.activation(out=sb_cols[:], in_=vec_ps[:, 0:4], func=ACT.Copy, scale=512.0)
         sa_ps = bank(7, [P, 2, P, 2], "sa_ps")
         for t in range(PACK):
@@ -101,53 +104,50 @@ def tile_attend_rollout_pl_kernel(tc, query, keys_words, keys_scales, qpool_word
 
         q_codes = sb_tile([P, Q], U32, "q_codes")
         q_scales = sb_tile([P, Q], U8, "q_scales")
-        neg_max = sb_tile([P, 8], F32, "neg_max")
+        neg_max = sb_tile([P, 4], F32, "neg_max")
         sums = sb_tile([P, 8], F32, "sums")
         inv = sb_tile([P, 8], F32, "inv")
-        p_tiles = []
 
         def quantise_query(h):
-            q_bf = sb_tile([P, Q // 2, PACK], BF16, "q_bf%d" % h)
-            nc.scalar.copy(out=q_bf[:].rearrange("p (c i) t -> p c t i", i=4),
-                           in_=q_raw[h].rearrange("p t (c i) -> p c t i", i=4))
-            cols = slice(h * 256, (h + 1) * 256)
-            nc.vector.quantize_mx(out=q_codes[:, cols].bitcast(FP8X4), scales=q_scales[:, cols],
-                                  in_=q_bf[:].rearrange("p c t -> p (c t)"))
+            q_bf = sb_tile([P, HALF * PACK], BF16, "q_bf%d" % h)
+            nc.scalar.copy(out=q_bf[:].rearrange("p (u m e t) -> p m t u e", u=2, e=2, t=PACK),
+                           in_=q_both[:, h].rearrange("p t (m u e) -> p m t u e", u=2, e=2))
+            cols = slice(h * HALF, (h + 1) * HALF)
+            quantise(q_codes[:, cols], q_scales[:, cols], q_bf[:])
 
-        def first_map(n):
+        def first_map(u, h):
+            n = 2 * u + h
             a_ps = bank(n, [P, I], "a_ps%d" % n)
-            cols = slice(n * P, (n + 1) * P)
+            cols = slice((2 * h + u) * P, (2 * h + u + 1) * P)
             nc.tensor.matmul_mx(out=a_ps[:], lhsT=q_codes[:, cols].bitcast(FP8X4), lhsT_scale=q_scales[:, cols],
                                 rhs=kw[:].bitcast(FP4X4), rhs_scale=ks[:], start=True, stop=True)
             nc.vector.tensor_reduce(out=neg_max[:, n:n + 1], in_=a_ps[:], axis=AX.X, op=ALU.max, negate=True)
             p_n = sb_tile([P, I], F32, "p%d" % n)
-            if n < 2:
+            if u == 0:
                 dealt = p_n[:].rearrange("p (t g r) -> p g t r", t=PACK, r=8)
                 scores = a_ps[:].rearrange("p (g t r) -> p g t r", t=PACK, r=8)
             else:
-                dealt = p_n[:].rearrange("p (u g r e) -> p g u r e", u=2, r=8, e=2)
-                scores = a_ps[:].rearrange("p (g u e r) -> p g u r e", u=2, r=8, e=2)
-            nc.scalar.activation(out=dealt, in_=scores, func=ACT.Exp, bias=neg_max[:, n:n + 1], accum_out=sums[:, n:n + 1])
-            p_tiles.append(p_n)
+                dealt = p_n[:].rearrange("p (v g r e) -> p g v r e", v=2, r=8, e=2)
+                scores = a_ps[:].rearrange("p (g v e r) -> p g v r e", v=2, r=8, e=2)
+            nc.scalar.activation(out=dealt, in_=scores, func=ACT.Exp, bias=neg_max[:, n:n + 1],
+                                 accum_out=sums[:, n:n + 1])
+            return p_n
 
         quantise_query(0)
-        qs_list = sb_tile([P, I], U8, "qs_list")
-        nc.vector.tensor_copy(out=qs_list[:], in_=qs_win[:].indirect(offs_sb[:]))
-        quantise_query(1)
-        first_map(0)
-        first_map(1)
         qs = sb_tile([P, I], U8, "qs")
-        nc.vector.tensor_copy(out=qs[:].bitcast(I32).rearrange("p (t g w) -> p g t w", t=4, w=2),
-                              in_=qs_list[:].bitcast(I32).rearrange("p (g t w) -> p g t w", t=4, w=2))
-        first_map(2)
+        nc.vector.tensor_copy(out=qs[:].rearrange("p (t g r) -> p g t r", t=4, r=8),
+                              in_=qs_win[:].indirect(offs_sb[:]))
+        quantise_query(1)
+        p_tiles = [first_map(0, 0), first_map(0, 1)]
+        p_tiles.append(first_map(1, 0))
         minus_one = sb_tile([P, 2], F32, "minus_one")
         nc.vector.memset(minus_one[:], -1.0)
         early_inv = sb_tile([P, 2], F32, "early_inv")
         nc.gpsimd.tensor_tensor(out=early_inv[:], in0=sums[:, 0:2], in1=minus_one[:], op=ALU.pow)
-        first_map(3)
-        shares = [sb_tile([P, I], F32, "share%d" % n) for n in range(2)]
-        for n in range(2):
-            nc.scalar.activation(out=shares[n][:], in_=p_tiles[n][:], func=ACT.Copy, scale=early_inv[:, n:n + 1])
+        p_tiles.append(first_map(1, 1))
+        shares = [sb_tile([P, I], F32, "share%d" % h) for h in range(2)]
+        for h in range(2):
+            nc.scalar.activation(out=shares[h][:], in_=p_tiles[h][:], func=ACT.Copy, scale=early_inv[:, h:h + 1])
         qw = sb_tile([P, I], U32, "qw")
         nc.vector.tensor_copy(out=qw[:].rearrange("p (t g r) -> p g t r", t=4, r=8),
                               in_=qw_win[:].bitcast(U32).indirect(offs_sb[:]))
@@ -157,30 +157,35 @@ def tile_attend_rollout_pl_kernel(tc, query, keys_words, keys_scales, qpool_word
         k2s = sb_tile([P, J], U8, "k2s")
         nc.vector.tensor_copy(out=k2s[:], in_=k2s_win[:].indirect(offs2_sb[:]))
 
-        wt_bf = sb_tile([P, Q * PACK], BF16, "wt_bf")
-        wt_words = wt_bf[:].bitcast(F32).rearrange("p (t m u) -> p t m u", t=4, u=2)
+        wt_bf = [sb_tile([P, HALF * PACK], BF16, "wt_bf%d" % u) for u in range(2)]
+        wt_words = [wt_bf[u][:].bitcast(F32).rearrange("p (e m v) -> p e m v", e=2, v=2) for u in range(2)]
+        wt_codes = [sb_tile([P, HALF], U32, "wt_codes%d" % u, ("p3", None)[u]) for u in range(2)]
+        wt_scales = [sb_tile([P, HALF], U8, "wt_scales%d" % u) for u in range(2)]
 
-        def weights_on_scalar():
-            turned = [bank(u, [P, 2, 256], "turned%d" % u) for u in range(2)]
-            for n in range(2):
-                for t in range(PACK):
-                    nc.tensor.transpose(turned[t // 2][:, t % 2, n * P:(n + 1) * P], shares[n][:, t * P:(t + 1) * P],
-                                        ident[:])
-            pairs = sb_tile([P, 2 * 256 * 2], BF16, "w_pairs")
-            places = pairs[:].rearrange("p (u k m e) -> p u e k m", u=2, k=PACK, e=2)
+        def first_pair_on_scalar():
+            turned = [bank(v, [P, 2, HALF], "turned%d" % v) for v in range(2)]
+            for v in range(2):
+                for h in range(2):
+                    for t in (2 * v, 2 * v + 1):
+                        nc.tensor.transpose(turned[v][:, t % 2, h * P:(h + 1) * P],
+                                            shares[h][:, t * P:(t + 1) * P], ident[:])
+            pairs = sb_tile([P, 2 * HALF * 2], BF16, "w_pairs")
+            places = pairs[:].rearrange("p (v e m z) -> p v z e m", v=2, e=2, z=2)
             for t in range(PACK):
                 nc.scalar.activation(out=places[:, t // 2, t % 2], func=ACT.Copy, scale=sa_cols[:, t:t + 1],
-                                     in_=turned[t // 2][:, t % 2, :].rearrange("p (m k) -> p k m", k=PACK))
-            nc.scalar.copy(out=wt_words[:, :, 0:64, :],
-                           in_=pairs[:].bitcast(F32).rearrange("p (u k m) -> p k m u", u=2, k=PACK))
+                                     in_=turned[t // 2][:, t % 2, :].rearrange("p (m e) -> p e m", e=2))
+            nc.scalar.copy(out=wt_words[0], in_=pairs[:].bitcast(F32).rearrange("p (v e m) -> p e m v", v=2, e=2))
 
-        def weigh(n, tag):
-            w_n = sb_tile([P, I], BF16, "w%d" % n, tag)
-            nc.vector.scalar_tensor_tensor(out=w_n[:], in0=p_tiles[n][:], scalar=inv[:, n:n + 1], in1=sa_all,
+        def weigh(h, tag):
+            w_h = sb_tile([P, I], BF16, "w%d" % h, tag)
+            nc.vector.scalar_tensor_tensor(out=w_h[:], in0=p_tiles[2 + h][:], scalar=inv[:, 2 + h:3 + h], in1=sa_all,
                                            op0=ALU.mult, op1=ALU.mult)
-            words = w_n[:].bitcast(F32)
-            for u in range(2):
-                nc.tensor.transpose(wt_ps[:, u, (n - 2) * P:(n - 1) * P], words[:, u * P:(u + 1) * P], ident[:])
+            return w_h
+
+        def turn(h, w_h):
+            words = w_h[:].bitcast(F32)
+            for v in range(2):
+                nc.tensor.transpose(wt_ps[:, v, h * P:(h + 1) * P], words[:, v * P:(v + 1) * P], ident[:])
 
         r_rows = []
 
@@ -189,54 +194,52 @@ def tile_attend_rollout_pl_kernel(tc, query, keys_words, keys_scales, qpool_word
             cols = slice(t * P, (t + 1) * P)
             nc.tensor.matmul_mx(out=b_ps[:], lhsT=qw[:, cols].bitcast(FP8X4), lhsT_scale=qs[QPOOL_ROW:P, cols],
                                 rhs=k2w[:].bitcast(FP8X4), rhs_scale=k2s[KEYS2_ROW:P, :], start=True, stop=True)
-            nc.vector.tensor_reduce(out=neg_max[:, 4 + t:5 + t], in_=b_ps[:], axis=AX.X, op=ALU.max, negate=True)
-            r_rows.append(sb_tile([P, J], F32, "r%d" % t, "w3" if t == 2 else None))
+            row_max = sb_tile([P, 1], F32, "row_max%d" % t)
+            nc.vector.tensor_reduce(out=row_max[:], in_=b_ps[:], axis=AX.X, op=ALU.max, negate=True)
+            r_rows.append(sb_tile([P, J], F32, "r%d" % t))
             nc.scalar.activation(out=r_rows[t][:], in_=b_ps[:], func=ACT.Exp,
-                                 bias=neg_max[:, 4 + t:5 + t], accum_out=sums[:, 4 + t:5 + t])
+                                 bias=row_max[:], accum_out=sums[:, 4 + t:5 + t])
 
         x_pairs = sb_tile([P, 2 * J * 2], BF16, "x_pairs")
-        x_places = x_pairs[:].rearrange("p (u j e) -> p u j e", u=2, e=2)
-        x_both = x_pairs[:].bitcast(F32).rearrange("p (u j) -> p u j", u=2)
+        x_places = x_pairs[:].rearrange("p (v j z) -> p v j z", v=2, z=2)
+        x_both = x_pairs[:].bitcast(F32).rearrange("p (v j) -> p v j", v=2)
         x_bf = [sb_tile([P, JC, PACK], BF16, "x_bf%d" % c) for c in range(CHUNKS)]
 
-        def scale_x(t, cols, out, inv_t):
-            nc.vector.tensor_scalar(out=out, in0=r_rows[t][:, cols], scalar1=inv_t,
+        def scale_x(t, cols, out):
+            nc.vector.tensor_scalar(out=out, in0=r_rows[t][:, cols], scalar1=inv[:, 4 + t:5 + t],
                                     scalar2=sb_cols[:, t:t + 1], op0=ALU.mult, op1=ALU.mult)
 
-        def weave_x(copy, c, halves):
-            words = x_bf[c][:].rearrange("p c t -> p (c t)").bitcast(F32).rearrange("p (c u) -> p c u", u=2)
-            copy(out=words[:, :, halves], in_=x_both[:, halves, c * JC:(c + 1) * JC].rearrange("p u c -> p c u"))
+        def weave_x(copy, c):
+            words = x_bf[c][:].rearrange("p c t -> p (c t)").bitcast(F32).rearrange("p (c v) -> p c v", v=2)
+            copy(out=words, in_=x_both[:, :, c * JC:(c + 1) * JC].rearrange("p v c -> p c v"))
 
         first, rest = slice(0, JC), slice(JC, J)
 
-        weights_on_scalar()
-        wt_ps = bank(3, [P, 2, 256], "wt_ps")
-        weigh(2, "k2s_win")
-        second_map(0)
-        second_map(1)
-        weigh(3, None)
-        nc.scalar.copy(out=wt_words[:, :, 64:128, :], in_=wt_ps[:].rearrange("p u (m t) -> p t m u", t=4))
-        second_map(2)
-        second_map(3)
-        wt_codes = sb_tile([P, Q], U32, "wt_codes")
-        wt_scales = sb_tile([P, Q], U8, "wt_scales")
+        first_pair_on_scalar()
+        wt_ps = bank(3, [P, 2, HALF], "wt_ps")
+        w_first = weigh(0, "k2s_win")
+        for t in range(PACK):
+            second_map(t)
+        turn(0, w_first)
+        turn(1, weigh(1, "row_max1"))
+        nc.scalar.copy(out=wt_words[1], in_=wt_ps[:].rearrange("p v (m e) -> p e m v", e=2))
 
         nc.vector.reciprocal(out=inv[:, 4:6], in_=sums[:, 4:6])
         row_scale = sb_tile([P, 2], F32, "row_scale")
         nc.vector.tensor_tensor(out=row_scale[:], in0=inv[:, 4:6], in1=sb_cols[:, 0:2], op=ALU.mult)
-        scale_x(0, first, x_bf[0][:, :, 0], inv[:, 4:5])
-        nc.vector.quantize_mx(out=wt_codes[:].bitcast(FP8X4), scales=wt_scales[:], in_=wt_bf[:])
-        scale_x(1, first, x_bf[0][:, :, 1], inv[:, 5:6])
+        scale_x(0, first, x_bf[0][:, :, 0])
+        quantise(wt_codes[0][:], wt_scales[0][:], wt_bf[0][:])
+        scale_x(1, first, x_bf[0][:, :, 1])
         nc.vector.reciprocal(out=inv[:, 6:7], in_=sums[:, 6:7])
-        scale_x(2, first, x_bf[0][:, :, 2], inv[:, 6:7])
+        scale_x(2, first, x_bf[0][:, :, 2])
         for t in range(2):
             for cols in (slice(JC, 2 * JC), slice(2 * JC, J)):
                 nc.scalar.activation(out=x_places[:, 0, cols, t], in_=r_rows[t][:, cols], func=ACT.Copy,
                                      scale=row_scale[:, t:t + 1])
         nc.vector.reciprocal(out=inv[:, 7:8], in_=sums[:, 7:8])
-        scale_x(2, rest, x_places[:, 1, rest, 0], inv[:, 6:7])
-        scale_x(3, first, x_bf[0][:, :, 3], inv[:, 7:8])
-        scale_x(3, rest, x_places[:, 1, rest, 1], inv[:, 7:8])
+        scale_x(2, rest, x_places[:, 1, rest, 0])
+        scale_x(3, first, x_bf[0][:, :, 3])
+        scale_x(3, rest, x_places[:, 1, rest, 1])
 
         x_codes = sb_tile([P, J], U32, "x_codes")
         x_scales = sb_tile([P, J], U8, "x_scales")
@@ -244,51 +247,55 @@ def tile_attend_rollout_pl_kernel(tc, query, keys_words, keys_scales, qpool_word
         y_scales = sb_tile([P, J], U8, "y_scales")
         y_rows = out_0.rearrange("(p t) j -> p t j", t=PACK)
         y_words = out_1[0].rearrange("p c r -> p (c r)").bitcast(I32)
+        y_sb = [sb_tile([P, PACK, JC], F32, "y_sb%d" % c) for c in range(CHUNKS)]
         y_bf = [sb_tile([P, JC, PACK], BF16, "y_bf%d" % c) for c in range(CHUNKS)]
 
-        def product(c):
+        def quantise_x(c):
             cols = slice(c * JC, (c + 1) * JC)
-            nc.vector.quantize_mx(out=x_codes[:, cols].bitcast(FP8X4), scales=x_scales[:, cols],
-                                  in_=x_bf[c][:].rearrange("p c t -> p (c t)"))
-            y_sb = sb_tile([P, PACK, JC], F32, "y_sb%d" % c)
-            banks = ((5, 4), (7,), (0,), (1,))[c]
-            places = PACK // len(banks)
-            for b, index in enumerate(banks):
-                y_ps = bank(index, [P, places, JC], "y_ps%d_%d" % (c, b))
-                for k in range(places):
-                    q_cols = slice((b * places + k) * P, (b * places + k + 1) * P)
-                    nc.tensor.matmul_mx(out=y_ps[:, k, :], lhsT=wt_codes[:, q_cols].bitcast(FP8X4),
-                                        lhsT_scale=wt_scales[:, q_cols], rhs=x_codes[:, cols].bitcast(FP8X4),
-                                        rhs_scale=x_scales[:, cols], start=True, stop=True)
-                part = slice(b * places, (b + 1) * places)
-                nc.scalar.copy(out=y_sb[:, part, :], in_=y_ps[:])
-                nc.sync.dma_start(out=y_rows[:, part, cols], in_=y_sb[:, part, :])
-            return y_sb
+            quantise(x_codes[:, cols], x_scales[:, cols], x_bf[c][:].rearrange("p c t -> p (c t)"))
 
-        def round_y(c, y_sb):
+        def product(c, pairs, index):
+            cols = slice(c * JC, (c + 1) * JC)
+            y_ps = bank(index, [P, 2 * len(pairs), JC], "y_ps%d_%d" % (c, pairs[0]))
+            for k, u in enumerate(pairs):
+                for e in range(2):
+                    q_cols = slice(e * P, (e + 1) * P)
+                    nc.tensor.matmul_mx(out=y_ps[:, 2 * k + e, :], lhsT=wt_codes[u][:, q_cols].bitcast(FP8X4),
+                                        lhsT_scale=wt_scales[u][:, q_cols], rhs=x_codes[:, cols].bitcast(FP8X4),
+                                        rhs_scale=x_scales[:, cols], start=True, stop=True)
+            part = slice(2 * pairs[0], 2 * pairs[-1] + 2)
+            nc.scalar.copy(out=y_sb[c][:, part, :], in_=y_ps[:])
+            nc.sync.dma_start(out=y_rows[:, part, cols], in_=y_sb[c][:, part, :])
+
+        def round_y(c):
             nc.vector.tensor_copy(out=y_bf[c][:].rearrange("p (c i) t -> p c t i", i=4),
-                                  in_=y_sb[:].rearrange("p t (c i) -> p c t i", i=4))
+                                  in_=y_sb[c][:].rearrange("p t (c i) -> p c t i", i=4))
 
         def planes(c):
             cols = slice(c * JC, (c + 1) * JC)
-            nc.vector.quantize_mx(out=y_codes[:, cols].bitcast(FP8X4), scales=y_scales[:, cols],
-                                  in_=y_bf[c][:].rearrange("p c t -> p (c t)"))
+            quantise(y_codes[:, cols], y_scales[:, cols], y_bf[c][:].rearrange("p c t -> p (c t)"))
             if c >= CHUNKS - 2:
                 done = slice(0, (c + 1) * JC) if c == CHUNKS - 2 else cols
                 nc.sync.dma_start(out=y_words[:, done], in_=y_codes[:, done].bitcast(I32))
 
-        y_tiles = [product(0)]
-        weave_x(nc.vector.tensor_copy, 1, slice(0, 2))
-        for c in range(1, CHUNKS):
-            if c + 1 < CHUNKS:
-                weave_x(nc.vector.tensor_copy, c + 1, slice(0, 2))
-            y_tiles.append(product(c))
-        round_y(0, y_tiles[0])
+        weave_x(nc.scalar.copy, 1)
+        quantise_x(0)
+        product(0, (0,), 5)
+        quantise(wt_codes[1][:], wt_scales[1][:], wt_bf[1][:])
+        product(0, (1,), 4)
+        quantise_x(1)
+        product(1, (0, 1), 7)
+        for c in range(2, CHUNKS):
+            weave_x(nc.vector.tensor_copy, c)
+        for c in range(2, CHUNKS):
+            quantise_x(c)
+            product(c, (0, 1), c - 2)
+        round_y(0)
         for c in range(CHUNKS - 2):
-            round_y(c + 1, y_tiles[c + 1])
+            round_y(c + 1)
             planes(c)
         planes(CHUNKS - 2)
-        round_y(CHUNKS - 1, y_tiles[CHUNKS - 1])
+        round_y(CHUNKS - 1)
         planes(CHUNKS - 1)
         for quad in range(4):
             queue = nc.scalar if quad % 2 else nc.sync

@@ -32,6 +32,7 @@ def tile_attend_rollout_pl_kernel(tc, query, keys_words, keys_scales, qpool_word
         lists = ctx.enter_context(tc.tile_pool(name="lists", bufs=1))
         keep = ctx.enter_context(tc.tile_pool(name="keep", bufs=1))
         placed = ctx.enter_context(tc.tile_pool(name="placed", bufs=1))
+        ring = ctx.enter_context(tc.tile_pool(name="ring", bufs=1))
         psum = ctx.enter_context(tc.psum_pool(name="psum", bufs=1))
 
         def sb_tile(shape, dtype, name, tag=None):
@@ -66,10 +67,10 @@ def tile_attend_rollout_pl_kernel(tc, query, keys_words, keys_scales, qpool_word
 
         offs_sb = lists.tile([P, I // 16], U16, name="offs_sb")
         offs2_sb = lists.tile([P, J // 16], U16, name="offs2_sb")
-        nc.sync.dma_start(offs_sb[:], offs)
-        nc.sync.dma_start(offs2_sb[:], offs2)
         kw_win = sb_tile([P, T], U16, "kw_win", "slot_a")
         nc.sync.dma_start(out=kw_win[:].bitcast(I32), in_=keys_words[0].bitcast(I32))
+        nc.sync.dma_start(offs_sb[:], offs)
+        nc.sync.dma_start(offs2_sb[:], offs2)
         load_scale_rows(nc.scalar, ks_win, keys_scales, KEYS_ROW)
         q_rows = query.rearrange("(p t) q -> p t q", t=PACK)
         q_both = placed.tile([P, 2, PACK, HALF], F32, name="q_both", offset=0, align_bytes=64)
@@ -157,10 +158,13 @@ def tile_attend_rollout_pl_kernel(tc, query, keys_words, keys_scales, qpool_word
         k2s = sb_tile([P, J], U8, "k2s")
         nc.vector.tensor_copy(out=k2s[:], in_=k2s_win[:].indirect(offs2_sb[:]))
 
-        wt_bf = [sb_tile([P, HALF * PACK], BF16, "wt_bf%d" % u) for u in range(2)]
-        wt_words = [wt_bf[u][:].bitcast(F32).rearrange("p (e m v) -> p e m v", e=2, v=2) for u in range(2)]
+        wt_bf = [sb_tile([P, HALF * PACK], BF16, "wt_bf0")]
+
+        def wt_words(u):
+            return wt_bf[u][:].bitcast(F32).rearrange("p (e m v) -> p e m v", e=2, v=2)
+
         wt_codes = [sb_tile([P, HALF], U32, "wt_codes%d" % u, ("p3", None)[u]) for u in range(2)]
-        wt_scales = [sb_tile([P, HALF], U8, "wt_scales%d" % u) for u in range(2)]
+        wt_scales = [sb_tile([P, HALF], U8, "wt_scales0")]
 
         def first_pair_on_scalar():
             turned = [bank(v, [P, 2, HALF], "turned%d" % v) for v in range(2)]
@@ -174,7 +178,7 @@ def tile_attend_rollout_pl_kernel(tc, query, keys_words, keys_scales, qpool_word
             for t in range(PACK):
                 nc.scalar.activation(out=places[:, t // 2, t % 2], func=ACT.Copy, scale=sa_cols[:, t:t + 1],
                                      in_=turned[t // 2][:, t % 2, :].rearrange("p (m e) -> p e m", e=2))
-            nc.scalar.copy(out=wt_words[0], in_=pairs[:].bitcast(F32).rearrange("p (v e m) -> p e m v", v=2, e=2))
+            nc.scalar.copy(out=wt_words(0), in_=pairs[:].bitcast(F32).rearrange("p (v e m) -> p e m v", v=2, e=2))
 
         def weigh(h, tag):
             w_h = sb_tile([P, I], BF16, "w%d" % h, tag)
@@ -200,46 +204,53 @@ def tile_attend_rollout_pl_kernel(tc, query, keys_words, keys_scales, qpool_word
             nc.scalar.activation(out=r_rows[t][:], in_=b_ps[:], func=ACT.Exp,
                                  bias=row_max[:], accum_out=sums[:, 4 + t:5 + t])
 
-        x_pairs = sb_tile([P, 2 * J * 2], BF16, "x_pairs")
-        x_places = x_pairs[:].rearrange("p (v j z) -> p v j z", v=2, z=2)
-        x_both = x_pairs[:].bitcast(F32).rearrange("p (v j) -> p v j", v=2)
-        x_bf = [sb_tile([P, JC, PACK], BF16, "x_bf%d" % c) for c in range(CHUNKS)]
+        x_pairs = [sb_tile([P, 2 * HALF * 2], BF16, "x_pairs%d" % a) for a in range(2)]
+        x_bf = {}
 
-        def scale_x(t, cols, out):
-            nc.vector.tensor_scalar(out=out, in0=r_rows[t][:, cols], scalar1=inv[:, 4 + t:5 + t],
-                                    scalar2=sb_cols[:, t:t + 1], op0=ALU.mult, op1=ALU.mult)
+        def x_place(t, a):
+            return x_pairs[a][:].rearrange("p (v j z) -> p v j z", v=2, z=2)[:, t // 2, :, t % 2]
 
-        def weave_x(copy, c):
+        def scale_x_on_vector(t, a):
+            nc.vector.tensor_scalar(out=x_place(t, a), in0=r_rows[t][:, a * HALF:(a + 1) * HALF],
+                                    scalar1=inv[:, 4 + t:5 + t], scalar2=sb_cols[:, t:t + 1],
+                                    op0=ALU.mult, op1=ALU.mult)
+
+        def scale_x_on_scalar(t, a):
+            nc.scalar.activation(out=x_place(t, a), in_=r_rows[t][:, a * HALF:(a + 1) * HALF], func=ACT.Copy,
+                                 scale=row_scale[:, t:t + 1])
+
+        def weave_x(c):
+            x_bf[c] = ring.tile([P, JC, PACK], BF16, name="x_bf%d" % c, offset=(0, 2048, 256, 2048)[c],
+                                align_bytes=64)
             words = x_bf[c][:].rearrange("p c t -> p (c t)").bitcast(F32).rearrange("p (c v) -> p c v", v=2)
-            copy(out=words, in_=x_both[:, :, c * JC:(c + 1) * JC].rearrange("p v c -> p c v"))
-
-        first, rest = slice(0, JC), slice(JC, J)
+            both = x_pairs[c // 2][:].bitcast(F32).rearrange("p (v j) -> p j v", v=2)
+            nc.vector.tensor_copy(out=words, in_=both[:, (c % 2) * JC:(c % 2 + 1) * JC, :])
 
         first_pair_on_scalar()
         wt_ps = bank(3, [P, 2, HALF], "wt_ps")
         w_first = weigh(0, "k2s_win")
-        for t in range(PACK):
+        for t in range(PACK - 1):
             second_map(t)
-        turn(0, w_first)
-        turn(1, weigh(1, "row_max1"))
-        nc.scalar.copy(out=wt_words[1], in_=wt_ps[:].rearrange("p v (m e) -> p e m v", e=2))
-
         nc.vector.reciprocal(out=inv[:, 4:6], in_=sums[:, 4:6])
+        second_map(PACK - 1)
+        nc.vector.reciprocal(out=inv[:, 6:7], in_=sums[:, 6:7])
         row_scale = sb_tile([P, 2], F32, "row_scale")
         nc.vector.tensor_tensor(out=row_scale[:], in0=inv[:, 4:6], in1=sb_cols[:, 0:2], op=ALU.mult)
-        scale_x(0, first, x_bf[0][:, :, 0])
-        quantise(wt_codes[0][:], wt_scales[0][:], wt_bf[0][:])
-        scale_x(1, first, x_bf[0][:, :, 1])
-        nc.vector.reciprocal(out=inv[:, 6:7], in_=sums[:, 6:7])
-        scale_x(2, first, x_bf[0][:, :, 2])
-        for t in range(2):
-            for cols in (slice(JC, 2 * JC), slice(2 * JC, J)):
-                nc.scalar.activation(out=x_places[:, 0, cols, t], in_=r_rows[t][:, cols], func=ACT.Copy,
-                                     scale=row_scale[:, t:t + 1])
+        turn(0, w_first)
+        turn(1, weigh(1, "row_max1"))
+
+        scale_x_on_scalar(0, 0)
+        scale_x_on_scalar(0, 1)
+        scale_x_on_scalar(1, 0)
+        wt_bf.append(sb_tile([P, HALF * PACK], BF16, "wt_bf1", "r0"))
+        nc.scalar.copy(out=wt_words(1), in_=wt_ps[:].rearrange("p v (m e) -> p e m v", e=2))
+        scale_x_on_scalar(1, 1)
+        for a in range(2):
+            scale_x_on_vector(2, a)
         nc.vector.reciprocal(out=inv[:, 7:8], in_=sums[:, 7:8])
-        scale_x(2, rest, x_places[:, 1, rest, 0])
-        scale_x(3, first, x_bf[0][:, :, 3])
-        scale_x(3, rest, x_places[:, 1, rest, 1])
+        quantise(wt_codes[0][:], wt_scales[0][:], wt_bf[0][:])
+        for a in range(2):
+            scale_x_on_vector(3, a)
 
         x_codes = sb_tile([P, J], U32, "x_codes")
         x_scales = sb_tile([P, J], U8, "x_scales")
@@ -254,7 +265,7 @@ def tile_attend_rollout_pl_kernel(tc, query, keys_words, keys_scales, qpool_word
             cols = slice(c * JC, (c + 1) * JC)
             quantise(x_codes[:, cols], x_scales[:, cols], x_bf[c][:].rearrange("p c t -> p (c t)"))
 
-        def product(c, pairs, index):
+        def product(c, pairs, index, stored):
             cols = slice(c * JC, (c + 1) * JC)
             y_ps = bank(index, [P, 2 * len(pairs), JC], "y_ps%d_%d" % (c, pairs[0]))
             for k, u in enumerate(pairs):
@@ -265,7 +276,8 @@ def tile_attend_rollout_pl_kernel(tc, query, keys_words, keys_scales, qpool_word
                                         rhs_scale=x_scales[:, cols], start=True, stop=True)
             part = slice(2 * pairs[0], 2 * pairs[-1] + 2)
             nc.scalar.copy(out=y_sb[c][:, part, :], in_=y_ps[:])
-            nc.sync.dma_start(out=y_rows[:, part, cols], in_=y_sb[c][:, part, :])
+            if stored is not None:
+                nc.sync.dma_start(out=y_rows[:, stored, cols], in_=y_sb[c][:, stored, :])
 
         def round_y(c):
             nc.vector.tensor_copy(out=y_bf[c][:].rearrange("p (c i) t -> p c t i", i=4),
@@ -278,18 +290,21 @@ def tile_attend_rollout_pl_kernel(tc, query, keys_words, keys_scales, qpool_word
                 done = slice(0, (c + 1) * JC) if c == CHUNKS - 2 else cols
                 nc.sync.dma_start(out=y_words[:, done], in_=y_codes[:, done].bitcast(I32))
 
-        weave_x(nc.scalar.copy, 1)
+        weave_x(0)
+        weave_x(1)
         quantise_x(0)
-        product(0, (0,), 5)
-        quantise(wt_codes[1][:], wt_scales[1][:], wt_bf[1][:])
-        product(0, (1,), 4)
+        product(0, (0,), 5, slice(0, 2))
         quantise_x(1)
-        product(1, (0, 1), 7)
+        product(1, (0,), 4, None)
+        wt_scales.append(ring.tile([P, HALF], U8, name="wt_scales1", offset=0, align_bytes=64))
+        quantise(wt_codes[1][:], wt_scales[1][:], wt_bf[1][:])
+        product(0, (1,), 7, slice(2, 4))
+        product(1, (1,), 6, slice(0, 4))
         for c in range(2, CHUNKS):
-            weave_x(nc.vector.tensor_copy, c)
+            weave_x(c)
         for c in range(2, CHUNKS):
             quantise_x(c)
-            product(c, (0, 1), c - 2)
+            product(c, (0, 1), c - 2, slice(0, 4))
         round_y(0)
         for c in range(CHUNKS - 2):
             round_y(c + 1)

@@ -258,60 +258,67 @@ def tile_attend_rollout_pl_kernel(tc, query, keys_words, keys_scales, qpool_word
         y_scales = sb_tile([P, J], U8, "y_scales")
         y_rows = out_0.rearrange("(p t) j -> p t j", t=PACK)
         y_words = out_1[0].rearrange("p c r -> p (c r)").bitcast(I32)
-        y_sb = [sb_tile([P, PACK, JC], F32, "y_sb%d" % c) for c in range(CHUNKS)]
-        y_bf = [sb_tile([P, JC, PACK], BF16, "y_bf%d" % c) for c in range(CHUNKS)]
+        y_sb = [sb_tile([P, PACK, HALF], F32, "y_sb%d" % a) for a in range(2)]
+        y_bf = [sb_tile([P, 2 * JC * PACK], BF16, "y_bf%d" % a) for a in range(2)]
 
         def quantise_x(c):
             cols = slice(c * JC, (c + 1) * JC)
             quantise(x_codes[:, cols], x_scales[:, cols], x_bf[c][:].rearrange("p c t -> p (c t)"))
 
-        def product(c, pairs, index, stored):
+        def product(c, u, index):
             cols = slice(c * JC, (c + 1) * JC)
-            y_ps = bank(index, [P, 2 * len(pairs), JC], "y_ps%d_%d" % (c, pairs[0]))
-            for k, u in enumerate(pairs):
-                for e in range(2):
-                    q_cols = slice(e * P, (e + 1) * P)
-                    nc.tensor.matmul_mx(out=y_ps[:, 2 * k + e, :], lhsT=wt_codes[u][:, q_cols].bitcast(FP8X4),
-                                        lhsT_scale=wt_scales[u][:, q_cols], rhs=x_codes[:, cols].bitcast(FP8X4),
-                                        rhs_scale=x_scales[:, cols], start=True, stop=True)
-            part = slice(2 * pairs[0], 2 * pairs[-1] + 2)
-            nc.scalar.copy(out=y_sb[c][:, part, :], in_=y_ps[:])
-            if stored is not None:
-                nc.sync.dma_start(out=y_rows[:, stored, cols], in_=y_sb[c][:, stored, :])
+            y_ps = bank(index, [P, 2, JC], "y_ps%d_%d" % (c, u))
+            for e in range(2):
+                q_cols = slice(e * P, (e + 1) * P)
+                nc.tensor.matmul_mx(out=y_ps[:, e, :], lhsT=wt_codes[u][:, q_cols].bitcast(FP8X4),
+                                    lhsT_scale=wt_scales[u][:, q_cols], rhs=x_codes[:, cols].bitcast(FP8X4),
+                                    rhs_scale=x_scales[:, cols], start=True, stop=True)
+            part = slice(2 * u, 2 * u + 2)
+            nc.scalar.copy(out=y_sb[c // 2][:, part, (c % 2) * JC:(c % 2 + 1) * JC], in_=y_ps[:])
+            if c % 2:
+                nc.sync.dma_start(out=y_rows[:, part, (c - 1) * JC:(c + 1) * JC], in_=y_sb[c // 2][:, part, :])
 
         def round_y(c):
-            nc.vector.tensor_copy(out=y_bf[c][:].rearrange("p (c i) t -> p c t i", i=4),
-                                  in_=y_sb[c][:].rearrange("p t (c i) -> p c t i", i=4))
+            rounded = y_bf[c // 2][:, (c % 2) * JC * PACK:(c % 2 + 1) * JC * PACK]
+            nc.vector.tensor_copy(out=rounded.rearrange("p (c i t) -> p c t i", i=4, t=PACK),
+                                  in_=y_sb[c // 2][:, :, (c % 2) * JC:(c % 2 + 1) * JC].rearrange(
+                                      "p t (c i) -> p c t i", i=4))
 
-        def planes(c):
-            cols = slice(c * JC, (c + 1) * JC)
-            quantise(y_codes[:, cols], y_scales[:, cols], y_bf[c][:].rearrange("p c t -> p (c t)"))
-            if c >= CHUNKS - 2:
-                done = slice(0, (c + 1) * JC) if c == CHUNKS - 2 else cols
-                nc.sync.dma_start(out=y_words[:, done], in_=y_codes[:, done].bitcast(I32))
+        def planes(first, count):
+            cols = slice(first * JC, (first + count) * JC)
+            start = (first % 2) * JC * PACK
+            quantise(y_codes[:, cols], y_scales[:, cols], y_bf[first // 2][:, start:start + count * JC * PACK])
+
+        def store_codes(a):
+            cols = slice(a * HALF, (a + 1) * HALF)
+            nc.sync.dma_start(out=y_words[:, cols], in_=y_codes[:, cols].bitcast(I32))
 
         weave_x(0)
         weave_x(1)
         quantise_x(0)
-        product(0, (0,), 5, slice(0, 2))
+        product(0, 0, 5)
         quantise_x(1)
-        product(1, (0,), 4, None)
+        product(1, 0, 4)
         wt_scales.append(ring.tile([P, HALF], U8, name="wt_scales1", offset=0, align_bytes=64))
         quantise(wt_codes[1][:], wt_scales[1][:], wt_bf[1][:])
-        product(0, (1,), 7, slice(2, 4))
-        product(1, (1,), 6, slice(0, 4))
+        product(0, 1, 7)
+        product(1, 1, 6)
         for c in range(2, CHUNKS):
             weave_x(c)
         for c in range(2, CHUNKS):
             quantise_x(c)
-            product(c, (0, 1), c - 2, slice(0, 4))
+            product(c, 0, c - 2)
+        for c in range(2, CHUNKS):
+            product(c, 1, c)
         round_y(0)
-        for c in range(CHUNKS - 2):
-            round_y(c + 1)
-            planes(c)
-        planes(CHUNKS - 2)
-        round_y(CHUNKS - 1)
-        planes(CHUNKS - 1)
+        round_y(1)
+        planes(0, 2)
+        store_codes(0)
+        round_y(2)
+        round_y(3)
+        planes(2, 1)
+        planes(3, 1)
+        store_codes(1)
         for quad in range(4):
             queue = nc.scalar if quad % 2 else nc.sync
             queue.dma_start(out=out_2[0, 4 * quad:4 * quad + 4, :].bitcast(I32),

@@ -156,7 +156,19 @@ def tile_attend_rollout_pl_kernel(tc, query, keys_words, keys_scales, qpool_word
         k2w = sb_tile([P, J], U32, "k2w")
         nc.vector.tensor_copy(out=k2w[:], in_=k2w_win[:].bitcast(U32).indirect(offs2_sb[:]))
         k2s = sb_tile([P, J], U8, "k2s")
-        nc.vector.tensor_copy(out=k2s[:], in_=k2s_win[:].indirect(offs2_sb[:]))
+        b_banks = [bank((4, 5, 6, 2)[t], [P, J], "b_ps%d" % t) for t in range(PACK)]
+
+        def second_scores(t, slots):
+            rows = slice(t * P, (t + 1) * P)
+            nc.tensor.matmul_mx(out=b_banks[t][:, slots], lhsT=qw[:, rows].bitcast(FP8X4),
+                                lhsT_scale=qs[QPOOL_ROW:P, rows], rhs=k2w[:, slots].bitcast(FP8X4),
+                                rhs_scale=k2s[KEYS2_ROW:P, slots], start=True, stop=True)
+
+        for a in range(2):
+            slots = slice(a * HALF, (a + 1) * HALF)
+            nc.vector.tensor_copy(out=k2s[:, slots], in_=k2s_win[:].indirect(offs2_sb[:, 16 * a:16 * (a + 1)]))
+            for t in range(2):
+                second_scores(t, slots)
 
         wt_bf = [sb_tile([P, HALF * PACK], BF16, "wt_bf0")]
 
@@ -194,10 +206,9 @@ def tile_attend_rollout_pl_kernel(tc, query, keys_words, keys_scales, qpool_word
         r_rows = []
 
         def second_map(t):
-            b_ps = bank((4, 5, 6, 2)[t], [P, J], "b_ps%d" % t)
-            cols = slice(t * P, (t + 1) * P)
-            nc.tensor.matmul_mx(out=b_ps[:], lhsT=qw[:, cols].bitcast(FP8X4), lhsT_scale=qs[QPOOL_ROW:P, cols],
-                                rhs=k2w[:].bitcast(FP8X4), rhs_scale=k2s[KEYS2_ROW:P, :], start=True, stop=True)
+            b_ps = b_banks[t]
+            if t >= 2:
+                second_scores(t, slice(0, J))
             row_max = sb_tile([P, 1], F32, "row_max%d" % t)
             nc.vector.tensor_reduce(out=row_max[:], in_=b_ps[:], axis=AX.X, op=ALU.max, negate=True)
             r_rows.append(sb_tile([P, J], F32, "r%d" % t))
@@ -229,21 +240,24 @@ def tile_attend_rollout_pl_kernel(tc, query, keys_words, keys_scales, qpool_word
         first_pair_on_scalar()
         wt_ps = bank(3, [P, 2, HALF], "wt_ps")
         w_first = weigh(0, "k2s_win")
-        for t in range(PACK - 1):
+        for t in range(PACK):
             second_map(t)
-        nc.vector.reciprocal(out=inv[:, 4:6], in_=sums[:, 4:6])
-        second_map(PACK - 1)
-        nc.vector.reciprocal(out=inv[:, 6:7], in_=sums[:, 6:7])
+        row_inv = sb_tile([P, 2], F32, "row_inv")
         row_scale = sb_tile([P, 2], F32, "row_scale")
-        nc.vector.tensor_tensor(out=row_scale[:], in0=inv[:, 4:6], in1=sb_cols[:, 0:2], op=ALU.mult)
+        for t in range(2):
+            nc.gpsimd.tensor_tensor(out=row_inv[:, t:t + 1], in0=sums[:, 4 + t:5 + t], in1=minus_one[:, 0:1],
+                                    op=ALU.pow)
+            nc.gpsimd.tensor_tensor(out=row_scale[:, t:t + 1], in0=row_inv[:, t:t + 1], in1=sb_cols[:, t:t + 1],
+                                    op=ALU.mult)
+        nc.vector.reciprocal(out=inv[:, 6:7], in_=sums[:, 6:7])
         turn(0, w_first)
         turn(1, weigh(1, "row_max1"))
 
         scale_x_on_scalar(0, 0)
-        scale_x_on_scalar(0, 1)
         scale_x_on_scalar(1, 0)
-        wt_bf.append(sb_tile([P, HALF * PACK], BF16, "wt_bf1", "r0"))
+        wt_bf.append(sb_tile([P, HALF * PACK], BF16, "wt_bf1"))
         nc.scalar.copy(out=wt_words(1), in_=wt_ps[:].rearrange("p v (m e) -> p e m v", e=2))
+        scale_x_on_scalar(0, 1)
         scale_x_on_scalar(1, 1)
         for a in range(2):
             scale_x_on_vector(2, a)
@@ -275,7 +289,9 @@ def tile_attend_rollout_pl_kernel(tc, query, keys_words, keys_scales, qpool_word
                                     rhs_scale=x_scales[:, cols], start=True, stop=True)
             part = slice(2 * u, 2 * u + 2)
             nc.scalar.copy(out=y_sb[c // 2][:, part, (c % 2) * JC:(c % 2 + 1) * JC], in_=y_ps[:])
-            if c % 2:
+            if (c // 2, u) == (0, 0):
+                nc.sync.dma_start(out=y_rows[:, part, cols], in_=y_sb[0][:, part, cols])
+            elif c % 2:
                 nc.sync.dma_start(out=y_rows[:, part, (c - 1) * JC:(c + 1) * JC], in_=y_sb[c // 2][:, part, :])
 
         def round_y(c):
@@ -312,7 +328,8 @@ def tile_attend_rollout_pl_kernel(tc, query, keys_words, keys_scales, qpool_word
             product(c, 1, c)
         round_y(0)
         round_y(1)
-        planes(0, 2)
+        planes(0, 1)
+        planes(1, 1)
         store_codes(0)
         round_y(2)
         round_y(3)

@@ -175,7 +175,6 @@ def tile_attend_rollout_pl_kernel(tc, query, keys_words, keys_scales, qpool_word
         def wt_words(u):
             return wt_bf[u][:].bitcast(F32).rearrange("p (e m v) -> p e m v", e=2, v=2)
 
-        wt_codes = [sb_tile([P, HALF], U32, "wt_codes%d" % u, ("p3", None)[u]) for u in range(2)]
         wt_scales = [sb_tile([P, HALF], U8, "wt_scales0")]
 
         def first_pair_on_scalar():
@@ -240,18 +239,17 @@ def tile_attend_rollout_pl_kernel(tc, query, keys_words, keys_scales, qpool_word
         first_pair_on_scalar()
         wt_ps = bank(3, [P, 2, HALF], "wt_ps")
         w_first = weigh(0, "k2s_win")
-        for t in range(PACK):
+        for t in range(PACK - 1):
             second_map(t)
-        row_inv = sb_tile([P, 2], F32, "row_inv")
+        nc.vector.reciprocal(out=inv[:, 4:6], in_=sums[:, 4:6])
+        second_map(PACK - 1)
         row_scale = sb_tile([P, 2], F32, "row_scale")
-        for t in range(2):
-            nc.gpsimd.tensor_tensor(out=row_inv[:, t:t + 1], in0=sums[:, 4 + t:5 + t], in1=minus_one[:, 0:1],
-                                    op=ALU.pow)
-            nc.gpsimd.tensor_tensor(out=row_scale[:, t:t + 1], in0=row_inv[:, t:t + 1], in1=sb_cols[:, t:t + 1],
-                                    op=ALU.mult)
-        nc.vector.reciprocal(out=inv[:, 6:7], in_=sums[:, 6:7])
+        nc.vector.tensor_tensor(out=row_scale[:], in0=inv[:, 4:6], in1=sb_cols[:, 0:2], op=ALU.mult)
         turn(0, w_first)
         turn(1, weigh(1, "row_max1"))
+        nc.vector.reciprocal(out=inv[:, 6:8], in_=sums[:, 6:8])
+        wt_codes = [sb_tile([P, HALF], U32, "wt_codes0", "row_max2")]
+        quantise(wt_codes[0][:], wt_scales[0][:], wt_bf[0][:])
 
         scale_x_on_scalar(0, 0)
         scale_x_on_scalar(1, 0)
@@ -260,11 +258,8 @@ def tile_attend_rollout_pl_kernel(tc, query, keys_words, keys_scales, qpool_word
         scale_x_on_scalar(0, 1)
         scale_x_on_scalar(1, 1)
         for a in range(2):
-            scale_x_on_vector(2, a)
-        nc.vector.reciprocal(out=inv[:, 7:8], in_=sums[:, 7:8])
-        quantise(wt_codes[0][:], wt_scales[0][:], wt_bf[0][:])
-        for a in range(2):
-            scale_x_on_vector(3, a)
+            for t in (2, 3):
+                scale_x_on_vector(t, a)
 
         x_codes = sb_tile([P, J], U32, "x_codes")
         x_scales = sb_tile([P, J], U8, "x_scales")
@@ -315,6 +310,7 @@ def tile_attend_rollout_pl_kernel(tc, query, keys_words, keys_scales, qpool_word
         product(0, 0, 5)
         quantise_x(1)
         product(1, 0, 4)
+        wt_codes.append(sb_tile([P, HALF], U32, "wt_codes1"))
         wt_scales.append(ring.tile([P, HALF], U8, name="wt_scales1", offset=0, align_bytes=64))
         quantise(wt_codes[1][:], wt_scales[1][:], wt_bf[1][:])
         product(0, 1, 7)

@@ -147,8 +147,9 @@ def tile_attend_rollout_pl_kernel(tc, query, keys_words, keys_scales, qpool_word
         nc.gpsimd.tensor_tensor(out=early_inv[:], in0=sums[:, 0:2], in1=minus_one[:], op=ALU.pow)
         p_tiles.append(first_map(1, 1))
         shares = [sb_tile([P, I], F32, "share%d" % h) for h in range(2)]
-        for h in range(2):
-            nc.scalar.activation(out=shares[h][:], in_=p_tiles[h][:], func=ACT.Copy, scale=early_inv[:, h:h + 1])
+        for h, cols in ((0, slice(0, I)), (1, slice(0, I // 2)), (1, slice(I // 2, I))):
+            nc.scalar.activation(out=shares[h][:, cols], in_=p_tiles[h][:, cols], func=ACT.Copy,
+                                 scale=early_inv[:, h:h + 1])
         qw = sb_tile([P, I], U32, "qw")
         nc.vector.tensor_copy(out=qw[:].rearrange("p (t g r) -> p g t r", t=4, r=8),
                               in_=qw_win[:].bitcast(U32).indirect(offs_sb[:]))
@@ -245,11 +246,9 @@ def tile_attend_rollout_pl_kernel(tc, query, keys_words, keys_scales, qpool_word
         second_map(PACK - 1)
         row_scale = sb_tile([P, 2], F32, "row_scale")
         nc.vector.tensor_tensor(out=row_scale[:], in0=inv[:, 4:6], in1=sb_cols[:, 0:2], op=ALU.mult)
+        nc.vector.reciprocal(out=inv[:, 6:7], in_=sums[:, 6:7])
         turn(0, w_first)
         turn(1, weigh(1, "row_max1"))
-        nc.vector.reciprocal(out=inv[:, 6:8], in_=sums[:, 6:8])
-        wt_codes = [sb_tile([P, HALF], U32, "wt_codes0", "row_max2")]
-        quantise(wt_codes[0][:], wt_scales[0][:], wt_bf[0][:])
 
         scale_x_on_scalar(0, 0)
         scale_x_on_scalar(1, 0)
@@ -258,8 +257,12 @@ def tile_attend_rollout_pl_kernel(tc, query, keys_words, keys_scales, qpool_word
         scale_x_on_scalar(0, 1)
         scale_x_on_scalar(1, 1)
         for a in range(2):
-            for t in (2, 3):
-                scale_x_on_vector(t, a)
+            scale_x_on_vector(2, a)
+        nc.vector.reciprocal(out=inv[:, 7:8], in_=sums[:, 7:8])
+        wt_codes = [sb_tile([P, HALF], U32, "wt_codes0", "p3")]
+        quantise(wt_codes[0][:], wt_scales[0][:], wt_bf[0][:])
+        for a in range(2):
+            scale_x_on_vector(3, a)
 
         x_codes = sb_tile([P, J], U32, "x_codes")
         x_scales = sb_tile([P, J], U8, "x_scales")

@@ -141,15 +141,12 @@ def tile_attend_rollout_pl_kernel(tc, query, keys_words, keys_scales, qpool_word
         quantise_query(1)
         p_tiles = [first_map(0, 0), first_map(0, 1)]
         p_tiles.append(first_map(1, 0))
-        minus_one = sb_tile([P, 2], F32, "minus_one")
-        nc.vector.memset(minus_one[:], -1.0)
-        early_inv = sb_tile([P, 2], F32, "early_inv")
-        nc.gpsimd.tensor_tensor(out=early_inv[:], in0=sums[:, 0:2], in1=minus_one[:], op=ALU.pow)
+        nc.vector.reciprocal(out=inv[:, 0:2], in_=sums[:, 0:2])
         p_tiles.append(first_map(1, 1))
         shares = [sb_tile([P, I], F32, "share%d" % h) for h in range(2)]
         for h, cols in ((0, slice(0, I)), (1, slice(0, I // 2)), (1, slice(I // 2, I))):
             nc.scalar.activation(out=shares[h][:, cols], in_=p_tiles[h][:, cols], func=ACT.Copy,
-                                 scale=early_inv[:, h:h + 1])
+                                 scale=inv[:, h:h + 1])
         qw = sb_tile([P, I], U32, "qw")
         nc.vector.tensor_copy(out=qw[:].rearrange("p (t g r) -> p g t r", t=4, r=8),
                               in_=qw_win[:].bitcast(U32).indirect(offs_sb[:]))
@@ -187,10 +184,13 @@ def tile_attend_rollout_pl_kernel(tc, query, keys_words, keys_scales, qpool_word
                                             shares[h][:, t * P:(t + 1) * P], ident[:])
             pairs = sb_tile([P, 2 * HALF * 2], BF16, "w_pairs")
             places = pairs[:].rearrange("p (v e m z) -> p v z e m", v=2, e=2, z=2)
-            for t in range(PACK):
-                nc.scalar.activation(out=places[:, t // 2, t % 2], func=ACT.Copy, scale=sa_cols[:, t:t + 1],
-                                     in_=turned[t // 2][:, t % 2, :].rearrange("p (m e) -> p e m", e=2))
-            nc.scalar.copy(out=wt_words(0), in_=pairs[:].bitcast(F32).rearrange("p (v e m) -> p e m v", v=2, e=2))
+            pair_words = pairs[:].bitcast(F32).rearrange("p (v e m) -> p e m v", v=2, e=2)
+            pieces = [(t, slice(0, 2)) for t in range(PACK - 1)] + [(PACK - 1, slice(e, e + 1)) for e in range(2)]
+            for t, rows in pieces:
+                nc.scalar.activation(out=places[:, t // 2, t % 2, rows], func=ACT.Copy, scale=sa_cols[:, t:t + 1],
+                                     in_=turned[t // 2][:, t % 2, :].rearrange("p (m e) -> p e m", e=2)[:, rows])
+            for e in range(2):
+                nc.scalar.copy(out=wt_words(0)[:, e], in_=pair_words[:, e])
 
         def weigh(h, tag):
             w_h = sb_tile([P, I], BF16, "w%d" % h, tag)

@@ -256,13 +256,12 @@ def tile_attend_rollout_pl_kernel(tc, query, keys_words, keys_scales, qpool_word
         nc.scalar.copy(out=wt_words(1), in_=wt_ps[:].rearrange("p v (m e) -> p e m v", e=2))
         scale_x_on_scalar(0, 1)
         scale_x_on_scalar(1, 1)
-        for a in range(2):
-            scale_x_on_vector(2, a)
+        scale_x_on_vector(2, 0)
         nc.vector.reciprocal(out=inv[:, 7:8], in_=sums[:, 7:8])
         wt_codes = [sb_tile([P, HALF], U32, "wt_codes0", "p3")]
         quantise(wt_codes[0][:], wt_scales[0][:], wt_bf[0][:])
-        for a in range(2):
-            scale_x_on_vector(3, a)
+        scale_x_on_vector(3, 0)
+        scale_x_on_vector(2, 1)
 
         x_codes = sb_tile([P, J], U32, "x_codes")
         x_scales = sb_tile([P, J], U8, "x_scales")
@@ -309,6 +308,7 @@ def tile_attend_rollout_pl_kernel(tc, query, keys_words, keys_scales, qpool_word
 
         weave_x(0)
         weave_x(1)
+        scale_x_on_vector(3, 1)
         quantise_x(0)
         product(0, 0, 5)
         quantise_x(1)

@@ -109,12 +109,14 @@ def tile_attend_rollout_pl_kernel(tc, query, keys_words, keys_scales, qpool_word
         sums = sb_tile([P, 8], F32, "sums")
         inv = sb_tile([P, 8], F32, "inv")
 
-        def quantise_query(h):
+        def quantise_query(h, pieces):
             q_bf = sb_tile([P, HALF * PACK], BF16, "q_bf%d" % h)
             nc.scalar.copy(out=q_bf[:].rearrange("p (u m e t) -> p m t u e", u=2, e=2, t=PACK),
                            in_=q_both[:, h].rearrange("p t (m u e) -> p m t u e", u=2, e=2))
-            cols = slice(h * HALF, (h + 1) * HALF)
-            quantise(q_codes[:, cols], q_scales[:, cols], q_bf[:])
+            width = HALF // pieces
+            for k in range(pieces):
+                cols = slice(h * HALF + k * width, h * HALF + (k + 1) * width)
+                quantise(q_codes[:, cols], q_scales[:, cols], q_bf[:, k * width * PACK:(k + 1) * width * PACK])
 
         def first_map(u, h):
             n = 2 * u + h
@@ -134,23 +136,29 @@ def tile_attend_rollout_pl_kernel(tc, query, keys_words, keys_scales, qpool_word
                                  accum_out=sums[:, n:n + 1])
             return p_n
 
-        quantise_query(0)
+        quantise_query(0, 1)
         qs = sb_tile([P, I], U8, "qs")
         nc.vector.tensor_copy(out=qs[:].rearrange("p (t g r) -> p g t r", t=4, r=8),
                               in_=qs_win[:].indirect(offs_sb[:]))
-        quantise_query(1)
-        p_tiles = [first_map(0, 0), first_map(0, 1)]
-        p_tiles.append(first_map(1, 0))
-        nc.vector.reciprocal(out=inv[:, 0:2], in_=sums[:, 0:2])
-        p_tiles.append(first_map(1, 1))
+        p_tiles = {0: first_map(0, 0)}
+        quantise_query(1, 2)
+        p_tiles[2] = first_map(1, 0)
+        nc.vector.reciprocal(out=inv[:, 0:1], in_=sums[:, 0:1])
+        p_tiles[1] = first_map(0, 1)
+        p_tiles[3] = first_map(1, 1)
         shares = [sb_tile([P, I], F32, "share%d" % h) for h in range(2)]
-        for h, cols in ((0, slice(0, I)), (1, slice(0, I // 2)), (1, slice(I // 2, I))):
+
+        def divide(h, cols):
             nc.scalar.activation(out=shares[h][:, cols], in_=p_tiles[h][:, cols], func=ACT.Copy,
                                  scale=inv[:, h:h + 1])
+
+        divide(0, slice(0, I))
         qw = sb_tile([P, I], U32, "qw")
         nc.vector.tensor_copy(out=qw[:].rearrange("p (t g r) -> p g t r", t=4, r=8),
                               in_=qw_win[:].bitcast(U32).indirect(offs_sb[:]))
-        nc.vector.reciprocal(out=inv[:, 2:4], in_=sums[:, 2:4])
+        nc.vector.reciprocal(out=inv[:, 1:4], in_=sums[:, 1:4])
+        divide(1, slice(0, I // 2))
+        divide(1, slice(I // 2, I))
         k2w = sb_tile([P, J], U32, "k2w")
         nc.vector.tensor_copy(out=k2w[:], in_=k2w_win[:].bitcast(U32).indirect(offs2_sb[:]))
         k2s = sb_tile([P, J], U8, "k2s")
@@ -177,11 +185,10 @@ def tile_attend_rollout_pl_kernel(tc, query, keys_words, keys_scales, qpool_word
 
         def first_pair_on_scalar():
             turned = [bank(v, [P, 2, HALF], "turned%d" % v) for v in range(2)]
-            for v in range(2):
-                for h in range(2):
-                    for t in (2 * v, 2 * v + 1):
-                        nc.tensor.transpose(turned[v][:, t % 2, h * P:(h + 1) * P],
-                                            shares[h][:, t * P:(t + 1) * P], ident[:])
+            for h in range(2):
+                for t in range(PACK):
+                    nc.tensor.transpose(turned[t // 2][:, t % 2, h * P:(h + 1) * P],
+                                        shares[h][:, t * P:(t + 1) * P], ident[:])
             pairs = sb_tile([P, 2 * HALF * 2], BF16, "w_pairs")
             places = pairs[:].rearrange("p (v e m z) -> p v z e m", v=2, e=2, z=2)
             pair_words = pairs[:].bitcast(F32).rearrange("p (v e m) -> p e m v", v=2, e=2)

@@ -84,6 +84,7 @@ def tile_attend_rollout_pl_kernel(tc, query, keys_words, keys_scales, qpool_word
         qw_win = placed.tile([P, T], I32, name="qw_win", offset=query_bytes, align_bytes=64)
         nc.sync.dma_start(out=qw_win[:], in_=qpool_words[0].rearrange("p n t -> p (n t)").bitcast(I32))
 
+
         kw = sb_tile([P, I], U16, "kw")
         nc.vector.tensor_copy(out=kw[:], in_=kw_win[:].indirect(offs_sb[:]))
         ks = sb_tile([P, I], U8, "ks")
@@ -105,64 +106,60 @@ def tile_attend_rollout_pl_kernel(tc, query, keys_words, keys_scales, qpool_word
 
         q_codes = sb_tile([P, Q], U32, "q_codes")
         q_scales = sb_tile([P, Q], U8, "q_scales")
-        neg_max = sb_tile([P, 4], F32, "neg_max")
+        neg_max = [sb_tile([P, 2], F32, "neg_max%d" % h) for h in range(2)]
         sums = sb_tile([P, 8], F32, "sums")
         inv = sb_tile([P, 8], F32, "inv")
 
-        def quantise_query(h, pieces):
+        def round_query(h):
             q_bf = sb_tile([P, HALF * PACK], BF16, "q_bf%d" % h)
             nc.scalar.copy(out=q_bf[:].rearrange("p (u m e t) -> p m t u e", u=2, e=2, t=PACK),
                            in_=q_both[:, h].rearrange("p t (m u e) -> p m t u e", u=2, e=2))
-            width = HALF // pieces
-            for k in range(pieces):
-                cols = slice(h * HALF + k * width, h * HALF + (k + 1) * width)
-                quantise(q_codes[:, cols], q_scales[:, cols], q_bf[:, k * width * PACK:(k + 1) * width * PACK])
+            return q_bf
 
-        def first_map(u, h):
-            n = 2 * u + h
-            a_ps = bank(n, [P, I], "a_ps%d" % n)
-            cols = slice((2 * h + u) * P, (2 * h + u + 1) * P)
+        def quantise_query(h, q_bf):
+            cols = slice(h * HALF, (h + 1) * HALF)
+            quantise(q_codes[:, cols], q_scales[:, cols], q_bf[:])
+
+        p_tiles = {}
+
+        def first_map(h, u, index):
+            n = 2 * h + u
+            a_ps = bank(index, [P, I], "a_ps%d" % n)
+            cols = slice(n * P, (n + 1) * P)
             nc.tensor.matmul_mx(out=a_ps[:], lhsT=q_codes[:, cols].bitcast(FP8X4), lhsT_scale=q_scales[:, cols],
                                 rhs=kw[:].bitcast(FP4X4), rhs_scale=ks[:], start=True, stop=True)
-            nc.vector.tensor_reduce(out=neg_max[:, n:n + 1], in_=a_ps[:], axis=AX.X, op=ALU.max, negate=True)
-            p_n = sb_tile([P, I], F32, "p%d" % n)
-            if u == 0:
-                dealt = p_n[:].rearrange("p (t g r) -> p g t r", t=PACK, r=8)
+            nc.vector.tensor_reduce(out=neg_max[h][:, u:u + 1], in_=a_ps[:], axis=AX.X, op=ALU.max, negate=True)
+            return a_ps
+
+        def first_exp(h, u, a_ps):
+            n = 2 * h + u
+            p_tiles[n] = sb_tile([P, I], F32, "p%d" % n)
+            if h == 0:
+                dealt = p_tiles[n][:].rearrange("p (t g r) -> p g t r", t=PACK, r=8)
                 scores = a_ps[:].rearrange("p (g t r) -> p g t r", t=PACK, r=8)
             else:
-                dealt = p_n[:].rearrange("p (v g r e) -> p g v r e", v=2, r=8, e=2)
+                dealt = p_tiles[n][:].rearrange("p (v g r e) -> p g v r e", v=2, r=8, e=2)
                 scores = a_ps[:].rearrange("p (g v e r) -> p g v r e", v=2, r=8, e=2)
-            nc.scalar.activation(out=dealt, in_=scores, func=ACT.Exp, bias=neg_max[:, n:n + 1],
+            nc.scalar.activation(out=dealt, in_=scores, func=ACT.Exp, bias=neg_max[h][:, u:u + 1],
                                  accum_out=sums[:, n:n + 1])
-            return p_n
 
-        quantise_query(0, 1)
+        q_bf = [round_query(h) for h in range(2)]
+        quantise_query(0, q_bf[0])
         qs = sb_tile([P, I], U8, "qs")
         nc.vector.tensor_copy(out=qs[:].rearrange("p (t g r) -> p g t r", t=4, r=8),
                               in_=qs_win[:].indirect(offs_sb[:]))
-        p_tiles = {0: first_map(0, 0)}
-        quantise_query(1, 2)
-        p_tiles[2] = first_map(1, 0)
-        nc.vector.reciprocal(out=inv[:, 0:1], in_=sums[:, 0:1])
-        p_tiles[1] = first_map(0, 1)
-        p_tiles[3] = first_map(1, 1)
-        shares = [sb_tile([P, I], F32, "share%d" % h) for h in range(2)]
-
-        def divide(h, cols):
-            nc.scalar.activation(out=shares[h][:, cols], in_=p_tiles[h][:, cols], func=ACT.Copy,
-                                 scale=inv[:, h:h + 1])
-
-        divide(0, slice(0, I))
+        quantise_query(1, q_bf[1])
+        for n in range(4):
+            first_exp(n // 2, n % 2, first_map(n // 2, n % 2, n))
+        nc.vector.reciprocal(out=inv[:, 0:2], in_=sums[:, 0:2])
         qw = sb_tile([P, I], U32, "qw")
         nc.vector.tensor_copy(out=qw[:].rearrange("p (t g r) -> p g t r", t=4, r=8),
                               in_=qw_win[:].bitcast(U32).indirect(offs_sb[:]))
-        nc.vector.reciprocal(out=inv[:, 1:4], in_=sums[:, 1:4])
-        divide(1, slice(0, I // 2))
-        divide(1, slice(I // 2, I))
+        nc.vector.reciprocal(out=inv[:, 2:4], in_=sums[:, 2:4])
         k2w = sb_tile([P, J], U32, "k2w")
         nc.vector.tensor_copy(out=k2w[:], in_=k2w_win[:].bitcast(U32).indirect(offs2_sb[:]))
         k2s = sb_tile([P, J], U8, "k2s")
-        b_banks = [bank((4, 5, 6, 2)[t], [P, J], "b_ps%d" % t) for t in range(PACK)]
+        b_banks = [bank(4 + t, [P, J], "b_ps%d" % t) for t in range(PACK - 1)]
 
         def second_scores(t, slots):
             rows = slice(t * P, (t + 1) * P)
@@ -176,39 +173,65 @@ def tile_attend_rollout_pl_kernel(tc, query, keys_words, keys_scales, qpool_word
             for t in range(2):
                 second_scores(t, slots)
 
-        wt_bf = [sb_tile([P, HALF * PACK], BF16, "wt_bf0")]
+        wt_bf = [sb_tile([P, HALF * PACK], BF16, "wt_bf%d" % u) for u in range(2)]
 
-        def wt_words(u):
-            return wt_bf[u][:].bitcast(F32).rearrange("p (e m v) -> p e m v", e=2, v=2)
+        def wt_words(u, h):
+            words = wt_bf[u][:].bitcast(F32).rearrange("p (e m v) -> p e m v", e=2, v=2)
+            return words[:, :, h * 64:(h + 1) * 64, :]
 
-        wt_scales = [sb_tile([P, HALF], U8, "wt_scales0")]
+        shares = [sb_tile([P, I], F32, "share%d" % u) for u in range(2)]
+        pairs = [sb_tile([P, 2 * P * 2], BF16, "w_pairs%d" % u) for u in range(2)]
 
-        def first_pair_on_scalar():
-            turned = [bank(v, [P, 2, HALF], "turned%d" % v) for v in range(2)]
-            for h in range(2):
-                for t in range(PACK):
-                    nc.tensor.transpose(turned[t // 2][:, t % 2, h * P:(h + 1) * P],
-                                        shares[h][:, t * P:(t + 1) * P], ident[:])
-            pairs = sb_tile([P, 2 * HALF * 2], BF16, "w_pairs")
-            places = pairs[:].rearrange("p (v e m z) -> p v z e m", v=2, e=2, z=2)
-            pair_words = pairs[:].bitcast(F32).rearrange("p (v e m) -> p e m v", v=2, e=2)
-            pieces = [(t, slice(0, 2)) for t in range(PACK - 1)] + [(PACK - 1, slice(e, e + 1)) for e in range(2)]
-            for t, rows in pieces:
-                nc.scalar.activation(out=places[:, t // 2, t % 2, rows], func=ACT.Copy, scale=sa_cols[:, t:t + 1],
-                                     in_=turned[t // 2][:, t % 2, :].rearrange("p (m e) -> p e m", e=2)[:, rows])
-            for e in range(2):
-                nc.scalar.copy(out=wt_words(0)[:, e], in_=pair_words[:, e])
+        def divide(u, cols):
+            nc.scalar.activation(out=shares[u][:, cols], in_=p_tiles[u][:, cols], func=ACT.Copy,
+                                 scale=inv[:, u:u + 1])
 
-        def weigh(h, tag):
-            w_h = sb_tile([P, I], BF16, "w%d" % h, tag)
-            nc.vector.scalar_tensor_tensor(out=w_h[:], in0=p_tiles[2 + h][:], scalar=inv[:, 2 + h:3 + h], in1=sa_all,
+        def turn_share(u, banks):
+            turned = [bank(index, [P, PACK // len(banks), P], "turned%d_%d" % (u, index)) for index in banks]
+            per_bank = PACK // len(banks)
+            for t in range(PACK):
+                nc.tensor.transpose(turned[t // per_bank][:, t % per_bank, :], shares[u][:, t * P:(t + 1) * P],
+                                    ident[:])
+            return [turned[t // per_bank][:, t % per_bank, :] for t in range(PACK)]
+
+        def times_sa(u, t, turned):
+            places = pairs[u][:].rearrange("p (v e m z) -> p v z e m", v=2, e=2, z=2)
+            nc.scalar.activation(out=places[:, t // 2, t % 2], func=ACT.Copy, scale=sa_cols[:, t:t + 1],
+                                 in_=turned[t].rearrange("p (m e) -> p e m", e=2))
+
+        def weave_w(u):
+            nc.scalar.copy(out=wt_words(u, 0),
+                           in_=pairs[u][:].bitcast(F32).rearrange("p (v e m) -> p e m v", v=2, e=2))
+
+        divide(0, slice(0, I // 2))
+        divide(0, slice(I // 2, I))
+        turned0 = turn_share(0, (0, 2))
+        divide(1, slice(0, I))
+        turned1 = turn_share(1, (1, 3))
+        for t in range(PACK):
+            times_sa(0, t, turned0)
+        times_sa(1, 0, turned1)
+        times_sa(1, 1, turned1)
+        weave_w(0)
+        times_sa(1, 2, turned1)
+        times_sa(1, 3, turned1)
+        weave_w(1)
+
+        def weigh(u):
+            w_u = sb_tile([P, I], BF16, "w%d" % u, ("k2s_win", "row_max1")[u])
+            nc.vector.scalar_tensor_tensor(out=w_u[:], in0=p_tiles[2 + u][:], scalar=inv[:, 2 + u:3 + u], in1=sa_all,
                                            op0=ALU.mult, op1=ALU.mult)
-            return w_h
+            return w_u
 
-        def turn(h, w_h):
-            words = w_h[:].bitcast(F32)
+        def turn(u, w_u):
+            wt_ps = bank((4, 0)[u], [P, 2, P], "wt_ps%d" % u)
+            words = w_u[:].bitcast(F32)
             for v in range(2):
-                nc.tensor.transpose(wt_ps[:, v, h * P:(h + 1) * P], words[:, v * P:(v + 1) * P], ident[:])
+                nc.tensor.transpose(wt_ps[:, v, :], words[:, v * P:(v + 1) * P], ident[:])
+            return wt_ps
+
+        def copy_turned(u, wt_ps):
+            nc.scalar.copy(out=wt_words(u, 1), in_=wt_ps[:].rearrange("p v (m e) -> p e m v", e=2))
 
         r_rows = []
 
@@ -244,9 +267,8 @@ def tile_attend_rollout_pl_kernel(tc, query, keys_words, keys_scales, qpool_word
             both = x_pairs[c // 2][:].bitcast(F32).rearrange("p (v j) -> p j v", v=2)
             nc.vector.tensor_copy(out=words, in_=both[:, (c % 2) * JC:(c % 2 + 1) * JC, :])
 
-        first_pair_on_scalar()
-        wt_ps = bank(3, [P, 2, HALF], "wt_ps")
-        w_first = weigh(0, "k2s_win")
+        b_banks.append(bank(2, [P, J], "b_ps3"))
+        w_first = weigh(0)
         for t in range(PACK - 1):
             second_map(t)
         nc.vector.reciprocal(out=inv[:, 4:6], in_=sums[:, 4:6])
@@ -254,21 +276,22 @@ def tile_attend_rollout_pl_kernel(tc, query, keys_words, keys_scales, qpool_word
         row_scale = sb_tile([P, 2], F32, "row_scale")
         nc.vector.tensor_tensor(out=row_scale[:], in0=inv[:, 4:6], in1=sb_cols[:, 0:2], op=ALU.mult)
         nc.vector.reciprocal(out=inv[:, 6:7], in_=sums[:, 6:7])
-        turn(0, w_first)
-        turn(1, weigh(1, "row_max1"))
+        wt_ps0 = turn(0, w_first)
+        wt_ps1 = turn(1, weigh(1))
 
         scale_x_on_scalar(0, 0)
         scale_x_on_scalar(1, 0)
-        wt_bf.append(sb_tile([P, HALF * PACK], BF16, "wt_bf1"))
-        nc.scalar.copy(out=wt_words(1), in_=wt_ps[:].rearrange("p v (m e) -> p e m v", e=2))
+        copy_turned(0, wt_ps0)
+        copy_turned(1, wt_ps1)
         scale_x_on_scalar(0, 1)
         scale_x_on_scalar(1, 1)
         scale_x_on_vector(2, 0)
         nc.vector.reciprocal(out=inv[:, 7:8], in_=sums[:, 7:8])
-        wt_codes = [sb_tile([P, HALF], U32, "wt_codes0", "p3")]
-        quantise(wt_codes[0][:], wt_scales[0][:], wt_bf[0][:])
-        scale_x_on_vector(3, 0)
+        wt_codes = [sb_tile([P, HALF], U32, "wt_codes0", "p3"), sb_tile([P, HALF], U32, "wt_codes1")]
+        wt_scales = [sb_tile([P, HALF], U8, "wt_scales0")]
         scale_x_on_vector(2, 1)
+        scale_x_on_vector(3, 0)
+        scale_x_on_vector(3, 1)
 
         x_codes = sb_tile([P, J], U32, "x_codes")
         x_scales = sb_tile([P, J], U8, "x_scales")
@@ -315,23 +338,22 @@ def tile_attend_rollout_pl_kernel(tc, query, keys_words, keys_scales, qpool_word
 
         weave_x(0)
         weave_x(1)
-        scale_x_on_vector(3, 1)
+        quantise(wt_codes[0][:], wt_scales[0][:], wt_bf[0][:])
         quantise_x(0)
-        product(0, 0, 5)
+        product(0, 0, 3)
         quantise_x(1)
-        product(1, 0, 4)
-        wt_codes.append(sb_tile([P, HALF], U32, "wt_codes1"))
+        product(1, 0, 5)
         wt_scales.append(ring.tile([P, HALF], U8, name="wt_scales1", offset=0, align_bytes=64))
         quantise(wt_codes[1][:], wt_scales[1][:], wt_bf[1][:])
-        product(0, 1, 7)
-        product(1, 1, 6)
+        product(0, 1, 6)
+        product(1, 1, 1)
         for c in range(2, CHUNKS):
             weave_x(c)
         for c in range(2, CHUNKS):
             quantise_x(c)
-            product(c, 0, c - 2)
+            product(c, 0, (2, 4)[c - 2])
         for c in range(2, CHUNKS):
-            product(c, 1, c)
+            product(c, 1, (7, 0)[c - 2])
         round_y(0)
         round_y(1)
         planes(0, 1)

@@ -64,6 +64,8 @@ def tile_attend_rollout_pl_kernel(tc, query, keys_words, keys_scales, qpool_word
         ident = sb_tile([P, P], F32, "ident")
         nc.vector.memset(ident[:], 0.0)
         make_identity(nc, ident[:], nomemset=True)
+        w_and_sb = sb_tile([P, 2, 2 * P], F32, "w_and_sb")
+        nc.vector.memset(w_and_sb[:, 0, P:2 * P], 0.0)
 
         offs_sb = lists.tile([P, I // 16], U16, name="offs_sb")
         offs2_sb = lists.tile([P, J // 16], U16, name="offs2_sb")
@@ -79,8 +81,6 @@ def tile_attend_rollout_pl_kernel(tc, query, keys_words, keys_scales, qpool_word
         load_scale_rows(nc.sync, qs_win, qpool_scales, QPOOL_ROW)
         nc.sync.dma_start(out=vec_rows[4:8, :].rearrange("t (g r) -> t g r", r=8),
                           in_=sa.rearrange("o (g t r) -> t g (r o)", t=4, r=8))
-        nc.sync.dma_start(out=vec_rows[0:4, :].rearrange("t (g r) -> t g r", r=8),
-                          in_=sb.rearrange("(g t r) o -> t g (r o)", t=4, r=8))
         qw_win = placed.tile([P, T], I32, name="qw_win", offset=query_bytes, align_bytes=64)
         nc.sync.dma_start(out=qw_win[:], in_=qpool_words[0].rearrange("p n t -> p (n t)").bitcast(I32))
 
@@ -92,13 +92,13 @@ def tile_attend_rollout_pl_kernel(tc, query, keys_words, keys_scales, qpool_word
         k2w_win = sb_tile([P, U], I32, "k2w_win", "slot_a")
         nc.sync.dma_start(out=k2w_win[:], in_=keys2_words[0].rearrange("p n t -> p (n t)").bitcast(I32))
         load_scale_rows(nc.sync, k2s_win, keys2_scales, KEYS2_ROW)
+        nc.sync.dma_start(out=w_and_sb[0:4, 0, P:2 * P].rearrange("t (g r) -> t g r", r=8),
+                          in_=sb.rearrange("(g t r) o -> t g (r o)", t=4, r=8))
 
         vec_ps = bank(6, [P, P], "vec_ps")
         nc.tensor.transpose(vec_ps[:], vec_rows[:], ident[:])
         sa_cols = sb_tile([P, PACK], F32, "sa_cols")
         nc.scalar.copy(out=sa_cols[:], in_=vec_ps[:, 4:8])
-        sb_cols = sb_tile([P, PACK], F32, "sb_cols")
-        nc.scalar.activation(out=sb_cols[:], in_=vec_ps[:, 0:4], func=ACT.Copy, scale=512.0)
         sa_ps = bank(7, [P, 2, P, 2], "sa_ps")
         for t in range(PACK):
             nc.tensor.transpose(sa_ps[:, t // 2, :, t % 2], sa_cols[:, t:t + 1].to_broadcast([P, P]), ident[:])
@@ -159,7 +159,7 @@ def tile_attend_rollout_pl_kernel(tc, query, keys_words, keys_scales, qpool_word
         k2w = sb_tile([P, J], U32, "k2w")
         nc.vector.tensor_copy(out=k2w[:], in_=k2w_win[:].bitcast(U32).indirect(offs2_sb[:]))
         k2s = sb_tile([P, J], U8, "k2s")
-        b_banks = [bank(4 + t, [P, J], "b_ps%d" % t) for t in range(PACK - 1)]
+        b_banks = [bank(4 + t, [P, J], "b_ps%d" % t) for t in range(2)]
 
         def second_scores(t, slots):
             rows = slice(t * P, (t + 1) * P)
@@ -217,21 +217,25 @@ def tile_attend_rollout_pl_kernel(tc, query, keys_words, keys_scales, qpool_word
         times_sa(1, 3, turned1)
         weave_w(1)
 
-        def weigh(u):
-            w_u = sb_tile([P, I], BF16, "w%d" % u, ("k2s_win", "row_max1")[u])
-            nc.vector.scalar_tensor_tensor(out=w_u[:], in0=p_tiles[2 + u][:], scalar=inv[:, 2 + u:3 + u], in1=sa_all,
+        def weigh(u, rows, out):
+            nc.vector.scalar_tensor_tensor(out=out, in0=p_tiles[2 + u][:].rearrange("p (v n) -> p v n", v=2)[:, rows],
+                                           scalar=inv[:, 2 + u:3 + u],
+                                           in1=sa_all.rearrange("p (v n) -> p v n", v=2)[:, rows],
                                            op0=ALU.mult, op1=ALU.mult)
-            return w_u
 
-        def turn(u, w_u):
-            wt_ps = bank((4, 0)[u], [P, 2, P], "wt_ps%d" % u)
-            words = w_u[:].bitcast(F32)
+        def turn(u, words):
+            wt_ps = bank((4, 1)[u], [P, 3, P], "wt_ps%d" % u)
             for v in range(2):
-                nc.tensor.transpose(wt_ps[:, v, :], words[:, v * P:(v + 1) * P], ident[:])
+                nc.tensor.transpose(wt_ps[:, v, :], words[v], ident[:])
             return wt_ps
 
+        def weigh_last(v):
+            half = sb_tile([P, 1, P], F32, "w1_%d" % v, ("k2s_win", "row_max1")[v])
+            weigh(1, slice(v, v + 1), half[:].bitcast(BF16))
+            return half[:, 0, :]
+
         def copy_turned(u, wt_ps):
-            nc.scalar.copy(out=wt_words(u, 1), in_=wt_ps[:].rearrange("p v (m e) -> p e m v", e=2))
+            nc.scalar.copy(out=wt_words(u, 1), in_=wt_ps[:, 0:2, :].rearrange("p v (m e) -> p e m v", e=2))
 
         r_rows = []
 
@@ -251,14 +255,14 @@ def tile_attend_rollout_pl_kernel(tc, query, keys_words, keys_scales, qpool_word
         def x_place(t, a):
             return x_pairs[a][:].rearrange("p (v j z) -> p v j z", v=2, z=2)[:, t // 2, :, t % 2]
 
-        def scale_x_on_vector(t, a):
-            nc.vector.tensor_scalar(out=x_place(t, a), in0=r_rows[t][:, a * HALF:(a + 1) * HALF],
+        def scale_x_on_vector(t, a, cols=slice(0, HALF)):
+            nc.vector.tensor_scalar(out=x_place(t, a)[:, cols], in0=r_rows[t][:, a * HALF:(a + 1) * HALF][:, cols],
                                     scalar1=inv[:, 4 + t:5 + t], scalar2=sb_cols[:, t:t + 1],
                                     op0=ALU.mult, op1=ALU.mult)
 
-        def scale_x_on_scalar(t, a):
-            nc.scalar.activation(out=x_place(t, a), in_=r_rows[t][:, a * HALF:(a + 1) * HALF], func=ACT.Copy,
-                                 scale=row_scale[:, t:t + 1])
+        def scale_x_on_scalar(t, a, cols=slice(0, HALF)):
+            nc.scalar.activation(out=x_place(t, a)[:, cols], in_=r_rows[t][:, a * HALF:(a + 1) * HALF][:, cols],
+                                 func=ACT.Copy, scale=row_scale[:, t:t + 1])
 
         def weave_x(c):
             x_bf[c] = ring.tile([P, JC, PACK], BF16, name="x_bf%d" % c, offset=(0, 2048, 256, 2048)[c],
@@ -267,21 +271,29 @@ def tile_attend_rollout_pl_kernel(tc, query, keys_words, keys_scales, qpool_word
             both = x_pairs[c // 2][:].bitcast(F32).rearrange("p (v j) -> p j v", v=2)
             nc.vector.tensor_copy(out=words, in_=both[:, (c % 2) * JC:(c % 2 + 1) * JC, :])
 
-        b_banks.append(bank(2, [P, J], "b_ps3"))
-        w_first = weigh(0)
-        for t in range(PACK - 1):
-            second_map(t)
+        b_banks.extend(bank((6, 2)[t], [P, J], "b_ps%d" % (2 + t)) for t in range(2))
+        weigh(0, slice(0, 2), w_and_sb[:].bitcast(BF16)[:, :, 0:2 * P])
+        w_last = [weigh_last(0)]
+        second_map(0)
+        second_map(1)
+        wt_ps0 = turn(0, [w_and_sb[:, v, 0:P] for v in range(2)])
+        nc.tensor.transpose(wt_ps0[:, 2, :], w_and_sb[:, 0, P:2 * P], ident[:])
+        sb_cols = sb_tile([P, PACK], F32, "sb_cols")
+        second_map(2)
+        nc.vector.tensor_scalar(out=sb_cols[:], in0=wt_ps0[:, 2, 0:4], scalar1=512.0, scalar2=None, op0=ALU.mult)
         nc.vector.reciprocal(out=inv[:, 4:6], in_=sums[:, 4:6])
         second_map(PACK - 1)
         row_scale = sb_tile([P, 2], F32, "row_scale")
         nc.vector.tensor_tensor(out=row_scale[:], in0=inv[:, 4:6], in1=sb_cols[:, 0:2], op=ALU.mult)
         nc.vector.reciprocal(out=inv[:, 6:7], in_=sums[:, 6:7])
-        wt_ps0 = turn(0, w_first)
-        wt_ps1 = turn(1, weigh(1))
+        w_last.append(weigh_last(1))
+        wt_ps1 = turn(1, w_last)
 
-        scale_x_on_scalar(0, 0)
-        scale_x_on_scalar(1, 0)
         copy_turned(0, wt_ps0)
+        for t in range(2):
+            scale_x_on_vector(t, 0, slice(0, JC))
+        for t in range(2):
+            scale_x_on_scalar(t, 0, slice(JC, HALF))
         copy_turned(1, wt_ps1)
         scale_x_on_scalar(0, 1)
         scale_x_on_scalar(1, 1)
@@ -291,6 +303,7 @@ def tile_attend_rollout_pl_kernel(tc, query, keys_words, keys_scales, qpool_word
         wt_scales = [sb_tile([P, HALF], U8, "wt_scales0")]
         scale_x_on_vector(2, 1)
         scale_x_on_vector(3, 0)
+        quantise(wt_codes[0][:], wt_scales[0][:], wt_bf[0][:])
         scale_x_on_vector(3, 1)
 
         x_codes = sb_tile([P, J], U32, "x_codes")
@@ -338,7 +351,6 @@ def tile_attend_rollout_pl_kernel(tc, query, keys_words, keys_scales, qpool_word
 
         weave_x(0)
         weave_x(1)
-        quantise(wt_codes[0][:], wt_scales[0][:], wt_bf[0][:])
         quantise_x(0)
         product(0, 0, 3)
         quantise_x(1)
@@ -346,14 +358,14 @@ def tile_attend_rollout_pl_kernel(tc, query, keys_words, keys_scales, qpool_word
         wt_scales.append(ring.tile([P, HALF], U8, name="wt_scales1", offset=0, align_bytes=64))
         quantise(wt_codes[1][:], wt_scales[1][:], wt_bf[1][:])
         product(0, 1, 6)
-        product(1, 1, 1)
+        product(1, 1, 0)
         for c in range(2, CHUNKS):
             weave_x(c)
         for c in range(2, CHUNKS):
             quantise_x(c)
             product(c, 0, (2, 4)[c - 2])
         for c in range(2, CHUNKS):
-            product(c, 1, (7, 0)[c - 2])
+            product(c, 1, (7, 1)[c - 2])
         round_y(0)
         round_y(1)
         planes(0, 1)

@@ -180,7 +180,7 @@ def tile_attend_rollout_pl_kernel(tc, query, keys_words, keys_scales, qpool_word
             return words[:, :, h * 64:(h + 1) * 64, :]
 
         shares = [sb_tile([P, I], F32, "share%d" % u) for u in range(2)]
-        pairs = [sb_tile([P, 2 * P * 2], BF16, "w_pairs%d" % u) for u in range(2)]
+        placed_w = [sb_tile([P, PACK, 2, P // 2], F32, "placed_w%d" % u) for u in range(2)]
 
         def divide(u, cols):
             nc.scalar.activation(out=shares[u][:, cols], in_=p_tiles[u][:, cols], func=ACT.Copy,
@@ -195,13 +195,12 @@ def tile_attend_rollout_pl_kernel(tc, query, keys_words, keys_scales, qpool_word
             return [turned[t // per_bank][:, t % per_bank, :] for t in range(PACK)]
 
         def times_sa(u, t, turned):
-            places = pairs[u][:].rearrange("p (v e m z) -> p v z e m", v=2, e=2, z=2)
-            nc.scalar.activation(out=places[:, t // 2, t % 2], func=ACT.Copy, scale=sa_cols[:, t:t + 1],
+            nc.scalar.activation(out=placed_w[u][:, t], func=ACT.Copy, scale=sa_cols[:, t:t + 1],
                                  in_=turned[t].rearrange("p (m e) -> p e m", e=2))
 
         def weave_w(u):
-            nc.scalar.copy(out=wt_words(u, 0),
-                           in_=pairs[u][:].bitcast(F32).rearrange("p (v e m) -> p e m v", v=2, e=2))
+            columns = wt_bf[u][:].rearrange("p (e h c i t) -> p h e c t i", e=2, h=2, i=4, t=PACK)
+            nc.scalar.copy(out=columns[:, 0], in_=placed_w[u][:].rearrange("p t e (c i) -> p e c t i", i=4))
 
         divide(0, slice(0, I // 2))
         divide(0, slice(I // 2, I))

@@ -173,7 +173,7 @@ def tile_attend_rollout_pl_kernel(tc, query, keys_words, keys_scales, qpool_word
             for t in range(2):
                 second_scores(t, slots)
 
-        wt_bf = [sb_tile([P, HALF * PACK], BF16, "wt_bf%d" % u) for u in range(2)]
+        wt_bf = [sb_tile([P, HALF * PACK], BF16, "wt_bf0")]
 
         def wt_words(u, h):
             words = wt_bf[u][:].bitcast(F32).rearrange("p (e m v) -> p e m v", e=2, v=2)
@@ -214,7 +214,6 @@ def tile_attend_rollout_pl_kernel(tc, query, keys_words, keys_scales, qpool_word
         weave_w(0)
         times_sa(1, 2, turned1)
         times_sa(1, 3, turned1)
-        weave_w(1)
 
         def weigh(u, rows, out):
             nc.vector.scalar_tensor_tensor(out=out, in0=p_tiles[2 + u][:].rearrange("p (v n) -> p v n", v=2)[:, rows],
@@ -279,30 +278,32 @@ def tile_attend_rollout_pl_kernel(tc, query, keys_words, keys_scales, qpool_word
         nc.tensor.transpose(wt_ps0[:, 2, :], w_and_sb[:, 0, P:2 * P], ident[:])
         sb_cols = sb_tile([P, PACK], F32, "sb_cols")
         second_map(2)
-        nc.vector.tensor_scalar(out=sb_cols[:], in0=wt_ps0[:, 2, 0:4], scalar1=512.0, scalar2=None, op0=ALU.mult)
-        nc.vector.reciprocal(out=inv[:, 4:6], in_=sums[:, 4:6])
         second_map(PACK - 1)
+        nc.vector.reciprocal(out=inv[:, 4:6], in_=sums[:, 4:6])
+        nc.vector.tensor_scalar(out=sb_cols[:], in0=wt_ps0[:, 2, 0:4], scalar1=512.0, scalar2=None, op0=ALU.mult)
+        w_last.append(weigh_last(1))
+        wt_ps1 = turn(1, w_last)
         row_scale = sb_tile([P, 2], F32, "row_scale")
         nc.vector.tensor_tensor(out=row_scale[:], in0=inv[:, 4:6], in1=sb_cols[:, 0:2], op=ALU.mult)
         nc.vector.reciprocal(out=inv[:, 6:7], in_=sums[:, 6:7])
-        w_last.append(weigh_last(1))
-        wt_ps1 = turn(1, w_last)
 
         copy_turned(0, wt_ps0)
         for t in range(2):
             scale_x_on_vector(t, 0, slice(0, JC))
         for t in range(2):
             scale_x_on_scalar(t, 0, slice(JC, HALF))
+        wt_bf.append(sb_tile([P, HALF * PACK], BF16, "wt_bf1", "row_max3"))
+        weave_w(1)
         copy_turned(1, wt_ps1)
         scale_x_on_scalar(0, 1)
         scale_x_on_scalar(1, 1)
         scale_x_on_vector(2, 0)
+        scale_x_on_vector(2, 1)
         nc.vector.reciprocal(out=inv[:, 7:8], in_=sums[:, 7:8])
         wt_codes = [sb_tile([P, HALF], U32, "wt_codes0", "p3"), sb_tile([P, HALF], U32, "wt_codes1")]
         wt_scales = [sb_tile([P, HALF], U8, "wt_scales0")]
-        scale_x_on_vector(2, 1)
-        scale_x_on_vector(3, 0)
         quantise(wt_codes[0][:], wt_scales[0][:], wt_bf[0][:])
+        scale_x_on_vector(3, 0)
         scale_x_on_vector(3, 1)
 
         x_codes = sb_tile([P, J], U32, "x_codes")

@@ -298,13 +298,12 @@ def tile_attend_rollout_pl_kernel(tc, query, keys_words, keys_scales, qpool_word
         scale_x_on_scalar(0, 1)
         scale_x_on_scalar(1, 1)
         scale_x_on_vector(2, 0)
-        scale_x_on_vector(2, 1)
         nc.vector.reciprocal(out=inv[:, 7:8], in_=sums[:, 7:8])
+        scale_x_on_vector(2, 1)
         wt_codes = [sb_tile([P, HALF], U32, "wt_codes0", "p3"), sb_tile([P, HALF], U32, "wt_codes1")]
         wt_scales = [sb_tile([P, HALF], U8, "wt_scales0")]
-        quantise(wt_codes[0][:], wt_scales[0][:], wt_bf[0][:])
         scale_x_on_vector(3, 0)
-        scale_x_on_vector(3, 1)
+        quantise(wt_codes[0][:], wt_scales[0][:], wt_bf[0][:])
 
         x_codes = sb_tile([P, J], U32, "x_codes")
         x_scales = sb_tile([P, J], U8, "x_scales")
@@ -355,6 +354,7 @@ def tile_attend_rollout_pl_kernel(tc, query, keys_words, keys_scales, qpool_word
         product(0, 0, 3)
         quantise_x(1)
         product(1, 0, 5)
+        scale_x_on_vector(3, 1)
         wt_scales.append(ring.tile([P, HALF], U8, name="wt_scales1", offset=0, align_bytes=64))
         quantise(wt_codes[1][:], wt_scales[1][:], wt_bf[1][:])
         product(0, 1, 6)

from contextlib import ExitStack

import concourse.mybir as mybir
from concourse.masks import make_identity

F32 = mybir.dt.float32
BF16 = mybir.dt.bfloat16
I32 = mybir.dt.int32
U32 = mybir.dt.uint32
U16 = mybir.dt.uint16
U8 = mybir.dt.uint8
FP8X4 = mybir.dt.float8_e4m3fn_x4
FP4X4 = mybir.dt.float4_e2m1fn_x4
ALU = mybir.AluOpType
ACT = mybir.ActivationFunctionType
AX = mybir.AxisListType

P = 128
PACK = 4
D, T, I, U, J, Q = 512, 2048, 512, 2048, 512, 512
FLOPS = 2 * D * Q * I + 2 * D * I * J + 2 * I * Q * J
KEYS_ROW, KEYS2_ROW, QPOOL_ROW = 0, 4, 8
CHUNKS = 4
JC = J // CHUNKS
HALF = Q // 2


def tile_attend_rollout_pl_kernel(tc, query, keys_words, keys_scales, qpool_words, qpool_scales,
                                       keys2_words, keys2_scales, sa, sb, offs, offs2, out_0, out_1, out_2):
    nc = tc.nc
    with ExitStack() as ctx:
        lists = ctx.enter_context(tc.tile_pool(name="lists", bufs=1))
        keep = ctx.enter_context(tc.tile_pool(name="keep", bufs=1))
        placed = ctx.enter_context(tc.tile_pool(name="placed", bufs=1))
        ring = ctx.enter_context(tc.tile_pool(name="ring", bufs=1))
        psum = ctx.enter_context(tc.psum_pool(name="psum", bufs=1))

        def sb_tile(shape, dtype, name, tag=None):
            return keep.tile(shape, dtype, name=name, tag=tag or name, align_bytes=64)

        def bank(index, shape, name):
            return psum.tile(shape, F32, name=name, tag="bank%d" % index)

        def zeroed_scale_window(name):
            window = sb_tile([P, T], U8, name)
            nc.vector.memset(window[:].bitcast(I32), 0)
            return window

        def load_scale_rows(queue, window, scales, row):
            for r in range(4):
                queue.dma_start(out=window[row + r:P:32, :].bitcast(I32), in_=scales[0, r:16:4, :].bitcast(I32))

        def quantise(codes, scales, values):
            nc.vector.quantize_mx(out=codes.bitcast(FP8X4), scales=scales, in_=values)

        query_bytes = PACK * Q * 4
        ks_win = zeroed_scale_window("ks_win")
        zeros = placed.tile([P, P], F32, name="zeros", offset=query_bytes - 256, align_bytes=64)
        nc.vector.memset(zeros[:], 0.0)
        vec_rows = sb_tile([P, P], F32, "vec_rows")
        nc.vector.tensor_copy(out=vec_rows[:], in_=zeros[:])
        qs_win = zeroed_scale_window("qs_win")
        k2s_win = zeroed_scale_window("k2s_win")
        ident = sb_tile([P, P], F32, "ident")
        nc.vector.memset(ident[:], 0.0)
        make_identity(nc, ident[:], nomemset=True)
        w_and_sb = sb_tile([P, 2, 2 * P], F32, "w_and_sb")
        nc.vector.memset(w_and_sb[:, 0, P:2 * P], 0.0)

        offs_sb = lists.tile([P, I // 16], U16, name="offs_sb")
        offs2_sb = lists.tile([P, J // 16], U16, name="offs2_sb")
        kw_win = sb_tile([P, T], U16, "kw_win", "slot_a")
        nc.sync.dma_start(out=kw_win[:].bitcast(I32), in_=keys_words[0].bitcast(I32))
        nc.sync.dma_start(offs_sb[:], offs)
        nc.sync.dma_start(offs2_sb[:], offs2)
        load_scale_rows(nc.scalar, ks_win, keys_scales, KEYS_ROW)
        q_rows = query.rearrange("(p t) q -> p t q", t=PACK)
        q_both = placed.tile([P, 2, PACK, HALF], F32, name="q_both", offset=0, align_bytes=64)
        for h in range(2):
            nc.sync.dma_start(out=q_both[:, h], in_=q_rows[:, :, h * HALF:(h + 1) * HALF])
        load_scale_rows(nc.sync, qs_win, qpool_scales, QPOOL_ROW)
        nc.sync.dma_start(out=vec_rows[4:8, :].rearrange("t (g r) -> t g r", r=8),
                          in_=sa.rearrange("o (g t r) -> t g (r o)", t=4, r=8))
        qw_win = placed.tile([P, T], I32, name="qw_win", offset=query_bytes, align_bytes=64)
        nc.sync.dma_start(out=qw_win[:], in_=qpool_words[0].rearrange("p n t -> p (n t)").bitcast(I32))


        kw = sb_tile([P, I], U16, "kw")
        nc.vector.tensor_copy(out=kw[:], in_=kw_win[:].indirect(offs_sb[:]))
        ks = sb_tile([P, I], U8, "ks")
        nc.vector.tensor_copy(out=ks[:], in_=ks_win[:].indirect(offs_sb[:]))
        k2w_win = sb_tile([P, U], I32, "k2w_win", "slot_a")
        nc.sync.dma_start(out=k2w_win[:], in_=keys2_words[0].rearrange("p n t -> p (n t)").bitcast(I32))
        load_scale_rows(nc.sync, k2s_win, keys2_scales, KEYS2_ROW)
        nc.sync.dma_start(out=w_and_sb[0:4, 0, P:2 * P].rearrange("t (g r) -> t g r", r=8),
                          in_=sb.rearrange("(g t r) o -> t g (r o)", t=4, r=8))

        vec_ps = bank(6, [P, P], "vec_ps")
        nc.tensor.transpose(vec_ps[:], vec_rows[:], ident[:])
        sa_cols = sb_tile([P, PACK], F32, "sa_cols")
        nc.scalar.copy(out=sa_cols[:], in_=vec_ps[:, 4:8])
        sa_ps = bank(7, [P, 2, P, 2], "sa_ps")
        for t in range(PACK):
            nc.tensor.transpose(sa_ps[:, t // 2, :, t % 2], sa_cols[:, t:t + 1].to_broadcast([P, P]), ident[:])
        sa_all = sa_ps[:].rearrange("p u n e -> p (u n e)")

        q_codes = sb_tile([P, Q], U32, "q_codes")
        q_scales = sb_tile([P, Q], U8, "q_scales")
        neg_max = [sb_tile([P, 2], F32, "neg_max%d" % h) for h in range(2)]
        sums = sb_tile([P, 8], F32, "sums")
        inv = sb_tile([P, 8], F32, "inv")

        def round_query(h):
            q_bf = sb_tile([P, HALF * PACK], BF16, "q_bf%d" % h)
            nc.scalar.copy(out=q_bf[:].rearrange("p (u m e t) -> p m t u e", u=2, e=2, t=PACK),
                           in_=q_both[:, h].rearrange("p t (m u e) -> p m t u e", u=2, e=2))
            return q_bf

        def quantise_query(h, q_bf):
            cols = slice(h * HALF, (h + 1) * HALF)
            quantise(q_codes[:, cols], q_scales[:, cols], q_bf[:])

        p_tiles = {}

        def first_map(h, u, index):
            n = 2 * h + u
            a_ps = bank(index, [P, I], "a_ps%d" % n)
            cols = slice(n * P, (n + 1) * P)
            nc.tensor.matmul_mx(out=a_ps[:], lhsT=q_codes[:, cols].bitcast(FP8X4), lhsT_scale=q_scales[:, cols],
                                rhs=kw[:].bitcast(FP4X4), rhs_scale=ks[:], start=True, stop=True)
            nc.vector.tensor_reduce(out=neg_max[h][:, u:u + 1], in_=a_ps[:], axis=AX.X, op=ALU.max, negate=True)
            return a_ps

        def first_exp(h, u, a_ps):
            n = 2 * h + u
            p_tiles[n] = sb_tile([P, I], F32, "p%d" % n)
            if h == 0:
                dealt = p_tiles[n][:].rearrange("p (t g r) -> p g t r", t=PACK, r=8)
                scores = a_ps[:].rearrange("p (g t r) -> p g t r", t=PACK, r=8)
            else:
                dealt = p_tiles[n][:].rearrange("p (v g r e) -> p g v r e", v=2, r=8, e=2)
                scores = a_ps[:].rearrange("p (g v e r) -> p g v r e", v=2, r=8, e=2)
            nc.scalar.activation(out=dealt, in_=scores, func=ACT.Exp, bias=neg_max[h][:, u:u + 1],
                                 accum_out=sums[:, n:n + 1])

        q_bf = [round_query(h) for h in range(2)]
        quantise_query(0, q_bf[0])
        qs = sb_tile([P, I], U8, "qs")
        nc.vector.tensor_copy(out=qs[:].rearrange("p (t g r) -> p g t r", t=4, r=8),
                              in_=qs_win[:].indirect(offs_sb[:]))
        quantise_query(1, q_bf[1])
        for n in range(4):
            first_exp(n // 2, n % 2, first_map(n // 2, n % 2, n))
        nc.vector.reciprocal(out=inv[:, 0:2], in_=sums[:, 0:2])
        qw = sb_tile([P, I], U32, "qw")
        nc.vector.tensor_copy(out=qw[:].rearrange("p (t g r) -> p g t r", t=4, r=8),
                              in_=qw_win[:].bitcast(U32).indirect(offs_sb[:]))
        nc.vector.reciprocal(out=inv[:, 2:4], in_=sums[:, 2:4])
        k2w = sb_tile([P, J], U32, "k2w")
        nc.vector.tensor_copy(out=k2w[:], in_=k2w_win[:].bitcast(U32).indirect(offs2_sb[:]))
        k2s = sb_tile([P, J], U8, "k2s")
        b_banks = [bank(4 + t, [P, J], "b_ps%d" % t) for t in range(2)]

        def second_scores(t, slots):
            rows = slice(t * P, (t + 1) * P)
            nc.tensor.matmul_mx(out=b_banks[t][:, slots], lhsT=qw[:, rows].bitcast(FP8X4),
                                lhsT_scale=qs[QPOOL_ROW:P, rows], rhs=k2w[:, slots].bitcast(FP8X4),
                                rhs_scale=k2s[KEYS2_ROW:P, slots], start=True, stop=True)

        for a in range(2):
            slots = slice(a * HALF, (a + 1) * HALF)
            nc.vector.tensor_copy(out=k2s[:, slots], in_=k2s_win[:].indirect(offs2_sb[:, 16 * a:16 * (a + 1)]))
            for t in range(2):
                second_scores(t, slots)

        wt_bf = [sb_tile([P, HALF * PACK], BF16, "wt_bf0")]

        def wt_words(u, h):
            words = wt_bf[u][:].bitcast(F32).rearrange("p (e m v) -> p e m v", e=2, v=2)
            return words[:, :, h * 64:(h + 1) * 64, :]

        shares = [sb_tile([P, I], F32, "share%d" % u) for u in range(2)]
        placed_w = [sb_tile([P, PACK, 2, P // 2], F32, "placed_w%d" % u) for u in range(2)]

        def divide(u, cols):
            nc.scalar.activation(out=shares[u][:, cols], in_=p_tiles[u][:, cols], func=ACT.Copy,
                                 scale=inv[:, u:u + 1])

        def turn_share(u, banks):
            turned = [bank(index, [P, PACK // len(banks), P], "turned%d_%d" % (u, index)) for index in banks]
            per_bank = PACK // len(banks)
            for t in range(PACK):
                nc.tensor.transpose(turned[t // per_bank][:, t % per_bank, :], shares[u][:, t * P:(t + 1) * P],
                                    ident[:])
            return [turned[t // per_bank][:, t % per_bank, :] for t in range(PACK)]

        def times_sa(u, t, turned):
            nc.scalar.activation(out=placed_w[u][:, t], func=ACT.Copy, scale=sa_cols[:, t:t + 1],
                                 in_=turned[t].rearrange("p (m e) -> p e m", e=2))

        def weave_w(u):
            columns = wt_bf[u][:].rearrange("p (e h c i t) -> p h e c t i", e=2, h=2, i=4, t=PACK)
            nc.scalar.copy(out=columns[:, 0], in_=placed_w[u][:].rearrange("p t e (c i) -> p e c t i", i=4))

        divide(0, slice(0, I // 2))
        divide(0, slice(I // 2, I))
        turned0 = turn_share(0, (0, 2))
        divide(1, slice(0, I))
        turned1 = turn_share(1, (1, 3))
        for t in range(PACK):
            times_sa(0, t, turned0)
        times_sa(1, 0, turned1)
        times_sa(1, 1, turned1)
        weave_w(0)
        times_sa(1, 2, turned1)
        times_sa(1, 3, turned1)

        def weigh(u, rows, out):
            nc.vector.scalar_tensor_tensor(out=out, in0=p_tiles[2 + u][:].rearrange("p (v n) -> p v n", v=2)[:, rows],
                                           scalar=inv[:, 2 + u:3 + u],
                                           in1=sa_all.rearrange("p (v n) -> p v n", v=2)[:, rows],
                                           op0=ALU.mult, op1=ALU.mult)

        def turn(u, words):
            wt_ps = bank((4, 1)[u], [P, 3, P], "wt_ps%d" % u)
            for v in range(2):
                nc.tensor.transpose(wt_ps[:, v, :], words[v], ident[:])
            return wt_ps

        def weigh_last(v):
            half = sb_tile([P, 1, P], F32, "w1_%d" % v, ("k2s_win", "row_max1")[v])
            weigh(1, slice(v, v + 1), half[:].bitcast(BF16))
            return half[:, 0, :]

        def copy_turned(u, wt_ps):
            nc.scalar.copy(out=wt_words(u, 1), in_=wt_ps[:, 0:2, :].rearrange("p v (m e) -> p e m v", e=2))

        r_rows = []

        def second_map(t):
            b_ps = b_banks[t]
            if t >= 2:
                second_scores(t, slice(0, J))
            row_max = sb_tile([P, 1], F32, "row_max%d" % t)
            nc.vector.tensor_reduce(out=row_max[:], in_=b_ps[:], axis=AX.X, op=ALU.max, negate=True)
            r_rows.append(sb_tile([P, J], F32, "r%d" % t))
            nc.scalar.activation(out=r_rows[t][:], in_=b_ps[:], func=ACT.Exp,
                                 bias=row_max[:], accum_out=sums[:, 4 + t:5 + t])

        x_pairs = [sb_tile([P, 2 * HALF * 2], BF16, "x_pairs%d" % a) for a in range(2)]
        x_bf = {}

        def x_place(t, a):
            return x_pairs[a][:].rearrange("p (v j z) -> p v j z", v=2, z=2)[:, t // 2, :, t % 2]

        def scale_x_on_vector(t, a, cols=slice(0, HALF)):
            nc.vector.tensor_scalar(out=x_place(t, a)[:, cols], in0=r_rows[t][:, a * HALF:(a + 1) * HALF][:, cols],
                                    scalar1=inv[:, 4 + t:5 + t], scalar2=sb_cols[:, t:t + 1],
                                    op0=ALU.mult, op1=ALU.mult)

        def scale_x_on_scalar(t, a, cols=slice(0, HALF)):
            nc.scalar.activation(out=x_place(t, a)[:, cols], in_=r_rows[t][:, a * HALF:(a + 1) * HALF][:, cols],
                                 func=ACT.Copy, scale=row_scale[:, t:t + 1])

        def weave_x(c):
            x_bf[c] = ring.tile([P, JC, PACK], BF16, name="x_bf%d" % c, offset=(0, 2048, 256, 2048)[c],
                                align_bytes=64)
            words = x_bf[c][:].rearrange("p c t -> p (c t)").bitcast(F32).rearrange("p (c v) -> p c v", v=2)
            both = x_pairs[c // 2][:].bitcast(F32).rearrange("p (v j) -> p j v", v=2)
            nc.vector.tensor_copy(out=words, in_=both[:, (c % 2) * JC:(c % 2 + 1) * JC, :])

        b_banks.extend(bank((6, 2)[t], [P, J], "b_ps%d" % (2 + t)) for t in range(2))
        weigh(0, slice(0, 2), w_and_sb[:].bitcast(BF16)[:, :, 0:2 * P])
        w_last = [weigh_last(0)]
        second_map(0)
        second_map(1)
        wt_ps0 = turn(0, [w_and_sb[:, v, 0:P] for v in range(2)])
        nc.tensor.transpose(wt_ps0[:, 2, :], w_and_sb[:, 0, P:2 * P], ident[:])
        sb_cols = sb_tile([P, PACK], F32, "sb_cols")
        second_map(2)
        second_map(PACK - 1)
        nc.vector.reciprocal(out=inv[:, 4:6], in_=sums[:, 4:6])
        nc.vector.tensor_scalar(out=sb_cols[:], in0=wt_ps0[:, 2, 0:4], scalar1=512.0, scalar2=None, op0=ALU.mult)
        w_last.append(weigh_last(1))
        wt_ps1 = turn(1, w_last)
        row_scale = sb_tile([P, 2], F32, "row_scale")
        nc.vector.tensor_tensor(out=row_scale[:], in0=inv[:, 4:6], in1=sb_cols[:, 0:2], op=ALU.mult)
        nc.vector.reciprocal(out=inv[:, 6:7], in_=sums[:, 6:7])

        copy_turned(0, wt_ps0)
        for t in range(2):
            scale_x_on_vector(t, 0, slice(0, JC))
        for t in range(2):
            scale_x_on_scalar(t, 0, slice(JC, HALF))
        wt_bf.append(sb_tile([P, HALF * PACK], BF16, "wt_bf1", "row_max3"))
        weave_w(1)
        copy_turned(1, wt_ps1)
        scale_x_on_scalar(0, 1)
        scale_x_on_scalar(1, 1)
        scale_x_on_vector(2, 0)
        nc.vector.reciprocal(out=inv[:, 7:8], in_=sums[:, 7:8])
        scale_x_on_vector(2, 1)
        wt_codes = [sb_tile([P, HALF], U32, "wt_codes0", "p3"), sb_tile([P, HALF], U32, "wt_codes1")]
        wt_scales = [sb_tile([P, HALF], U8, "wt_scales0")]
        scale_x_on_vector(3, 0)
        quantise(wt_codes[0][:], wt_scales[0][:], wt_bf[0][:])

        x_codes = sb_tile([P, J], U32, "x_codes")
        x_scales = sb_tile([P, J], U8, "x_scales")
        y_codes = sb_tile([P, J], U32, "y_codes")
        y_scales = sb_tile([P, J], U8, "y_scales")
        y_rows = out_0.rearrange("(p t) j -> p t j", t=PACK)
        y_words = out_1[0].rearrange("p c r -> p (c r)").bitcast(I32)
        y_sb = [sb_tile([P, PACK, HALF], F32, "y_sb%d" % a) for a in range(2)]
        y_bf = [sb_tile([P, 2 * JC * PACK], BF16, "y_bf%d" % a) for a in range(2)]

        def quantise_x(c):
            cols = slice(c * JC, (c + 1) * JC)
            quantise(x_codes[:, cols], x_scales[:, cols], x_bf[c][:].rearrange("p c t -> p (c t)"))

        def product(c, u, index):
            cols = slice(c * JC, (c + 1) * JC)
            y_ps = bank(index, [P, 2, JC], "y_ps%d_%d" % (c, u))
            for e in range(2):
                q_cols = slice(e * P, (e + 1) * P)
                nc.tensor.matmul_mx(out=y_ps[:, e, :], lhsT=wt_codes[u][:, q_cols].bitcast(FP8X4),
                                    lhsT_scale=wt_scales[u][:, q_cols], rhs=x_codes[:, cols].bitcast(FP8X4),
                                    rhs_scale=x_scales[:, cols], start=True, stop=True)
            part = slice(2 * u, 2 * u + 2)
            nc.scalar.copy(out=y_sb[c // 2][:, part, (c % 2) * JC:(c % 2 + 1) * JC], in_=y_ps[:])
            if (c // 2, u) == (0, 0):
                nc.sync.dma_start(out=y_rows[:, part, cols], in_=y_sb[0][:, part, cols])
            elif c % 2:
                nc.sync.dma_start(out=y_rows[:, part, (c - 1) * JC:(c + 1) * JC], in_=y_sb[c // 2][:, part, :])

        def round_y(c):
            rounded = y_bf[c // 2][:, (c % 2) * JC * PACK:(c % 2 + 1) * JC * PACK]
            nc.vector.tensor_copy(out=rounded.rearrange("p (c i t) -> p c t i", i=4, t=PACK),
                                  in_=y_sb[c // 2][:, :, (c % 2) * JC:(c % 2 + 1) * JC].rearrange(
                                      "p t (c i) -> p c t i", i=4))

        def planes(first, count):
            cols = slice(first * JC, (first + count) * JC)
            start = (first % 2) * JC * PACK
            quantise(y_codes[:, cols], y_scales[:, cols], y_bf[first // 2][:, start:start + count * JC * PACK])

        def store_codes(a):
            cols = slice(a * HALF, (a + 1) * HALF)
            nc.sync.dma_start(out=y_words[:, cols], in_=y_codes[:, cols].bitcast(I32))

        weave_x(0)
        weave_x(1)
        quantise_x(0)
        product(0, 0, 3)
        quantise_x(1)
        product(1, 0, 5)
        scale_x_on_vector(3, 1)
        wt_scales.append(ring.tile([P, HALF], U8, name="wt_scales1", offset=0, align_bytes=64))
        quantise(wt_codes[1][:], wt_scales[1][:], wt_bf[1][:])
        product(0, 1, 6)
        product(1, 1, 0)
        for c in range(2, CHUNKS):
            weave_x(c)
        for c in range(2, CHUNKS):
            quantise_x(c)
            product(c, 0, (2, 4)[c - 2])
        for c in range(2, CHUNKS):
            product(c, 1, (7, 1)[c - 2])
        round_y(0)
        round_y(1)
        planes(0, 1)
        planes(1, 1)
        store_codes(0)
        round_y(2)
        round_y(3)
        planes(2, 1)
        planes(3, 1)
        store_codes(1)
        for quad in range(4):
            queue = nc.scalar if quad % 2 else nc.sync
            queue.dma_start(out=out_2[0, 4 * quad:4 * quad + 4, :].bitcast(I32),
                            in_=y_scales[32 * quad:32 * quad + 4, :].bitcast(I32))
